import numpy as np, ml_dtypes
CORES = [40,64,80,88,96,104,120,144]
N = 8
BF = ml_dtypes.bfloat16
def gentries(a):
    return np.ascontiguousarray(a.reshape(8, 16, -1).transpose(0, 2, 1)).reshape(8, -1)
def gtable(e):
    e = np.asarray(e); return np.ascontiguousarray(e.reshape(8, -1, 16).transpose(0, 2, 1)).reshape(128, -1).astype(np.int32)
P, L, G, RO, J = 1024, 3, 1024, 3, 2
K = L * G; W = P + K
H = P // 16; C = G // 32
B = 2 ** J + 2; Y = 16; T = 3 + B + 2 * Y
ENDS = [RO - 1, 2 * RO - 2, 2 * RO - 1, 2 * RO - 1 + B, 2 * RO - 1 + 2 * B, 2 * RO - 1 + 2 * B + 2 * Y, 2 * RO + 1 + 2 * B + 3 * Y]; X = ENDS[-1] + 1
TIES = [[28, 17, 21, 9], [41, 18, 23, 5], [42, 38, 35, 13], [44, 27, 18, 7], [45, 22, 34, 4], [45, 35, 43, 14], [49, 48, 43, 15], [52, 5, 50, 11]]
def pick(rng, top, shape, pw):
    return np.minimum((top * rng.random(shape) ** pw).astype(np.int64), top - 1)
def wiring(rng, kinds=(0, 1, 2, 3, 4, 5, 6), pw=(1.0,) * 8):
    o = np.argsort(rng.random((8, P)), axis=1); z = o[:, :16]; q = o[:, 16:16 + 8 * H].reshape(8, 4, H, 2); ex = o[:, 16 + 8 * H:16 + 8 * H + X]; k = np.arange(K)
    fa = np.zeros((N, 8, K), np.int64); fb = np.zeros((N, 8, K), np.int64); cd = np.zeros((8, K), np.int64); tp = np.zeros((8, P), np.int64)
    for g in range(8):
        w = pw[g]; tops = P + k // G * G; pairs = []
        last = np.sort(np.append(G - 512 + rng.permutation(511)[:T - 1], G - 1)); sp = (L - 1) * G + last
        fa[:, g] = pick(rng, tops, (N, K), w); fb[:, g] = pick(rng, tops, (N, K), w); cd[g] = pick(rng, P + k, K, w); tp[g] = pick(rng, W, P, w)
        for l in range(L):
            top = P + l * G; m = l * G + rng.permutation(G)
            if l == L - 1: m = l * G + np.concatenate([rng.permutation(np.setdiff1d(np.arange(G), last)), last])
            pr = np.sort(m[:14 * C].reshape(7, C, 2), axis=2)
            for j, kind in enumerate(kinds):
                n1, n2 = pr[j, :, 0], pr[j, :, 1]
                a1 = pick(rng, top, (N, C), w); b1 = pick(rng, top, (N, C), w); a2 = a1.copy(); i = rng.integers(0, H, (N, C))
                if kind == 3: i = np.tile(i[:1], (N, 1)); b1 = np.tile(z[g, rng.integers(0, 16, C)], (N, 1))
                if kind >= 2: s = q[g, (0, 1, 2, 2, 3)[kind - 2]]; a1, a2 = s[i, 0], s[i, 1]
                if kind in (1, 5): a2[rng.integers(0, N, C), np.arange(C)] = pick(rng, top, C, w)
                if kind in (2, 4, 6) and rng.random() < 0.5: fa[:, g, n1] = b1; fb[:, g, n1] = a1; fa[:, g, n2] = b1; fb[:, g, n2] = a2
                else: fa[:, g, n1] = a1; fb[:, g, n1] = b1; fa[:, g, n2] = a2; fb[:, g, n2] = b1
                cd[g, n2] = P + n1
                if kind == 4: pairs.append(pr[j])
            s = m[14 * C:18 * C]; a1 = pick(rng, top, 4 * C, w)
            fa[:, g, s] = a1; fb[:, g, s] = z[g, rng.integers(0, 16, 4 * C)]; cd[g, s] = a1
            if l > 0:
                s = m[18 * C:22 * C]; i = pick(rng, l * G, 4 * C, w)
                fa[:, g, s] = fa[:, g, i]; fb[:, g, s] = fb[:, g, i]; cd[g, s] = P + i
            s = np.sort(m[22 * C:28 * C].reshape(C, 6), axis=1)
            fa[:, g, s] = pick(rng, top, (N, C, 1), w); fb[:, g, s] = pick(rng, top, (N, C, 1), w); cd[g, s[:, 1:]] = P + s[:, :-1]
        pt = np.concatenate(pairs)
        tp[g, z[g, :4]] = z[g, :4]; tp[g, q[g, 2, :, 1]] = tp[g, q[g, 2, :, 0]]; tp[g, q[g, 3]] = P + pt[rng.integers(0, len(pt), H)]
        ua, ub, us, e, h, nr, vw, full = np.split(ex[g], ENDS); t = rng.permutation(T - 1)
        n0 = np.sort(sp[t[:2]]); n1 = np.sort(sp[t[2:2 + B]]); n2 = np.sort(sp[t[2 + B:]].reshape(Y, 2), axis=1)
        fb[:, g, sp] = z[g, rng.integers(0, 4, (N, T))]
        fa[:, g, n0] = ua[0]; fa[:, g, K - 1] = ub[0]; cd[g, n0[1]] = P + n0[0]; cd[g, K - 1] = P + n0[1]
        fa[:, g, n1] = e; cd[g, n1[1:]] = P + n1[:-1]
        fa[:, g, n2] = nr.reshape(Y, 2); cd[g, n2[:, 1]] = P + n2[:, 0]
        tp[g, ua] = np.append(ua[1:], us); tp[g, ub] = np.append(ub[1:], us); tp[g, us] = us; tp[g, e] = h; tp[g, h] = e; tp[g, nr] = nr; tp[g, full] = full
        tp[g, vw] = P + np.concatenate([[K - 1, n1[-1]], n2[:, 1]])
    return z, q, ex, fa, fb, cd, tp
def gaps(rng):
    S = 16 * N; a = 16 * rng.integers(0, N, 3) + rng.integers(0, 14, 3); b = 16 * rng.integers(0, N - 2, 3) + rng.integers(0, 16, 3); u = 2 * rng.integers(0, 8 * N, 2)
    c = [([S - 1], [1]), ([0], [1]), ([S - 16], [1]), ([a[0], a[0] + 1], [2, -1]), ([a[1], a[1] + 1], [-1, 2]), ([b[0], b[0] + 16], [2, -1]), ([b[1], b[1] + 16], [-1, 2]),
         ([u[0], u[0] + 1], [255, -1]), ([u[1], u[1] + 1], [-1, 255]), ([a[2], a[2] + 1, a[2] + 2], [1, -2, 1]), ([b[2], b[2] + 16, b[2] + 32], [1, -2, 1])]
    for i in rng.integers(0, len(TIES), 2): c.append((TIES[i], [1, 1, -1, -1]))
    for i in range(3): c.append((rng.permutation(S)[:4], [1, 1, -1, -1]))
    return c
def plant(rng, xx, z, q, ex, lo=(0,) * 8, hi=(16 * N,) * 8):
    for g in range(8):
        v = xx[g]; n0, n1 = q[g, 1, :, 0], q[g, 1, :, 1]; s = hi[g] - lo[g]
        v[:, z[g]] = 0; v[:, q[g, 0, :, 1]] = v[:, q[g, 0, :, 0]]
        v[:, n0] = np.clip(v[:, n0], 1, 254); v[:, n1] = v[:, n0]
        i = rng.integers(0, s, H); j = (i + 1 + rng.integers(0, s - 1, H)) % s; mode = rng.permutation(np.arange(H) % 4)
        v[lo[g] + i, n1] += np.where(mode < 2, 1, np.where(mode == 2, -1, 0)); v[lo[g] + j, n1] -= (mode == 1).astype(np.int64)
        ua, ub, us, e, h, nr, vw, full = np.split(ex[g], ENDS)
        i = rng.integers(0, 16 * N, RO - 1); v[i, ub] = 255 - v[i, ua]
        v[rng.integers(0, 16 * N), e] = 255 * (np.arange(B) % 2); v[:, h] = v[:, h[:1]]; v[:, full] = 255
        for j, (places, d) in enumerate(gaps(rng)):
            places = np.array(places); d = np.array(d); n = nr[2 * j:2 * j + 2]
            if rng.random() < 0.5: n = n[::-1]
            c = np.clip(v[:, n[0]], 2, 253); c[places] = np.where(d == 255, 0, c[places]); v[:, n[0]] = c
            c = c.copy(); c[places] += d; v[:, n[1]] = c
    return xx
def quiet(g, xx, z, ex, fa, fb, cd):
    v = np.zeros((N, 16, W), np.int64); v[..., :P] = xx[g].reshape(N, 16, P)
    for l in range(L):
        s = slice(l * G, (l + 1) * G)
        v[..., P + l * G:P + (l + 1) * G] = np.minimum(np.take_along_axis(v, fa[:, g, None, s], 2), 255 - np.take_along_axis(v, fb[:, g, None, s], 2))
    own = v[..., P:]; same = np.all(own == v[..., cd[g]], axis=(0, 1)); zero = np.all(own == 0, axis=(0, 1))
    cd[g] = np.where(same, np.where(zero, ex[g, -1], z[g, 0]), cd[g])
def pack(xx, fa, fb, cd, tp):
    x = np.ascontiguousarray(xx.reshape(8, N, 16, P).transpose(1, 0, 2, 3)).reshape(N, 128, P)
    return {"x": x.astype(np.float32).astype(BF), "fa": np.stack([gtable(e) for e in fa]), "fb": np.stack([gtable(e) for e in fb]), "cd": np.stack([gtable(cd)] * N), "tp": np.stack([gtable(tp)] * N)}
def setup_inputs(rng):
    z, q, ex, fa, fb, cd, tp = wiring(rng)
    return pack(plant(rng, rng.integers(0, 256, (8, 16 * N, P)), z, q, ex), fa, fb, cd, tp)
def setup_inputs_near(rng):
    z, q, ex, fa, fb, cd, tp = wiring(rng, kinds=(3, 3, 3, 3, 4, 5, 1))
    for g in range(8): tp[g, z[g]] = z[g]; tp[g, q[g, 1, :H // 2]] = q[g, 1, :H // 2]
    one = (0, N - 1, 1, N - 2); lo = [16 * one[g] if g < 4 else 0 for g in range(8)]; hi = [16 * one[g] + 16 if g < 4 else 16 * N for g in range(8)]
    xx = plant(rng, rng.integers(0, 256, (8, 16 * N, P)), z, q, ex, lo, hi)
    for g in (4, 7): quiet(g, xx, z, ex, fa, fb, cd)
    return pack(xx, fa, fb, cd, tp)
def setup_inputs_chains(rng):
    z, q, ex, fa, fb, cd, tp = wiring(rng); n = G // 32; h = n // 2
    for g in range(1, 8, 2):
        last = None
        for l in range(L):
            top = P + l * G; s = l * G + np.sort(rng.permutation(G).reshape(n, 32), axis=1)
            a = rng.integers(0, top, (N, n)); b = rng.integers(0, top, (N, n))
            if l > 0: a[:, :h] = P + last[:h]; b[:, :h] = z[g, 0]; cd[g, s[:h, 0]] = P + last[:h]
            fa[:, g, s] = a[:, :, None]; fb[:, g, s] = b[:, :, None]; cd[g, s[:, 1:]] = P + s[:, :-1]
            cut = rng.random((n, 32)) < 0.08; cut[:, 0] = False; cut[0, 16] = True; c = s[cut]
            fa[rng.integers(0, N, len(c)), g, c] = rng.integers(0, top, len(c)); last = s[:, -1]
    return pack(plant(rng, rng.integers(0, 256, (8, 16 * N, P)), z, q, ex), fa, fb, cd, tp)
def setup_inputs_flat(rng):
    z, q, ex, fa, fb, cd, tp = wiring(rng)
    xx = plant(rng, 255 * rng.integers(0, 2, (8, 16 * N, P)), z, q, ex); o = rng.permutation(8)
    xx[o[0]] = 0; xx[o[1]] = 255
    return pack(xx, fa, fb, cd, tp)
def setup_inputs_ends(rng):
    z, q, ex, fa, fb, cd, tp = wiring(rng); k = np.arange(K); tops = P + k // G * G
    fa[:, 0] = np.where(rng.random((N, K)) < 0.5, 0, tops - 1); fb[:, 0] = np.where(rng.random((N, K)) < 0.5, 0, tops - 1)
    fb[:, 1] = fa[:, 1]
    cd[2] = P + k - 1
    m = rng.random(K) < 0.5; fa[:, 3, m] = 0; fb[:, 3, m] = z[3, 0]; cd[3] = 0
    tp[4] = rng.choice(np.array([0, P - 1, P, W - 1]), P)
    cd[5] = np.where(rng.random(K) < 0.5, 0, P + k - 1); fa[:, 5] = np.where(rng.random(K) < 0.5, tops - 1, fa[:, 5])
    fa[:, 6] = tops - 1; fb[:, 6] = z[6, 0]; cd[6] = P + k - 1
    return pack(plant(rng, rng.integers(0, 256, (8, 16 * N, P)), z, q, ex), fa, fb, cd, tp)
def setup_inputs_spread(rng):
    pw = rng.permutation(np.array([0.35, 0.35, 0.6, 1.0, 1.0, 1.5, 3.0, 3.0])); z, q, ex, fa, fb, cd, tp = wiring(rng, pw=pw)
    e = np.exp2(rng.integers(-3, 4, (8, 1, P)) + rng.integers(-1, 2, (8, 16 * N, 1)))
    return pack(plant(rng, np.minimum((256 * rng.random((8, 16 * N, P)) ** e).astype(np.int64), 255), z, q, ex), fa, fb, cd, tp)
def check_inputs(d):
    bad = []; k = np.arange(K); x = np.asarray(d["x"]).astype(np.float32)
    if not (np.all(x >= 0) and np.all(x <= 255) and np.all(x == np.floor(x))): bad.append("whole numbers from 0 to 255 in x")
    for name, top in (("fa", P + k // G * G), ("fb", P + k // G * G), ("cd", P + k), ("tp", W)):
        e = np.stack([gentries(s) for s in d[name]]).astype(np.int64)
        if np.any(e < 0) or np.any(e >= top): bad.append("range of " + name)
    for name in ("cd", "tp"):
        if np.any(d[name] != d[name][:1]): bad.append(name + " alike on all ranks")
    return bad
def reference(x, fa, fb, cd, tp):
    now = x.astype(np.float32).astype(np.int32).reshape(N, 8, 16, P)
    a = np.stack([gentries(e) for e in fa]).astype(np.int64); b = np.stack([gentries(e) for e in fb]).astype(np.int64)
    c = gentries(cd[0]).astype(np.int64); taps = gentries(tp[0]).astype(np.int64)
    for rnd in range(RO):
        v = np.zeros((N, 8, 16, W), np.int32); v[..., :P] = now
        for l in range(L):
            s = slice(l * G, (l + 1) * G)
            v[..., P + l * G:P + (l + 1) * G] = np.minimum(np.take_along_axis(v, a[:, :, None, s], 3), 255 - np.take_along_axis(v, b[:, :, None, s], 3))
        differ = v[..., P:] != np.take_along_axis(v, c[None, :, None, :], 3)
        mm = np.add.reduce(np.add.reduce(differ.astype(np.int32), axis=2), axis=0)
        rep = np.tile(np.arange(W), (8, 1)); rep[:, P:] = np.where(mm == 0, c, rep[:, P:])
        for j in range(J): rep = np.take_along_axis(rep, rep, 1)
        a = np.take_along_axis(rep[None], a, 2); b = np.take_along_axis(rep[None], b, 2)
        taps = np.take_along_axis(rep, taps, 1)
        now = np.take_along_axis(v, taps[None, :, None, :], 3)
    return {"yv": v.reshape(N, 128, W).astype(np.float32).astype(BF), "ya": np.stack([gtable(e) for e in a]).astype(np.float32), "yb": np.stack([gtable(e) for e in b]).astype(np.float32),
            "yt": np.stack([gtable(taps)] * N).astype(np.float32)}

@@ -1,0 +1,420 @@
+from concourse.bass import DstId, RemoteDMATransfer
+from concourse.mybir import AluOpType as ALU, ActivationFunctionType as ACT
+
+B16, F32, I32, U16 = "bfloat16", "float32", "int32", "uint16"
+SCRATCH = {n: ("sbuf", [128] + list(s), d) for n, s, d in [
+    ("vb0", [4096], B16), ("vb1", [4096], B16), ("vb2", [4096], B16), ("wb1", [3072], B16), ("wb2", [3072], B16),
+    ("tb", [9216], B16), ("df", [9216], B16), ("vc", [9216], B16), ("tab", [4096], B16), ("fl", [4096], B16),
+    ("gf", [9 * 512], B16), ("gch", [6 * 384], B16), ("gfin", [4096], B16), ("fi", [384], I32), ("ci", [256], I32),
+    ("lab", [384], U16), ("lct", [256], U16), ("lr", [5 * 64], U16), ("lfin", [256], U16), ("rm", [8 * 256], I32),
+    ("cdi", [256], I32), ("cdf", [256], F32), ("idw", [128], I32), ("thl", [64], B16), ("si", [48], I32), ("sf", [48], F32),
+    ("ones", [128], F32), ("neg", [128], F32), ("oneb", [4, 8], B16), ("zv", [144], B16), ("zj", [4, 144], B16), ("zs", [256], B16),
+    ("i16", [16], F32), ("pls", [128], F32), ("nls", [128], F32), ("psl", [128], F32),
+    ("vl", [96, 6], F32), ("lf", [96 * 4], U16), ("d1", [96 * 5], F32), ("d0", [72 * 5], F32), ("rs", [72 * 5], F32),
+    ("lu", [6 * 24], U16), ("xv", [9 * 64], B16), ("ru", [5 * 8], U16), ("rh", [4 * 8], B16), ("rf", [8], F32), ("oo", [384], F32)]}
+SCRATCH.update({n: ("dram", s, d) for n, s, d in [
+    ("dt", [8, 4096], B16), ("rd", [9, 128, 64], B16), ("dv", [72, 128, 64], B16), ("ru1", [5, 128, 8], U16), ("ru2", [40, 128, 8], U16),
+    ("rh1", [4, 128, 8], B16), ("rh2", [32, 128, 8], B16), ("rf1", [1, 128, 8], F32), ("rf2", [8, 128, 8], F32)]})
+SCRATCH.update({n: ("psum", [128, 512], F32) for n in ("pv0", "pv1", "pc", "pp", "po0", "po1")})
+SCRATCH["pf"] = ("psum", [128, 8, 64], F32)
+SEMAPHORES = (["qV", "qS", "qP", "qG", "left"] + ["a%d" % e for e in range(9)] + ["b%d" % e for e in range(9)]
+              + ["m%d" % i for i in range(60)])
+BACK = [0, 1, 2, 3, 4, 6, 7, 8]
+BOTH = (0, 4, 8)
+VCH = [(0, 512), (512, 1024)]
+COPY = ["VVVV", "SV", "SV"] + ["GGGV"] * 6
+
+ORDER = {
+    "V": "m_oneb m_ones m_tab1 m_tab0 c_cdf c_b0 m_zj c_ct c_sf t_lo c_a0 c_ab m_zv A0_0 A0_1 vc0_0 A0_2 A0_3 vc0_2 vc0_1 vc0_3 vt0_0 vt0_1 "
+         "l_s1 A1_0 A1_1 m_zs m_neg vc1_1 l_s2 A2_0 vt1_0 l_s3 vt1_1 A2_1 m_pf vt2_0 vc2_1 m_vl vt2_1 A3_0 lfA ev2 A3_1 w1v0 lu0 A3_2 "
+         "w3_0 sc_0 w5_0 A3_3 vc3_3 vt3_0 vt3_1 w3_1 sc_1 w5_1 lf0 ev3 wV3 w3_2 sc_2 w5_2 A4_0 lu1 A4_1 A4_2 A4_3 vc4_3 vt4_0 vt4_1 ev4 "
+         "A5_0 A5_1 lf1 A5_2 A5_3 vc5_3 w3_3 sc_3 w5_3 vt5_0 vt5_1 A6_0 ev5 A6_1 A6_2 A6_3 vc6_3 w1v4 vt6_0 w3_4 sc_4 w5_4 vt6_1 "
+         "A7_0 A7_1 A7_2 A7_3 ev6 vc7_3 vt7_0 vt7_1 wV7 ev7 w3_5 sc_5 lu2 A8_0 A8_1 A8_2 A8_3 vc8_3 vt8_0 vt8_1 lf2 ev8 c_oa c_ob "
+         "rm3 rm1 rm0 rm2 w3_6 sc_6 w4_6 w5_6 rm4 rm5 w3_7 sc_7 w4_7 w5_7 rm6 rm7 rm8 w1v8 fb1_1 w3_8 sc_8 w5_8 fb1_0 fb2_0 fb2_1",
+    "S": "ld_b0 ld_a ld_ct ld_b t_hi B0_0 B0_1 B0_2 B0_3 B1_0 B1_1 e_s1 ev0 g_s1 vc1_0 B2_0 g_s2 e_x1 B2_1 vc2_0 g_s3 e_x2 e_s2 ev1 tap1 "
+         "B3_0 e_x3 B3_1 B3_2 w1_0 B3_3 cp1 edA gu0 w1_1 eu0 w1_2 ed0 wS3 B4_0 B4_1 B4_2 B4_3 gu1 wS4 B5_0 B5_1 B5_2 B5_3 eu1 w1_3 ed1 tap2 "
+         "B6_0 B6_1 cp2 B6_2 B6_3 w1_4 wS6 B7_0 B7_1 B7_2 B7_3 o_vi w1_5 wS7 B8_0 B8_1 gu2 B8_2 B8_3 eu2 o_v2 o_v0 w1_6 ed2 w1_7 o_v1 "
+         "w1_8 fa1 fa2 ef1 o_l1 ef2 o_l2",
+    "P": "p_t p_s pv0_0 pv0_1 x_s1 x_s2 pv1_0 pv1_1 x_s3 pv2_0 pv2_1 pu0 pdA w2_0 xu00 xu10 w2_1 xu20 xu30 pv3_0 pv3_1 pd0 w2_2 pu1 "
+         "xu01 xu11 pv4_0 pv4_1 xu21 xu31 pd1 w2_3 pv5_0 pv5_1 w2_4 pv6_0 pv6_1 w2_5 pv7_0 pv7_1 pu2 xu02 xu12 xu22 xu32 pv8_0 pv8_1 pd2 "
+         "w2_6 w2_7 w2_8 xf1 xf2",
+    "G": "io_id io_cd g_i16 g_fl0 g_fl3 g_psl g_zv0 g_zv g_zj0 g_zj sv0 g_fl1 g_pls sv1 g_fl2 g_nls g_zs0 g_zs sv2 vc3_0 vc3_1 sr0 vc3_2 "
+         "sr1 sv3 sr2 vc4_0 vc4_1 vc4_2 sv4 vc5_0 vc5_1 vc5_2 sr3 sv5 vc6_0 vc6_1 vc6_2 sr4 vc7_0 vc7_1 vc7_2 sv6 sv7 vc8_0 vc8_1 vc8_2 "
+         "sv8 sr6 sr7 sr8",
+    "Y": "ld_x ld_c16 ld_si ld_id dt_c tab_c dt_in dt_1 dt_2 dt_3 F0 tab_j F1 F2 lr0 lr1 F3 lr2 F4 lr3 F5 lr4 F6 F7 o_l0 F8 lr6 lr7 o_t",
+}
+
+
+def relays(rank_core, T, topo):
+    ok = [c for c in topo.cores_of(rank_core) if c != rank_core and all(topo.may_write(c, d) for d in T.cores)]
+    near = [c for c in ok if topo.die(c) == topo.die(rank_core)]
+    far = [c for c in ok if topo.die(c) != topo.die(rank_core)]
+    return near[0], far[0], near[1]
+
+
+def bits(engines):
+    return sum(1 << e for e in engines)
+
+
+def dst_id(d, src, topo):
+    rid, pid = topo.addr(d, src)
+    return DstId(rid=rid, pnc=pid)
+
+
+def deal(core, dests, each, topo):
+    masks = {}
+    used = []
+    for d in sorted(dests, key=lambda c: len(topo.engines(core, c))):
+        e = [x for x in topo.engines(core, d) if x not in used][:each]
+        used += e
+        masks[d] = bits(e)
+    return masks
+
+
+def relay_votes(g, core, s, which, T, topo):
+    n = len(T.cores)
+    dests = [T.cores[d] for d in range(n) if ((d - s) % n) % 2 == which]
+    masks = deal(core, dests, 2, topo)
+    for e in range(9):
+        g.wait_ge(T.sem["a%d" % e], 8)
+        g.remote_dma_fused([RemoteDMATransfer(dst_ids=[dst_id(d, core, topo)], dma_engine_mask=masks[d], remote_sem=T.sem["a%d" % e],
+                                              src=T.rd[e], dst=T.dv[8 * e + s]) for d in dests], local_sem=T.sem.left)
+    g.wait_ge(T.sem.left, 9 * 2 * len(dests))
+
+
+def back_sides(e, s, T):
+    if e < 5:
+        return [(T.ru1[e], T.ru2[8 * e + s])]
+    if e < 8:
+        return [(T.rh1[2 * (e - 6) + h], T.rh2[8 * (2 * (e - 6) + h) + s]) for h in range(2)]
+    return [(T.rf1[0], T.rf2[s])]
+
+
+def relay_results(g, core, s, T, topo):
+    masks = deal(core, list(T.cores), 1, topo)
+    n = 0
+    for e in BACK:
+        g.wait_ge(T.sem["b%d" % e], 16)
+        for a, b in back_sides(e, s, T):
+            g.remote_dma_fused([RemoteDMATransfer(dst_ids=[dst_id(d, core, topo)], dma_engine_mask=masks[d],
+                                                  remote_sem=T.sem["b%d" % e], src=a, dst=b) for d in T.cores],
+                               local_sem=T.sem.left)
+            n += len(T.cores)
+    g.wait_ge(T.sem.left, n)
+
+
+def rank_program(g, core, T, topo):
+    r = T.rank_of(core)
+    if r is None:
+        for s, c in enumerate(T.cores):
+            if core in topo.cores_of(c):
+                ra, rb, rc = relays(c, T, topo)
+                if core == ra:
+                    relay_votes(g, core, s, 0, T, topo)
+                elif core == rb:
+                    relay_votes(g, core, s, 1, T, topo)
+                elif core == rc:
+                    relay_results(g, core, s, T, topo)
+        return
+    ra, rb, rc = relays(core, T, topo)
+    V, S, PE, SY = g.vector, g.scalar, g.tensor, g.sync
+    defs = {}
+    vb = [T.vb0, T.vb1, T.vb2]
+    wb = [T.vb0, T.wb1, T.wb2]
+
+    def op(name, fn, deps=()):
+        defs[name] = ("op", fn, list(deps))
+
+    def dma(name, pairs, deps=()):
+        defs[name] = ("dma", pairs, list(deps))
+
+    def mm(out, parts):
+        def fn():
+            ins = None
+            for j, (lhs, rhs, st, sp) in enumerate(parts):
+                ins = PE.matmul(out[j], lhs, rhs, st, sp)
+            return ins
+        return fn
+
+    def pick(out, rhs_of, lhs_of):
+        return mm([out] * 16, [(lhs_of(i), rhs_of(i), i == 0, i == 15) for i in range(16)])
+
+    def zrow(j):
+        return lambda i: T.zj[:, j, 15 - i:143 - i]
+
+    def copy(q, out, src):
+        if q == "S":
+            return lambda: S.activation(out, src, ACT.Copy)
+        return lambda: V.tensor_copy(out, src)
+
+    def after(name, c):
+        return ["~%s_%d" % (name, c - 1)] if c else []
+
+    mine = slice(16 * r, 16 * r + 16)
+    dma("ld_b0", [(T.fi[:, 320:384], T.fb[:, 0:64])])
+    dma("ld_x", [(T.vb0[:, 0:1024], T.x[:])])
+    dma("ld_a", [(T.fi[:, 0:192], T.fa[:])])
+    dma("ld_b", [(T.fi[:, 192:320], T.fb[:, 64:192])])
+    dma("ld_ct", [(T.ci[:, 0:192], T.cd[:]), (T.ci[:, 192:256], T.tp[:])])
+    dma("ld_c16", [(T.cdi[0:16, 64:256], T.cd[mine, :])])
+    dma("ld_si", [(T.si[:, 8 * l:8 * l + 8], T.cd[mine, 64 * l:64 * l + 64]) for l in range(3)] + [(T.si[:, 40:48], T.tp[mine, :])])
+    dma("ld_id", [(T.si[:, 24 + 8 * l:32 + 8 * l], T.idw[0:16, 64 * l:64 * l + 64]) for l in range(2)], ["io_id"])
+    for nm, ap, val in [("ones", T.ones[:], 1.0), ("neg", T.neg[:], -1.0), ("oneb", T.oneb[:], 1.0), ("zv", T.zv[:], 0.0),
+                        ("zj", T.zj[:], 0.0), ("zs", T.zs[:], 0.0), ("vl", T.vl[:, :, 5], 0.0), ("tab0", T.tab[:, 0:2048], 0.0),
+                        ("tab1", T.tab[:, 2048:4096], 0.0),
+                        ("pf", T.pf[:, :, 0:5], 1.0)]:
+        op("m_" + nm, lambda ap=ap, val=val: V.memset(ap, val))
+    op("io_cd", lambda: g.iota(T.cdi[0:16, 0:64], [[16, 64]], 0, 1))
+    op("io_id", lambda: g.iota(T.idw[0:16, :], [[16, 128]], 1024, 1))
+    zvv, zjv, zsv = T.zv[:, 15:143:16], T.zj[:, :, 15:143:16], T.zs[:, 120:128]
+    for nm, out, src, pat, cmp, base, cm, deps in [
+            ("i16", T.i16[0:16, :], T.ones[0:16, 0:16], [[-1, 16]], ALU.is_equal, 0, 1, ["m_ones"]),
+            ("psl", T.psl[:], T.ones[:], [[-1, 8], [-8, 16]], ALU.is_equal, 0, 1, ["m_ones"]),
+            ("pls", T.pls[:], T.ones[:], [[-1, 16], [-16, 8]], ALU.is_equal, 0, 1, ["m_ones"]),
+            ("nls", T.nls[:], T.neg[:], [[-1, 16], [-16, 8]], ALU.is_equal, 0, 1, ["m_neg"]),
+            ("zv0", zvv, T.oneb[:, 0, :], [[-16, 8]], ALU.is_ge, 0, 1, ["m_oneb", "m_zv"]),
+            ("zj0", zjv, T.oneb[:], [[-2, 4], [-16, 8]], ALU.is_ge, 0, 1, ["m_oneb", "m_zj"]),
+            ("zs0", zsv, T.oneb[:, 0, :], [[-16, 8]], ALU.is_ge, -8, 1, ["m_oneb", "m_zs"]),
+            ("zv", zvv, zvv, [[16, 8]], ALU.is_ge, 15, -1, ["g_zv0"]),
+            ("zj", zjv, zjv, [[2, 4], [16, 8]], ALU.is_ge, 1, -1, ["g_zj0"]),
+            ("zs", zsv, zsv, [[16, 8]], ALU.is_ge, 15, -1, ["g_zs0"])]:
+        op("g_" + nm, lambda a=(out, src, pat, cmp, 0.0, base, cm): g.affine_select(*a), deps)
+    for j in range(4):
+        op("g_fl%d" % j, lambda j=j: g.iota(T.fl[:, 1024 * j:1024 * j + 1024], [[0, 1024]], 0, 0, allow_small_or_imprecise_dtypes=True))
+    op("c_b0", copy("V", T.lab[:, 320:384], T.fi[:, 320:384]), ["ld_b0"])
+    op("c_a0", copy("V", T.lab[:, 0:64], T.fi[:, 0:64]), ["ld_a"])
+    op("c_ab", copy("V", T.lab[:, 64:320], T.fi[:, 64:320]), ["ld_a", "ld_b"])
+    op("c_ct", copy("V", T.lct[:], T.ci[:]), ["ld_ct"])
+    op("c_oa", copy("V", T.oo[:, 0:64], T.fi[:, 0:64]), ["ld_a", "~vt8_1"])
+    op("c_ob", copy("V", T.oo[:, 64:128], T.fi[:, 320:384]), ["ld_b0", "~vt8_1"])
+    dma("o_l0", [(T.ya[:, 0:64], T.oo[:, 0:64]), (T.yb[:, 0:64], T.oo[:, 64:128])], ["c_oa", "c_ob"])
+    X = T.fi[:, 64:320]
+    rm = [T.rm[:, 256 * i:256 * i + 256] for i in range(8)]
+    ab = ["ld_a", "ld_b", "~vt8_1"]
+    op("rm0", lambda: V.tensor_scalar(rm[0], X, 15, None, ALU.bitwise_and), ab)
+    op("rm1", lambda: V.tensor_scalar(rm[1], X, 4, 63, ALU.logical_shift_right, ALU.bitwise_and), ab)
+    op("rm2", lambda: V.tensor_scalar(rm[2], X, 1024.0, 63.0, ALU.is_ge, ALU.mult), ab)
+    op("rm3", lambda: V.tensor_scalar(rm[3], X, 1024.0, -15.0, ALU.is_ge, ALU.mult), ab)
+    op("rm4", lambda: V.tensor_tensor(rm[4], rm[0], rm[2], ALU.mult), ["rm0", "rm2"])
+    op("rm5", lambda: V.tensor_tensor(rm[5], rm[1], rm[3], ALU.mult), ["rm1", "rm3"])
+    op("rm6", lambda: V.tensor_tensor(rm[6], rm[4], X, ALU.add), ["rm4"])
+    op("rm7", lambda: V.tensor_tensor(rm[7], rm[6], rm[5], ALU.add), ["rm5", "rm6"])
+    op("rm8", copy("V", T.lfin[:], rm[7]), ["rm7"])
+    op("c_cdf", copy("V", T.cdf[0:16, :], T.cdi[0:16, :]), ["ld_c16", "io_cd"])
+    op("p_t", mm([T.po0[:, 0:16], T.po0[:, 16:32]], [(T.cdf[0:16, 128 * h:128 * h + 128], T.i16[0:16, :], True, True) for h in range(2)]),
+       ["c_cdf", "g_i16"])
+    op("t_hi", copy("S", T.thl[:, 0:32], T.po0[:, 0:32]), ["p_t"])
+    op("t_lo", lambda: V.tensor_tensor(T.thl[:, 32:64], T.po0[:, 0:32], T.thl[:, 0:32], ALU.subtract), ["t_hi"])
+    dma("dt_c", [(T.dt[h, 2048 * a:2048 * a + 2048], T.thl[:, 32 * h + 16 * a:32 * h + 16 * a + 16]) for h in range(2) for a in range(2)],
+        ["t_hi", "t_lo"])
+    dma("tab_c", [(T.tab[16 * a:16 * a + 2, :], T.dt[0:2, :]) for a in range(8)], ["dt_c", "m_tab0", "m_tab1"])
+    dma("dt_in", [(T.dt[2 * j:2 * j + 2, 0:1024], T.dt[0:2, 0:1024]) for j in range(1, 4)], ["dt_c"])
+    op("c_sf", copy("V", T.sf[:], T.si[:]), ["ld_si", "ld_id"])
+    op("p_s", mm([T.pp[:, 0:48]], [(T.psl[:], T.sf[:], True, True)]), ["c_sf", "g_psl"])
+    op("l_s1", copy("V", T.lu[:, 0:24], T.pp[:, 0:24]), ["p_s"])
+    op("e_s1", copy("S", T.vl[:, 0:24, 3], T.pp[:, 0:24]), ["l_s1"])
+    op("e_s2", copy("S", T.vl[:, 0:16, 4], T.pp[:, 24:40]), ["l_s1"])
+    for j in range(1, 4):
+        c0 = 384 * (j - 1)
+        op("g_s%d" % j, copy("S", T.gch[:, c0:c0 + 384], T.tab[:, :].indirect(T.lu[:, 24 * (j - 1):24 * j])), ["l_s%d" % j, "tab_c"])
+        op("x_s%d" % j, pick(T.pc[:, 0:24], lambda i, c0=c0: T.gch[:, c0 + i:c0 + 384:16], zrow(0)),
+           ["g_s%d" % j, "g_zj"] + (["e_x%d" % (j - 1)] if j > 1 else []))
+        if j < 3:
+            op("l_s%d" % (j + 1), copy("V", T.lu[:, 24 * j:24 * j + 24], T.pc[:, 0:24]), ["x_s%d" % j])
+        op("e_x%d" % j, copy("S", T.vl[:, 0:24, 3 - j], T.pc[:, 0:24]), ["l_s%d" % (j + 1) if j < 3 else "x_s3"])
+        dma("dt_%d" % j, [(T.dt[2 * j + h, 1024 * (l + 1):1024 * (l + 2)], T.gch[h:128:16, c0 + 128 * l:c0 + 128 * l + 128])
+                          for h in range(2) for l in range(3)], ["g_s%d" % j])
+    dma("tab_j", [(T.tab[16 * a + 2:16 * a + 8, :], T.dt[2:8, :]) for a in range(8)], ["dt_1", "dt_2", "dt_3", "dt_in"])
+
+    def finish(tag, a, b, deps, pp_free):
+        n = b - a
+        op("lf" + tag, copy("V", T.lf[:, 4 * a:4 * b], T.vl[:, a:b, 1:5]), deps)
+        op("pd" + tag, mm([T.pp[:, 0:5 * n]] * 2, [(T.pls[:], T.vl[:, a:b, 0:5], True, False), (T.nls[:], T.vl[:, a:b, 1:6], False, True)]),
+           deps + ["g_pls", "g_nls", "m_vl"] + pp_free)
+        op("ed" + tag, copy("S", T.d1[:, 5 * a:5 * b], T.pp[:, 0:5 * n]), ["pd" + tag])
+
+    finish("A", 0, 16, ["e_s1", "e_s2", "e_x1", "e_x2", "e_x3"], [])
+
+    def chain(t, a, n, c0, u_rhs, deps, before):
+        op("pu" + t, mm([T.pc[:, 4:5 * n:5]], [(T.psl[:], u_rhs, True, True)]), deps + ["e_x3" if before == "A" else "eu" + before])
+        lst = T.lu[:, c0:c0 + n]
+        op("lu" + t, copy("V", lst, T.pc[:, 4:5 * n:5]), ["pu" + t])
+        op("gu" + t, copy("S", T.gch[:, 16 * c0:16 * (c0 + n)], T.tab[:, :].indirect(lst)), ["lu" + t, "tab_j"])
+        for j in range(4):
+            op("xu%d" % j + t, pick(T.pc[:, 3 - j:5 * n:5], lambda i: T.gch[:, 16 * c0 + i:16 * (c0 + n):16], zrow(j)),
+               ["gu" + t] + (["~xu%d" % (j - 1) + t] if j else []))
+        op("eu" + t, copy("S", T.vl[:, a:a + n, 0:5], T.pc[:, 0:5 * n]), ["xu3" + t])
+        finish(t, a, a + n, ["eu" + t], ["ed" + before])
+
+    TAG = ["A", "A", "0", "1", "1", "1", "2", "2", "2"]
+    chain("0", 24, 8, 72, T.sf[:, 40:48], ["c_sf"], "A")
+    for k in (1, 2):
+        chain("%d" % k, 32 * k, 24, 72 + 24 * k, T.rs[:, 120 * (k - 1) + 4:120 * k:5], ["sc_%d" % e for e in range(3 * k - 3, 3 * k)],
+              TAG[3 * k - 1])
+
+    acol, bcol = [0, 64, 128], [320, 192, 256]
+    dsta = [dst_id(c, core, topo) for c in (ra, rb, rc)]
+    eng = topo.engines(core, ra)
+    half = [bits(eng[:len(eng) // 2]), bits(eng[len(eng) // 2:])]
+    nleft = 0
+    done = []
+    for e in range(9):
+        k, l = divmod(e, 3)
+        win = (vb[k] if l == 0 else wb[k])[:, 0:1024 * (l + 1)]
+        chunks = len(COPY[e])
+        n = 1024 // chunks
+        if e == 0:
+            need = ["ld_x"]
+        elif l == 0:
+            need = ["tap%d" % k]
+        elif k == 0:
+            need = done
+        else:
+            need = ["wS%d" % (e - 1), "cp%d" % k] + (["wV%d" % (e - 1)] if e in BOTH else [])
+        for c in range(chunks):
+            t = T.tb[:, 1024 * e + n * c:1024 * e + n * (c + 1)]
+            lb = T.lab[:, bcol[l] + n // 16 * c:bcol[l] + n // 16 * (c + 1)]
+            la = T.lab[:, acol[l] + n // 16 * c:acol[l] + n // 16 * (c + 1)]
+            out = vb[k][:, 1024 * (l + 1) + n * c:1024 * (l + 1) + n * (c + 1)]
+            op("B%d_%d" % (e, c), lambda t=t, lb=lb, win=win: S.activation(t, win.indirect(lb), ACT.Identity, bias=255.0, scale=-1.0),
+               need + ["c_b0" if l == 0 else "c_ab"] + after("B%d" % e, c))
+            op("A%d_%d" % (e, c), lambda t=t, la=la, win=win, out=out: V.tensor_tensor(out, win.indirect(la), t, ALU.min),
+               need + ["B%d_%d" % (e, c), "c_a0" if l == 0 else "c_ab"] + after("A%d" % e, c))
+            cp = T.vc[:, 1024 * e + n * c:1024 * e + n * (c + 1)]
+            if COPY[e][c] == "G":
+                op("vc%d_%d" % (e, c), lambda cp=cp, out=out, n=n: g.affine_select(cp, out, [[0, n]], ALU.is_ge, 0.0, 0, 0),
+                   ["A%d_%d" % (e, c)])
+            else:
+                op("vc%d_%d" % (e, c), copy(COPY[e][c], cp, out), ["A%d_%d" % (e, c)])
+        done = ["A%d_%d" % (e, c) for c in range(chunks)]
+        full = vb[k][:, 0:1024 * (l + 2)]
+        pv = [T.pv0, T.pv1][e % 2][:, 0:64]
+        for c, (a, b) in enumerate(VCH):
+            op("vt%d_%d" % (e, c), lambda a=a, b=b, e=e, l=l, full=full: V.tensor_tensor(
+                T.df[:, 1024 * e + a:1024 * e + b], full.indirect(T.lct[:, 64 * l + a // 16:64 * l + b // 16]),
+                T.vc[:, 1024 * e + a:1024 * e + b], ALU.not_equal),
+               done + ["vc%d_%d" % (e, j) for j in range(a // n, (b + n - 1) // n)] + ["c_ct"] + after("vt%d" % e, c))
+            ii = range(a // 64, b // 64)
+            op("pv%d_%d" % (e, c), mm([pv] * len(ii), [(T.zv[:, 15 - i:143 - i], T.df[:, 1024 * e + 64 * i:1024 * e + 64 * i + 64],
+                                                        i == 0, i == 15) for i in ii]),
+               ["vt%d_%d" % (e, c), "g_zv"] + after("pv%d" % e, c) + (["ev%d" % (e - 2)] if e > 1 else []))
+        xv = T.xv[:, 64 * e:64 * e + 64]
+        op("ev%d" % e, copy("S" if e < 2 else "V", xv, pv), ["pv%d_%d" % (e, len(VCH) - 1)])
+        defs["sv%d" % e] = ("rem", [RemoteDMATransfer(dst_ids=[dsta[h]], dma_engine_mask=half[h], remote_sem=T.sem["a%d" % e],
+                                                      src=xv, dst=T.rd[e]) for h in range(2)], ["ev%d" % e])
+        nleft += len(eng)
+        if k > 0 and l < 2:
+            lst0 = 64 * (e - 3)
+            for q, a, b in ([("S", 0, 512), ("V", 512, 1024)] if e + 1 in BOTH else [("S", 0, 1024)]):
+                op("w%s%d" % (q, e), copy(q, wb[k][:, 1024 * (l + 1) + a:1024 * (l + 1) + b],
+                                          full.indirect(T.lr[:, lst0 + a // 16:lst0 + b // 16])), done + ["lr%d" % (e - 3)])
+        if l == 2 and k < 2:
+            lst = T.lct[:, 192:256] if k == 0 else T.lr[:, 128:192]
+            op("tap%d" % (k + 1), copy("S", vb[k + 1][:, 0:1024], full.indirect(lst)), done + (["c_ct"] if k == 0 else ["lr2"]))
+            dma("cp%d" % (k + 1), [(wb[k + 1][:, 0:1024], vb[k + 1][:, 0:1024])], ["tap%d" % (k + 1)])
+        if k == 2:
+            if l == 0:
+                dma("o_vi", [(T.yv[:, 0:1024], T.vb2[:, 0:1024])], ["tap2"])
+            dma("o_v%d" % l, [(T.yv[:, 1024 * (l + 1):1024 * (l + 2)], T.vb2[:, 1024 * (l + 1):1024 * (l + 2)])], done)
+        defs["av%d" % e] = ("ext", T.sem["a%d" % e], 16)
+        war = ["g_fl%d" % (l + 1)] if k == 0 else ["w1_%d" % (3 * k - 1), "w1v%d" % BOTH[k - 1]]
+        dma("F%d" % e, [(T.fl[16 * a + 8:16 * a + 16, 1024 * (l + 1):1024 * (l + 2)], T.dv[8 * e:8 * e + 8, mine, :]) for a in range(8)],
+            war + ["av%d" % e])
+        a0 = 32 * k + (24 if e == 2 else 8 * l)
+        parts = [("S", "w1_", 0, 16), ("V", "w1v", 16, 32)] if e in BOTH else [("S", "w1_", 0, 32)]
+        for q, nm, a, b in parts:
+            op(nm + "%d" % e, copy(q, T.gf[:, 512 * e + 16 * a:512 * e + 16 * b],
+                                   T.fl[:, 0:1024 * (l + 2)].indirect(T.lf[:, 4 * a0 + a:4 * a0 + b])),
+               ["F%d" % e, "lf" + TAG[e]] + (["g_fl0"] if e == 0 else ["F%d" % (e - 1), "~w1_%d" % (e - 1)]))
+        op("w2_%d" % e, pick(T.pf[:, :, 1:5], lambda i, e=e: T.gf[:, 512 * e + i:512 * e + 512:16], lambda i: T.zs[:, 120 - 8 * i:248 - 8 * i]),
+           [nm + "%d" % e for q, nm, a, b in parts] + ["g_zs", "m_pf"] + (["w3_%d" % (e - 1)] if e else []))
+        op("w3_%d" % e, lambda e=e: V.tensor_scalar(T.d0[:, 40 * e:40 * e + 40], T.pf[:, :, 0:5], 0.0, None, ALU.is_equal), ["w2_%d" % e])
+        op("sc_%d" % e, lambda e=e, a0=a0: V.tensor_tensor_scan(T.rs[:, 40 * e:40 * e + 40], T.d0[:, 40 * e:40 * e + 40],
+                                                               T.d1[:, 5 * a0:5 * a0 + 40], 0.0, ALU.mult, ALU.add),
+           ["w3_%d" % e, "ed" + TAG[e]])
+        res = T.rs[:, 40 * e + 4:40 * e + 40:5]
+        if e in BACK:
+            sem = T.sem["b%d" % e]
+            nleft += len(eng)
+            if e < 5 or e == 8:
+                tile = T.ru[:, 8 * e:8 * e + 8] if e < 5 else T.rf[:]
+                op("w5_%d" % e, copy("V", tile, res), ["sc_%d" % e])
+                tr = [(tile, back_sides(e, r, T)[0][0], bits(eng))]
+            else:
+                hi, lo = [T.rh[:, 16 * (e - 6) + 8 * h:16 * (e - 6) + 8 * h + 8] for h in range(2)]
+                op("w4_%d" % e, copy("V", hi, res), ["sc_%d" % e])
+                op("w5_%d" % e, lambda hi=hi, lo=lo, res=res: V.tensor_tensor(lo, res, hi, ALU.subtract), ["w4_%d" % e])
+                tr = [((hi, lo)[h], back_sides(e, r, T)[h][0], half[h]) for h in range(2)]
+            defs["sr%d" % e] = ("rem", [RemoteDMATransfer(dst_ids=[dsta[2]], dma_engine_mask=m, remote_sem=sem, src=a, dst=b)
+                                        for a, b, m in tr], ["w5_%d" % e])
+            defs["ar%d" % e] = ("ext", sem, 8 * len(tr))
+            if e < 5:
+                dma("lr%d" % e, [(T.lr[:, 64 * e:64 * e + 64], T.ru2[8 * e:8 * e + 8])], ["ar%d" % e])
+            elif e < 8:
+                dma("lr%d" % e, [(T.tab[h:128:16, 1024 * (l + 1):1024 * (l + 2)], T.rh2[8 * (2 * l + h):8 * (2 * l + h) + 8])
+                                 for h in range(2)], ["ar%d" % e, "gu2"])
+            else:
+                dma("o_t", [(T.yt[:], T.rf2[:])], ["ar8"])
+    for l in (1, 2):
+        c0 = 2048 * (l - 1)
+        fw = T.tab[:, 0:1024 * (l + 1)]
+        deps = ["rm8", "lr6"] + (["lr7"] if l == 2 else [])
+        op("fa%d" % l, copy("S", T.gfin[:, c0:c0 + 1024], fw.indirect(T.lfin[:, 64 * (l - 1):64 * l])), deps)
+        for h in range(2):
+            op("fb%d_%d" % (l, h), copy("V", T.gfin[:, c0 + 1024 + 512 * h:c0 + 1536 + 512 * h],
+                                        fw.indirect(T.lfin[:, 64 * (l + 1) + 32 * h:64 * (l + 1) + 32 * h + 32])), deps)
+        po = [T.po0, T.po1][l - 1][:, 0:128]
+        op("xf%d" % l, pick(po, lambda i, c0=c0: T.gfin[:, c0 + i:c0 + 2048:16], zrow(0)), ["fa%d" % l, "fb%d_0" % l, "fb%d_1" % l, "t_lo"])
+        op("ef%d" % l, copy("S", T.oo[:, 128 * l:128 * l + 128], po), ["xf%d" % l])
+        dma("o_l%d" % l, [(T.ya[:, 64 * l:64 * l + 64], T.oo[:, 128 * l:128 * l + 64]),
+                          (T.yb[:, 64 * l:64 * l + 64], T.oo[:, 128 * l + 64:128 * l + 128])], ["ef%d" % l])
+
+    order = {
+        q: s for q, s in ORDER.items()}
+    queue = {"V": V, "S": S, "P": PE, "G": g, "Y": SY}
+    order = {q: s.split() for q, s in order.items()}
+    wanted = set(d for v in defs.values() if v[0] != "ext" for d in v[2] if d[0] != "~")
+    token, nd = {}, 0
+    for name, v in defs.items():
+        if v[0] == "ext":
+            token[name] = (name, v[1], v[2])
+    for q, names in order.items():
+        cnt = 0
+        for name in names:
+            kind = defs[name][0]
+            if kind == "op" and name in wanted:
+                cnt += 1
+                token[name] = ("q" + q, T.sem["q" + q], cnt)
+            elif kind == "dma":
+                token[name] = ("m%d" % nd, T.sem["m%d" % nd], 16 * len(defs[name][1]))
+                nd += 1
+    placed = [n for names in order.values() for n in names]
+    assert sorted(placed) == sorted(n for n, v in defs.items() if v[0] != "ext")
+    waited = {}
+    for q, names in order.items():
+        seen = {}
+        for name in names:
+            kind, what, deps = defs[name]
+            most = {}
+            for d in [d for d in deps if d[0] != "~"]:
+                key, sem, val = token[d]
+                if val > most.get(key, (None, 0))[1]:
+                    most[key] = (sem, val)
+            for key, (sem, val) in most.items():
+                if val > seen.get(key, 0):
+                    queue[q].wait_ge(sem, val)
+                    seen[key] = val
+                    waited[key] = max(waited.get(key, 0), val)
+            if kind == "op":
+                ins = what()
+                if name in wanted:
+                    ins.then_inc(token[name][1], 1)
+            elif kind == "dma":
+                for out, src in what:
+                    queue[q].dma_start(out, src).then_inc(token[name][1], 16)
+            else:
+                g.remote_dma_fused(what, local_sem=T.sem.left)
+    g.wait_ge(T.sem.left, nleft)
+    for name, (key, sem, val) in token.items():
+        if val > waited.get(key, 0):
+            g.wait_ge(sem, val)

@@ -4,52 +4,44 @@ from concourse.mybir import AluOpType as ALU, ActivationFunctionType as ACT
 B16, F32, I32, U16 = "bfloat16", "float32", "int32", "uint16"
 SCRATCH = {n: ("sbuf", [128] + list(s), d) for n, s, d in [
     ("vb0", [4096], B16), ("vb1", [4096], B16), ("vb2", [4096], B16), ("wb1", [3072], B16), ("wb2", [3072], B16),
-    ("tb", [9216], B16), ("df", [9216], B16), ("vc", [9216], B16), ("tab", [4096], B16), ("fl", [4096], B16),
-    ("gf", [9 * 512], B16), ("gch", [6 * 384], B16), ("gfin", [4096], B16), ("fi", [384], I32), ("ci", [256], I32),
-    ("lab", [384], U16), ("lct", [256], U16), ("lr", [5 * 64], U16), ("lfin", [256], U16), ("rm", [8 * 256], I32),
+    ("t0", [4096], B16), ("tb", [6144], B16), ("df", [9216], B16), ("vc", [9216], B16), ("tab", [4096], B16), ("tx", [1024], B16),
+    ("gf", [9 * 512], B16), ("gch", [2048], B16), ("gfin", [4096], B16), ("fi", [384], I32), ("ci", [256], I32), ("ci2", [192], I32),
+    ("lab", [384], U16), ("lab2", [384], U16), ("lct", [256], U16), ("lc2", [192], U16), ("lr", [5 * 64], U16),
     ("cdi", [256], I32), ("cdf", [256], F32), ("idw", [128], I32), ("thl", [64], B16), ("si", [48], I32), ("sf", [48], F32),
-    ("ones", [128], F32), ("neg", [128], F32), ("oneb", [4, 8], B16), ("zv", [144], B16), ("zj", [4, 144], B16), ("zs", [256], B16),
-    ("i16", [16], F32), ("pls", [128], F32), ("nls", [128], F32), ("psl", [128], F32),
-    ("vl", [96, 6], F32), ("lf", [96 * 4], U16), ("d1", [96 * 5], F32), ("d0", [72 * 5], F32), ("rs", [72 * 5], F32),
-    ("lu", [6 * 24], U16), ("xv", [9 * 64], B16), ("ru", [5 * 8], U16), ("rh", [4 * 8], B16), ("rf", [8], F32), ("oo", [384], F32)]}
+    ("ones", [128], F32), ("oneb", [128], B16), ("one4", [4, 8], B16), ("zv", [144], B16), ("zu", [144], B16), ("zo", [144], B16),
+    ("z1", [144], B16), ("zj", [4, 144], B16), ("zs", [256], B16), ("i16", [16], F32), ("e16", [16], F32), ("f16", [128], F32),
+    ("ee", [128], F32), ("own", [64], F32), ("pls", [128], F32), ("psl", [128], F32), ("oi", [8], I32), ("of", [4], U16),
+    ("eye", [128], F32), ("big", [8], B16), ("vl", [80 * 8], F32), ("lf", [72 * 4], U16), ("rs", [72 * 8], F32),
+    ("lu", [144], U16), ("xv", [9 * 64], B16), ("mk", [7 * 64], F32), ("rh", [32], B16), ("rf", [8], F32), ("oo", [384], F32)]}
 SCRATCH.update({n: ("dram", s, d) for n, s, d in [
-    ("dt", [8, 4096], B16), ("rd", [9, 128, 64], B16), ("dv", [72, 128, 64], B16), ("ru1", [5, 128, 8], U16), ("ru2", [40, 128, 8], U16),
-    ("rh1", [4, 128, 8], B16), ("rh2", [32, 128, 8], B16), ("rf1", [1, 128, 8], F32), ("rf2", [8, 128, 8], F32)]})
-SCRATCH.update({n: ("psum", [128, 512], F32) for n in ("pv0", "pv1", "pc", "pp", "po0", "po1")})
-SCRATCH["pf"] = ("psum", [128, 8, 64], F32)
-SEMAPHORES = (["qV", "qS", "qP", "qG", "left"] + ["a%d" % e for e in range(9)] + ["b%d" % e for e in range(9)]
-              + ["m%d" % i for i in range(60)])
-BACK = [0, 1, 2, 3, 4, 6, 7, 8]
-BOTH = (0, 4, 8)
-VCH = [(0, 512), (512, 1024)]
-COPY = ["VVVV", "SV", "SV"] + ["GGGV"] * 6
-
-ORDER = {
-    "V": "m_oneb m_ones m_tab1 m_tab0 c_cdf c_b0 m_zj c_ct c_sf t_lo c_a0 c_ab m_zv A0_0 A0_1 vc0_0 A0_2 A0_3 vc0_2 vc0_1 vc0_3 vt0_0 vt0_1 "
-         "l_s1 A1_0 A1_1 m_zs m_neg vc1_1 l_s2 A2_0 vt1_0 l_s3 vt1_1 A2_1 m_pf vt2_0 vc2_1 m_vl vt2_1 A3_0 lfA ev2 A3_1 w1v0 lu0 A3_2 "
-         "w3_0 sc_0 w5_0 A3_3 vc3_3 vt3_0 vt3_1 w3_1 sc_1 w5_1 lf0 ev3 wV3 w3_2 sc_2 w5_2 A4_0 lu1 A4_1 A4_2 A4_3 vc4_3 vt4_0 vt4_1 ev4 "
-         "A5_0 A5_1 lf1 A5_2 A5_3 vc5_3 w3_3 sc_3 w5_3 vt5_0 vt5_1 A6_0 ev5 A6_1 A6_2 A6_3 vc6_3 w1v4 vt6_0 w3_4 sc_4 w5_4 vt6_1 "
-         "A7_0 A7_1 A7_2 A7_3 ev6 vc7_3 vt7_0 vt7_1 wV7 ev7 w3_5 sc_5 lu2 A8_0 A8_1 A8_2 A8_3 vc8_3 vt8_0 vt8_1 lf2 ev8 c_oa c_ob "
-         "rm3 rm1 rm0 rm2 w3_6 sc_6 w4_6 w5_6 rm4 rm5 w3_7 sc_7 w4_7 w5_7 rm6 rm7 rm8 w1v8 fb1_1 w3_8 sc_8 w5_8 fb1_0 fb2_0 fb2_1",
-    "S": "ld_b0 ld_a ld_ct ld_b t_hi B0_0 B0_1 B0_2 B0_3 B1_0 B1_1 e_s1 ev0 g_s1 vc1_0 B2_0 g_s2 e_x1 B2_1 vc2_0 g_s3 e_x2 e_s2 ev1 tap1 "
-         "B3_0 e_x3 B3_1 B3_2 w1_0 B3_3 cp1 edA gu0 w1_1 eu0 w1_2 ed0 wS3 B4_0 B4_1 B4_2 B4_3 gu1 wS4 B5_0 B5_1 B5_2 B5_3 eu1 w1_3 ed1 tap2 "
-         "B6_0 B6_1 cp2 B6_2 B6_3 w1_4 wS6 B7_0 B7_1 B7_2 B7_3 o_vi w1_5 wS7 B8_0 B8_1 gu2 B8_2 B8_3 eu2 o_v2 o_v0 w1_6 ed2 w1_7 o_v1 "
-         "w1_8 fa1 fa2 ef1 o_l1 ef2 o_l2",
-    "P": "p_t p_s pv0_0 pv0_1 x_s1 x_s2 pv1_0 pv1_1 x_s3 pv2_0 pv2_1 pu0 pdA w2_0 xu00 xu10 w2_1 xu20 xu30 pv3_0 pv3_1 pd0 w2_2 pu1 "
-         "xu01 xu11 pv4_0 pv4_1 xu21 xu31 pd1 w2_3 pv5_0 pv5_1 w2_4 pv6_0 pv6_1 w2_5 pv7_0 pv7_1 pu2 xu02 xu12 xu22 xu32 pv8_0 pv8_1 pd2 "
-         "w2_6 w2_7 w2_8 xf1 xf2",
-    "G": "io_id io_cd g_i16 g_fl0 g_fl3 g_psl g_zv0 g_zv g_zj0 g_zj sv0 g_fl1 g_pls sv1 g_fl2 g_nls g_zs0 g_zs sv2 vc3_0 vc3_1 sr0 vc3_2 "
-         "sr1 sv3 sr2 vc4_0 vc4_1 vc4_2 sv4 vc5_0 vc5_1 vc5_2 sr3 sv5 vc6_0 vc6_1 vc6_2 sr4 vc7_0 vc7_1 vc7_2 sv6 sv7 vc8_0 vc8_1 vc8_2 "
-         "sv8 sr6 sr7 sr8",
-    "Y": "ld_x ld_c16 ld_si ld_id dt_c tab_c dt_in dt_1 dt_2 dt_3 F0 tab_j F1 F2 lr0 lr1 F3 lr2 F4 lr3 F5 lr4 F6 F7 o_l0 F8 lr6 lr7 o_t",
-}
+    ("dt", [8, 4096], B16), ("hl", [4, 128, 96], U16), ("kl", [32, 128, 12], U16), ("hq", [8, 128, 256], B16), ("kq", [64, 128, 32], B16),
+    ("hh", [6, 128, 512], B16), ("kh", [48, 128, 64], B16), ("hv", [3, 128, 64], B16), ("kv", [24, 128, 64], B16),
+    ("hr", [2, 128, 16], B16), ("kr", [16, 128, 16], B16), ("ht", [1, 128, 8], F32), ("kt", [8, 128, 8], F32)]})
+SCRATCH.update({n: ("psum", [128, 512], F32) for n in ("pv0", "pv1", "pp", "po0", "po1", "pl", "pf", "pc")})
+AT = [7, 5, 3, 1, 0]
+BIG = 4096.0
+MSG = {"L": (True, "l", [(h, h, None) for h in range(4)]),
+       "X0": (True, "q", [(0, 0, None), (2, 1, None)]), "X1": (True, "q", [(1, 2, None), (3, 3, None)]),
+       "Yi": (True, "h", [(0, 0, None), (2, 1, None)]), "Y0": (True, "h", [(1, 2, None), (3, 3, None)]),
+       "Y1": (True, "h", [(0, 4, None), (2, 5, None)]),
+       "Y20": (True, "q", [(0, 4, None), (2, 5, None)]), "Y21": (True, "q", [(0, 6, None), (2, 7, None)]),
+       "V0": (False, "v", [(1, 0, 0), (3, 0, 1)]), "V1": (False, "v", [(1, 1, 0), (3, 1, 1)]), "V2": (False, "v", [(1, 2, 0), (3, 2, 1)]),
+       "R6": (False, "r", [(1, 0, None)]), "R7": (False, "r", [(1, 1, None)]), "T": (False, "t", [(1, 0, None)])}
+SEMAPHORES = ["qV", "qS", "qP", "qG", "left"] + ["a" + m for m in MSG] + ["m%d" % i for i in range(70)]
+HALVES, QUARTERS = [(0, 512), (512, 1024)], [(0, 256), (256, 512), (512, 768), (768, 1024)]
+CUTS = [QUARTERS] * 3 + [HALVES] * 5 + [[(0, 512), (512, 768), (768, 1024)]]
+COPY = [""] * 3 + ["YG"] * 5 + ["GSS"]
+WIDE = (7, 8)
+SHARE = {"w1_7": 2, "w1_8": 2, "tap2": 2, "fb1": 1, "fb2": 1}
+WAKE, TURNS, SEED = 80, 600, 2
+PLAN = {}
 
 
 def relays(rank_core, T, topo):
     ok = [c for c in topo.cores_of(rank_core) if c != rank_core and all(topo.may_write(c, d) for d in T.cores)]
     near = [c for c in ok if topo.die(c) == topo.die(rank_core)]
     far = [c for c in ok if topo.die(c) != topo.die(rank_core)]
-    return near[0], far[0], near[1]
+    return near[:2] + far[:2]
 
 
 def bits(engines):
@@ -71,332 +63,418 @@ def deal(core, dests, each, topo):
     return masks
 
 
-def relay_votes(g, core, s, which, T, topo):
+def hand_on(g, core, s, h, T, topo):
     n = len(T.cores)
-    dests = [T.cores[d] for d in range(n) if ((d - s) % n) % 2 == which]
-    masks = deal(core, dests, 2, topo)
-    for e in range(9):
-        g.wait_ge(T.sem["a%d" % e], 8)
-        g.remote_dma_fused([RemoteDMATransfer(dst_ids=[dst_id(d, core, topo)], dma_engine_mask=masks[d], remote_sem=T.sem["a%d" % e],
-                                              src=T.rd[e], dst=T.dv[8 * e + s]) for d in dests], local_sem=T.sem.left)
-    g.wait_ge(T.sem.left, 9 * 2 * len(dests))
+    engines = len(topo.engines(T.cores[s], core))
+    left = 0
+    mine = [(m, slot, share) for m in PLAN["sends"] for hh, slot, share in MSG[m][2] if hh == h]
+    for j, (m, slot, share) in enumerate(mine):
+        dealt, b, parts = MSG[m]
+        sem = T.sem["a" + m]
+        dests = [d for d in range(n) if share is None or (d - s) % 2 == share]
+        each = n // len(dests)
+        masks = deal(core, [T.cores[d] for d in dests], each, topo)
+        if dealt:
+            g.sync.wait_ge(sem, engines // len(parts))
+            g.sync.dma_start(T["k" + b][n * slot:n * slot + n], T["h" + b][slot]).then_inc(T.sem["m%d" % j], 16)
+            g.wait_ge(T.sem["m%d" % j], 16)
+        else:
+            g.wait_ge(sem, engines // len(parts))
+        g.remote_dma_fused([RemoteDMATransfer(dst_ids=[dst_id(T.cores[d], core, topo)], dma_engine_mask=masks[T.cores[d]], remote_sem=sem,
+                                              src=T["k" + b][n * slot + d] if dealt else T["h" + b][slot], dst=T["k" + b][n * slot + s])
+                            for d in dests], local_sem=T.sem.left)
+        left += each * len(dests)
+    g.wait_ge(T.sem.left, left)
 
 
-def back_sides(e, s, T):
-    if e < 5:
-        return [(T.ru1[e], T.ru2[8 * e + s])]
-    if e < 8:
-        return [(T.rh1[2 * (e - 6) + h], T.rh2[8 * (2 * (e - 6) + h) + s]) for h in range(2)]
-    return [(T.rf1[0], T.rf2[s])]
+def plan(defs):
+    before = {n: [(d.lstrip("~"), 0 if d[0] == "~" else defs[d]["lat"] + WAKE) for d in v["deps"]] for n, v in defs.items()}
+    after = {n: [] for n in defs}
+    for n in defs:
+        for d, gap in before[n]:
+            after[d].append((n, gap))
 
-
-def relay_results(g, core, s, T, topo):
-    masks = deal(core, list(T.cores), 1, topo)
-    n = 0
-    for e in BACK:
-        g.wait_ge(T.sem["b%d" % e], 16)
-        for a, b in back_sides(e, s, T):
-            g.remote_dma_fused([RemoteDMATransfer(dst_ids=[dst_id(d, core, topo)], dma_engine_mask=masks[d],
-                                                  remote_sem=T.sem["b%d" % e], src=a, dst=b) for d in T.cores],
-                               local_sem=T.sem.left)
-            n += len(T.cores)
-    g.wait_ge(T.sem.left, n)
+    def place(rank, needs, frees, lead):
+        end, busy = {}, {q: [] for q in "VSPGYX"}
+        missing = {n: len(needs[n]) for n in defs}
+        ready = [n for n in defs if not missing[n]]
+        while ready:
+            n = min(ready, key=rank.get)
+            ready.remove(n)
+            t, cost, taken = max([end[d] + gap for d, gap in needs[n]] + [lead[n]]), defs[n]["cost"], busy[defs[n]["q"]]
+            at = len(taken)
+            for j, (a, b) in enumerate(taken):
+                if t + cost <= a:
+                    at = j
+                    break
+                t = max(t, b)
+            end[n] = t + cost
+            taken.insert(at, (t, t + cost))
+            for u, gap in frees[n]:
+                missing[u] -= 1
+                if not missing[u]:
+                    ready.append(u)
+        return end
+    none, last = {n: 0 for n in defs}, {n: v["lat"] for n, v in defs.items()}
+    best, seed = (1e9, None, {n: -j for j, n in enumerate(defs)}), SEED
+    for turn in range(TURNS):
+        rank = dict(best[2])
+        for n in defs:
+            seed = (seed * 1103515245 + 12345) % 2 ** 31
+            if seed % 3000 < 1000:
+                rank[n] += seed // 3000 % 2000 - 1000
+        for twice in range(2):
+            back = place(rank, after, before, last)
+            ahead = place({n: -back[n] for n in defs}, before, after, none)
+            rank = {n: -ahead[n] - last[n] for n in defs}
+        length = max(ahead[n] + last[n] for n in defs)
+        if length <= best[0]:
+            best = (length, ahead, rank)
+    PLAN["began"] = best[1]
+    PLAN["defs"] = defs
+    return {q: sorted((n for n in defs if defs[n]["q"] == q), key=lambda n: best[1][n]) for q in "VSPGYX"}
 
 
 def rank_program(g, core, T, topo):
     r = T.rank_of(core)
-    if r is None:
-        for s, c in enumerate(T.cores):
-            if core in topo.cores_of(c):
-                ra, rb, rc = relays(c, T, topo)
-                if core == ra:
-                    relay_votes(g, core, s, 0, T, topo)
-                elif core == rb:
-                    relay_votes(g, core, s, 1, T, topo)
-                elif core == rc:
-                    relay_results(g, core, s, T, topo)
+    if r is not None:
+        rank_calls(g, core, r, T, topo, True)
         return
-    ra, rb, rc = relays(core, T, topo)
+    for s, c in enumerate(T.cores):
+        if core in topo.cores_of(c) and core in relays(c, T, topo):
+            if "sends" not in PLAN:
+                rank_calls(g, c, s, T, topo, False)
+            hand_on(g, core, s, relays(c, T, topo).index(core), T, topo)
+
+
+def rank_calls(g, core, r, T, topo, issue):
     V, S, PE, SY = g.vector, g.scalar, g.tensor, g.sync
+    hands = relays(core, T, topo)
+    eng = topo.engines(core, hands[0])
     defs = {}
     vb = [T.vb0, T.vb1, T.vb2]
     wb = [T.vb0, T.wb1, T.wb2]
+    fl = [T.t0, T.vb0, T.t0]
 
-    def op(name, fn, deps=()):
-        defs[name] = ("op", fn, list(deps))
+    def put(name, q, kind, what, deps, cost, lat=0):
+        defs[name] = {"q": q, "kind": kind, "what": what, "deps": list(deps), "cost": cost, "lat": lat}
 
-    def dma(name, pairs, deps=()):
-        defs[name] = ("dma", pairs, list(deps))
+    def op(name, q, fn, deps=(), cycles=64):
+        put(name, q, "op", fn, deps, (170 if q == "G" else 40) + 0.9 * max(64, cycles))
 
-    def mm(out, parts):
+    def gather(name, q, fn, deps, n):
+        put(name, q, "op", fn, deps, 60 + 1.35 * n)
+
+    def dma(name, pairs, deps=(), q="Y", kb=0):
+        put(name, q, "dma", pairs, deps, 60 * len(pairs) + (3 * kb if q == "Y" else 0), 1100 + (0 if q == "Y" else 3 * kb))
+
+    def mm(name, parts, deps, cycles=64):
         def fn():
             ins = None
-            for j, (lhs, rhs, st, sp) in enumerate(parts):
-                ins = PE.matmul(out[j], lhs, rhs, st, sp)
+            for out, lhs, rhs, st, sp in parts:
+                ins = PE.matmul(out, lhs, rhs, st, sp)
             return ins
-        return fn
+        put(name, "P", "op", fn, deps, 0.5 * cycles * len(parts))
+        defs[name]["parts"] = len(parts)
 
-    def pick(out, rhs_of, lhs_of):
-        return mm([out] * 16, [(lhs_of(i), rhs_of(i), i == 0, i == 15) for i in range(16)])
+    def pick(name, out, rhs_of, lhs_of, deps):
+        mm(name, [(out, lhs_of(i), rhs_of(i), i == 0, i == 15) for i in range(16)], deps)
+
+    def slide(z):
+        return lambda i: z[:, 15 - i:143 - i]
 
     def zrow(j):
         return lambda i: T.zj[:, j, 15 - i:143 - i]
+
+    def power(j, p0, n):
+        return T.pc[:, 8 * p0 + AT[j]:8 * (p0 + n):8]
 
     def copy(q, out, src):
         if q == "S":
             return lambda: S.activation(out, src, ACT.Copy)
         return lambda: V.tensor_copy(out, src)
 
-    def after(name, c):
-        return ["~%s_%d" % (name, c - 1)] if c else []
+    def look(name, out, c0, win, lst, l0, n, deps):
+        parts = {0: [("S", 0, n)], 1: [("V", 0, n)], 2: [("S", 0, n // 2), ("V", n // 2, n)]}[SHARE.get(name, 0)]
+        for q, a, b in parts:
+            gather(name + q, q, copy(q, out[:, c0 + a:c0 + b], win.indirect(lst[:, l0 + a // 16:l0 + b // 16])), deps, b - a)
+        return [name + q for q, a, b in parts]
+
+    def send(m, srcs, deps, kb):
+        dealt, b, parts = MSG[m]
+        each = len(eng) // len(parts)
+        put("s" + m, "G", "rem", [RemoteDMATransfer(dst_ids=[dst_id(hands[h], core, topo)], dma_engine_mask=bits(eng[each * j:each * j + each]),
+                                                    remote_sem=T.sem["a" + m], src=srcs[j], dst=T["h" + b][slot])
+                                  for j, (h, slot, share) in enumerate(parts)], deps, 3800 if m == "L" else 420)
+        put("a" + m, "X", "ext", (T.sem["a" + m], 8 * len(parts)), ["s" + m], 0, (3500 if dealt else 2300) + 8 * kb)
 
     mine = slice(16 * r, 16 * r + 16)
-    dma("ld_b0", [(T.fi[:, 320:384], T.fb[:, 0:64])])
-    dma("ld_x", [(T.vb0[:, 0:1024], T.x[:])])
-    dma("ld_a", [(T.fi[:, 0:192], T.fa[:])])
-    dma("ld_b", [(T.fi[:, 192:320], T.fb[:, 64:192])])
-    dma("ld_ct", [(T.ci[:, 0:192], T.cd[:]), (T.ci[:, 192:256], T.tp[:])])
-    dma("ld_c16", [(T.cdi[0:16, 64:256], T.cd[mine, :])])
-    dma("ld_si", [(T.si[:, 8 * l:8 * l + 8], T.cd[mine, 64 * l:64 * l + 64]) for l in range(3)] + [(T.si[:, 40:48], T.tp[mine, :])])
+    acol, bcol = [64, 128, 192], [0, 256, 320]
+    dma("ld_0", [(T.fi[:, 0:64], T.fb[:, 0:64]), (T.fi[:, 64:128], T.fa[:, 0:64])], q="S", kb=250)
+    dma("ld_x", [(T.vb0[:, 0:1024], T.x[:])], kb=256)
+    dma("ld_ab", [(T.fi[:, 128:256], T.fa[:, 64:192]), (T.fi[:, 256:384], T.fb[:, 64:192])], ["~ld_x"], kb=150)
+    dma("ld_ct", [(T.ci[:, 0:192], T.cd[:]), (T.ci[:, 192:256], T.tp[:])], ["~ld_ab"], kb=150)
+    dma("ld_c16", [(T.cdi[0:16, 64:256], T.cd[mine, :])], ["~ld_ab"], kb=20)
+    dma("ld_si", [(T.si[:, 8 * l:8 * l + 8], T.cd[mine, 64 * l:64 * l + 64]) for l in range(3)] + [(T.si[:, 40:48], T.tp[mine, :])], ["~ld_ab"],
+        kb=100)
     dma("ld_id", [(T.si[:, 24 + 8 * l:32 + 8 * l], T.idw[0:16, 64 * l:64 * l + 64]) for l in range(2)], ["io_id"])
-    for nm, ap, val in [("ones", T.ones[:], 1.0), ("neg", T.neg[:], -1.0), ("oneb", T.oneb[:], 1.0), ("zv", T.zv[:], 0.0),
-                        ("zj", T.zj[:], 0.0), ("zs", T.zs[:], 0.0), ("vl", T.vl[:, :, 5], 0.0), ("tab0", T.tab[:, 0:2048], 0.0),
-                        ("tab1", T.tab[:, 2048:4096], 0.0),
-                        ("pf", T.pf[:, :, 0:5], 1.0)]:
-        op("m_" + nm, lambda ap=ap, val=val: V.memset(ap, val))
-    op("io_cd", lambda: g.iota(T.cdi[0:16, 0:64], [[16, 64]], 0, 1))
-    op("io_id", lambda: g.iota(T.idw[0:16, :], [[16, 128]], 1024, 1))
-    zvv, zjv, zsv = T.zv[:, 15:143:16], T.zj[:, :, 15:143:16], T.zs[:, 120:128]
-    for nm, out, src, pat, cmp, base, cm, deps in [
-            ("i16", T.i16[0:16, :], T.ones[0:16, 0:16], [[-1, 16]], ALU.is_equal, 0, 1, ["m_ones"]),
-            ("psl", T.psl[:], T.ones[:], [[-1, 8], [-8, 16]], ALU.is_equal, 0, 1, ["m_ones"]),
-            ("pls", T.pls[:], T.ones[:], [[-1, 16], [-16, 8]], ALU.is_equal, 0, 1, ["m_ones"]),
-            ("nls", T.nls[:], T.neg[:], [[-1, 16], [-16, 8]], ALU.is_equal, 0, 1, ["m_neg"]),
-            ("zv0", zvv, T.oneb[:, 0, :], [[-16, 8]], ALU.is_ge, 0, 1, ["m_oneb", "m_zv"]),
-            ("zj0", zjv, T.oneb[:], [[-2, 4], [-16, 8]], ALU.is_ge, 0, 1, ["m_oneb", "m_zj"]),
-            ("zs0", zsv, T.oneb[:, 0, :], [[-16, 8]], ALU.is_ge, -8, 1, ["m_oneb", "m_zs"]),
-            ("zv", zvv, zvv, [[16, 8]], ALU.is_ge, 15, -1, ["g_zv0"]),
-            ("zj", zjv, zjv, [[2, 4], [16, 8]], ALU.is_ge, 1, -1, ["g_zj0"]),
-            ("zs", zsv, zsv, [[16, 8]], ALU.is_ge, 15, -1, ["g_zs0"])]:
-        op("g_" + nm, lambda a=(out, src, pat, cmp, 0.0, base, cm): g.affine_select(*a), deps)
-    for j in range(4):
-        op("g_fl%d" % j, lambda j=j: g.iota(T.fl[:, 1024 * j:1024 * j + 1024], [[0, 1024]], 0, 0, allow_small_or_imprecise_dtypes=True))
-    op("c_b0", copy("V", T.lab[:, 320:384], T.fi[:, 320:384]), ["ld_b0"])
-    op("c_a0", copy("V", T.lab[:, 0:64], T.fi[:, 0:64]), ["ld_a"])
-    op("c_ab", copy("V", T.lab[:, 64:320], T.fi[:, 64:320]), ["ld_a", "ld_b"])
-    op("c_ct", copy("V", T.lct[:], T.ci[:]), ["ld_ct"])
-    op("c_oa", copy("V", T.oo[:, 0:64], T.fi[:, 0:64]), ["ld_a", "~vt8_1"])
-    op("c_ob", copy("V", T.oo[:, 64:128], T.fi[:, 320:384]), ["ld_b0", "~vt8_1"])
-    dma("o_l0", [(T.ya[:, 0:64], T.oo[:, 0:64]), (T.yb[:, 0:64], T.oo[:, 64:128])], ["c_oa", "c_ob"])
-    X = T.fi[:, 64:320]
-    rm = [T.rm[:, 256 * i:256 * i + 256] for i in range(8)]
-    ab = ["ld_a", "ld_b", "~vt8_1"]
-    op("rm0", lambda: V.tensor_scalar(rm[0], X, 15, None, ALU.bitwise_and), ab)
-    op("rm1", lambda: V.tensor_scalar(rm[1], X, 4, 63, ALU.logical_shift_right, ALU.bitwise_and), ab)
-    op("rm2", lambda: V.tensor_scalar(rm[2], X, 1024.0, 63.0, ALU.is_ge, ALU.mult), ab)
-    op("rm3", lambda: V.tensor_scalar(rm[3], X, 1024.0, -15.0, ALU.is_ge, ALU.mult), ab)
-    op("rm4", lambda: V.tensor_tensor(rm[4], rm[0], rm[2], ALU.mult), ["rm0", "rm2"])
-    op("rm5", lambda: V.tensor_tensor(rm[5], rm[1], rm[3], ALU.mult), ["rm1", "rm3"])
-    op("rm6", lambda: V.tensor_tensor(rm[6], rm[4], X, ALU.add), ["rm4"])
-    op("rm7", lambda: V.tensor_tensor(rm[7], rm[6], rm[5], ALU.add), ["rm5", "rm6"])
-    op("rm8", copy("V", T.lfin[:], rm[7]), ["rm7"])
-    op("c_cdf", copy("V", T.cdf[0:16, :], T.cdi[0:16, :]), ["ld_c16", "io_cd"])
-    op("p_t", mm([T.po0[:, 0:16], T.po0[:, 16:32]], [(T.cdf[0:16, 128 * h:128 * h + 128], T.i16[0:16, :], True, True) for h in range(2)]),
-       ["c_cdf", "g_i16"])
-    op("t_hi", copy("S", T.thl[:, 0:32], T.po0[:, 0:32]), ["p_t"])
-    op("t_lo", lambda: V.tensor_tensor(T.thl[:, 32:64], T.po0[:, 0:32], T.thl[:, 0:32], ALU.subtract), ["t_hi"])
+    dma("ld_c2", [(T.ci2[16 * a:16 * a + 16, :], T.cd[mine, :]) for a in range(8)], ["~ld_ct"], kb=96)
+    for nm, ap, val, n in [("ones", T.ones[:], 1.0, 128), ("oneb", T.oneb[:], 1.0, 64), ("one4", T.one4[:], 1.0, 16), ("zj", T.zj[:], 0.0, 288),
+                           ("tab0", T.tab[:, 0:1024], 0.0, 512), ("tab1", T.tab[:, 1024:2048], 0.0, 512), ("tab2", T.tab[:, 2048:3072], 0.0, 512),
+                           ("pc", T.pc[:, 0:384:2], BIG, 192), ("pf0", T.pf[:, 0:64:2], 0.0, 32),
+                           ("pf", T.pf[:, 0:64:8], BIG, 8)]:
+        op("m_" + nm, "V", lambda ap=ap, val=val: V.memset(ap, val), ["m_pf0"] if nm == "pf" else [], n)
+    for nm, ap, val, n in [("zv", T.zv[:], 0, 144), ("zu", T.zu[:], 0, 144), ("zo0", T.zo[:], 0, 144), ("z1", T.z1[:], 0, 144),
+                           ("zs", T.zs[:], 0, 256), ("t0", T.t0[:, 0:1024], 0, 1024), ("big", T.big[:], int(BIG), 8),
+                           ("zo", T.zo[:, 15:143:16], 1, 8)]:
+        op("m_" + nm, "G", lambda ap=ap, val=val, n=n: g.iota(ap, [[0, n]], val, 0, allow_small_or_imprecise_dtypes=True),
+           ["m_zo0"] if nm == "zo" else [], 2 * n)
+    op("m_tab3", "S", copy("S", T.tab[:, 3072:4096], T.tab[:, 0:1024]), ["m_tab0"], 1024)
+    op("io_cd", "G", lambda: g.iota(T.cdi[0:16, 0:64], [[16, 64]], 0, 1), [], 128)
+    op("io_id", "G", lambda: g.iota(T.idw[0:16, :], [[16, 128]], 1024, 1), [], 256)
+    op("io_of", "G", lambda: g.iota(T.oi[:, 0:4], [[0, 4]], 0, 1))
+    zvv, zuv, zjv, one8 = T.zv[:, 15:143:16], T.zu[:, 15:143:16], T.zj[:, :, 15:143:16], T.oneb[:, 0:8]
+    for nm, out, src, pat, cmp, base, deps, n in [
+            ("i16", T.i16[0:16, :], T.ones[0:16, 0:16], [[-1, 16]], ALU.is_equal, 0, ["m_ones"], 16),
+            ("f16", T.f16[0:16, :], T.ones[0:16, :], [[0, 8], [-1, 16]], ALU.is_equal, 0, ["m_ones"], 128),
+            ("psl", T.psl[:], T.ones[:], [[-1, 8], [-8, 16]], ALU.is_equal, 0, ["m_ones"], 128),
+            ("pls", T.pls[:], T.ones[:], [[-1, 16], [-16, 8]], ALU.is_equal, 0, ["m_ones"], 128),
+            ("eye", T.eye[:], T.ones[:], [[-1, 128]], ALU.is_equal, 0, ["m_ones"], 128),
+            ("z1", T.z1[:, 15:143:16], T.big[:], [[-16, 8]], ALU.is_equal, 0, ["m_big", "m_z1"], 8),
+            ("zs", T.zs[:, 120:128], T.big[:], [[-16, 8]], ALU.is_equal, 0, ["m_big", "m_zs"], 8),
+            ("zv0", zvv, one8, [[-16, 8]], ALU.is_ge, 0, ["m_oneb", "m_zv"], 8),
+            ("zu0", zuv, T.big[:], [[-16, 8]], ALU.is_ge, -8, ["m_big", "m_zu"], 8),
+            ("zj0", zjv, T.one4[:], [[-2, 4], [-16, 8]], ALU.is_ge, 0, ["m_one4", "m_zj"], 32),
+            ("own0", T.own[:], T.ones[:, 0:64], [[-16, 8], [0, 8]], ALU.is_ge, 0, ["m_ones"], 64)]:
+        op("g_" + nm, "G", lambda a=(out, src, pat, cmp, 0.0, base, 1): g.affine_select(*a), deps, 2 * n)
+    for nm, out, pat, base, n in [("zv", zvv, [[16, 8]], 15, 8), ("zu", zuv, [[16, 8]], 15, 8), ("zj", zjv, [[2, 4], [16, 8]], 1, 32),
+                                  ("own", T.own[:], [[16, 8], [0, 8]], 15, 64)]:
+        op("g_" + nm, "G", lambda a=(out, out, pat, ALU.is_ge, 0.0, base, -1): g.affine_select(*a), ["g_%s0" % nm], 2 * n)
+    mm("p_ee", [(T.pl[:, 0:128], T.f16[0:16, :], T.f16[0:16, :], True, True)], ["g_f16"], 512)
+    op("e_ee", "S", copy("S", T.ee[:], T.pl[:, 0:128]), ["p_ee"], 128)
+    op("c_of0", "V", lambda: V.tensor_scalar(T.oi[:, 4:8], T.oi[:, 0:4], 7, None, ALU.bitwise_and), ["io_of"])
+    op("c_of", "V", lambda: V.tensor_scalar(T.of[:], T.oi[:, 4:8], 8.0, 7.0, ALU.mult, ALU.add), ["c_of0"])
+    op("c_0", "V", copy("V", T.lab[:, 0:128], T.fi[:, 0:128]), ["ld_0"], 128)
+    op("c_ab", "V", copy("V", T.lab[:, 128:384], T.fi[:, 128:384]), ["ld_ab"], 256)
+    op("c_ct", "V", copy("V", T.lct[:], T.ci[:]), ["ld_ct"], 256)
+    op("c_c2", "V", copy("V", T.lc2[:], T.ci2[:]), ["ld_c2"], 192)
+    op("c_o0", "V", copy("V", T.oo[:, 0:128], T.fi[:, 0:128]), ["ld_0"], 128)
+    dma("o_l0", [(T.yb[:, 0:64], T.oo[:, 0:64]), (T.ya[:, 0:64], T.oo[:, 64:128])], ["c_o0"])
+    send("L", [T.lab[:, 96 * h:96 * h + 96] for h in range(4)], ["c_0", "c_ab"], 480)
+    dma("in_L", [(T.lab2[:, 96 * h:96 * h + 96], T.kl[8 * h:8 * h + 8]) for h in range(4)], ["aL"], kb=96)
+    op("c_cdf", "V", copy("V", T.cdf[0:16, :], T.cdi[0:16, :]), ["ld_c16", "io_cd"], 256)
+    mm("p_t", [(T.po0[:, 16 * h:16 * h + 16], T.cdf[0:16, 128 * h:128 * h + 128], T.i16[0:16, :], True, True) for h in range(2)],
+       ["c_cdf", "g_i16"], 256)
+    op("t_hi", "S", copy("S", T.thl[:, 0:32], T.po0[:, 0:32]), ["p_t"])
+    op("t_lo", "V", lambda: V.tensor_tensor(T.thl[:, 32:64], T.po0[:, 0:32], T.thl[:, 0:32], ALU.subtract), ["t_hi"])
     dma("dt_c", [(T.dt[h, 2048 * a:2048 * a + 2048], T.thl[:, 32 * h + 16 * a:32 * h + 16 * a + 16]) for h in range(2) for a in range(2)],
         ["t_hi", "t_lo"])
-    dma("tab_c", [(T.tab[16 * a:16 * a + 2, :], T.dt[0:2, :]) for a in range(8)], ["dt_c", "m_tab0", "m_tab1"])
+    dma("tab_c", [(T.tab[16 * a:16 * a + 2, :], T.dt[0:2, :]) for a in range(8)], ["dt_c", "m_tab1", "m_tab2", "m_tab3"], kb=128)
     dma("dt_in", [(T.dt[2 * j:2 * j + 2, 0:1024], T.dt[0:2, 0:1024]) for j in range(1, 4)], ["dt_c"])
-    op("c_sf", copy("V", T.sf[:], T.si[:]), ["ld_si", "ld_id"])
-    op("p_s", mm([T.pp[:, 0:48]], [(T.psl[:], T.sf[:], True, True)]), ["c_sf", "g_psl"])
-    op("l_s1", copy("V", T.lu[:, 0:24], T.pp[:, 0:24]), ["p_s"])
-    op("e_s1", copy("S", T.vl[:, 0:24, 3], T.pp[:, 0:24]), ["l_s1"])
-    op("e_s2", copy("S", T.vl[:, 0:16, 4], T.pp[:, 24:40]), ["l_s1"])
+    op("c_sf", "V", copy("V", T.sf[:], T.si[:]), ["ld_si", "ld_id"])
+    mm("p_s", [(T.pp[:, 0:48], T.psl[:], T.sf[:], True, True), (power(1, 0, 16), T.psl[:], T.sf[:, 0:16], True, True),
+               (power(0, 0, 16), T.psl[:], T.sf[:, 24:40], True, True), (power(0, 24, 8), T.psl[:], T.sf[:, 40:48], True, True)],
+       ["c_sf", "g_psl", "m_pc"], 256)
+    op("l_s1", "V", copy("V", T.lu[:, 0:48], T.pp[:, 0:48]), ["p_s"])
     for j in range(1, 4):
         c0 = 384 * (j - 1)
-        op("g_s%d" % j, copy("S", T.gch[:, c0:c0 + 384], T.tab[:, :].indirect(T.lu[:, 24 * (j - 1):24 * j])), ["l_s%d" % j, "tab_c"])
-        op("x_s%d" % j, pick(T.pc[:, 0:24], lambda i, c0=c0: T.gch[:, c0 + i:c0 + 384:16], zrow(0)),
-           ["g_s%d" % j, "g_zj"] + (["e_x%d" % (j - 1)] if j > 1 else []))
+        names = look("g_s%d" % j, T.gch, c0, T.tab[:, :], T.lu, [0, 64, 88][j - 1], 384, ["l_s%d" % j, "tab_c"])
+        pick("x_s%d" % j, power(j + 1, 0, 24), lambda i, c0=c0: T.gch[:, c0 + i:c0 + 384:16], zrow(0), names + ["g_zj"])
         if j < 3:
-            op("l_s%d" % (j + 1), copy("V", T.lu[:, 24 * j:24 * j + 24], T.pc[:, 0:24]), ["x_s%d" % j])
-        op("e_x%d" % j, copy("S", T.vl[:, 0:24, 3 - j], T.pc[:, 0:24]), ["l_s%d" % (j + 1) if j < 3 else "x_s3"])
+            op("l_s%d" % (j + 1), "V", copy("V", T.lu[:, 40 + 24 * j:64 + 24 * j], power(j + 1, 0, 24)), ["x_s%d" % j])
         dma("dt_%d" % j, [(T.dt[2 * j + h, 1024 * (l + 1):1024 * (l + 2)], T.gch[h:128:16, c0 + 128 * l:c0 + 128 * l + 128])
-                          for h in range(2) for l in range(3)], ["g_s%d" % j])
-    dma("tab_j", [(T.tab[16 * a + 2:16 * a + 8, :], T.dt[2:8, :]) for a in range(8)], ["dt_1", "dt_2", "dt_3", "dt_in"])
+                          for h in range(2) for l in range(3)], names)
+    dma("tab_j", [(T.tab[16 * a + 2:16 * a + 8, :], T.dt[2:8, :]) for a in range(8)], ["dt_1", "dt_2", "dt_3", "dt_in"], kb=384)
 
-    def finish(tag, a, b, deps, pp_free):
-        n = b - a
-        op("lf" + tag, copy("V", T.lf[:, 4 * a:4 * b], T.vl[:, a:b, 1:5]), deps)
-        op("pd" + tag, mm([T.pp[:, 0:5 * n]] * 2, [(T.pls[:], T.vl[:, a:b, 0:5], True, False), (T.nls[:], T.vl[:, a:b, 1:6], False, True)]),
-           deps + ["g_pls", "g_nls", "m_vl"] + pp_free)
-        op("ed" + tag, copy("S", T.d1[:, 5 * a:5 * b], T.pp[:, 0:5 * n]), ["pd" + tag])
+    def finish(tag, a, n, p0, deps):
+        op("lf" + tag, "V", copy("V", T.lf[:, 4 * a:4 * (a + n)], T.pc[:, 8 * p0 + 1:8 * (p0 + n):2]), deps, 4 * n)
+        op("eu" + tag, "S", copy("S", T.vl[:, 8 * a:8 * (a + n)], T.pc[:, 8 * p0:8 * (p0 + n)]), ["lf" + tag], 8 * n)
 
-    finish("A", 0, 16, ["e_s1", "e_s2", "e_x1", "e_x2", "e_x3"], [])
-
-    def chain(t, a, n, c0, u_rhs, deps, before):
-        op("pu" + t, mm([T.pc[:, 4:5 * n:5]], [(T.psl[:], u_rhs, True, True)]), deps + ["e_x3" if before == "A" else "eu" + before])
-        lst = T.lu[:, c0:c0 + n]
-        op("lu" + t, copy("V", lst, T.pc[:, 4:5 * n:5]), ["pu" + t])
-        op("gu" + t, copy("S", T.gch[:, 16 * c0:16 * (c0 + n)], T.tab[:, :].indirect(lst)), ["lu" + t, "tab_j"])
+    def chain(t, a, n, p0, l0, c0, deps, before):
+        names = look("gu" + t, T.gch, c0, T.tab[:, :], T.lu, l0, 16 * n, deps + ["tab_j"])
         for j in range(4):
-            op("xu%d" % j + t, pick(T.pc[:, 3 - j:5 * n:5], lambda i: T.gch[:, 16 * c0 + i:16 * (c0 + n):16], zrow(j)),
-               ["gu" + t] + (["~xu%d" % (j - 1) + t] if j else []))
-        op("eu" + t, copy("S", T.vl[:, a:a + n, 0:5], T.pc[:, 0:5 * n]), ["xu3" + t])
-        finish(t, a, a + n, ["eu" + t], ["ed" + before])
+            pick("xu%d" % j + t, power(j + 1, p0, n), lambda i: T.gch[:, c0 + i:c0 + 16 * n:16], zrow(j), names + [before])
+        finish(t, a, n, p0, ["xu%d" % j + t for j in range(4)] + ["pu" + t])
 
-    TAG = ["A", "A", "0", "1", "1", "1", "2", "2", "2"]
-    chain("0", 24, 8, 72, T.sf[:, 40:48], ["c_sf"], "A")
-    for k in (1, 2):
-        chain("%d" % k, 32 * k, 24, 72 + 24 * k, T.rs[:, 120 * (k - 1) + 4:120 * k:5], ["sc_%d" % e for e in range(3 * k - 3, 3 * k)],
-              TAG[3 * k - 1])
+    finish("0", 0, 16, 0, ["x_s3"])
+    for t, e0, e1, l0 in [(1, 2, 5, 40), (2, 5, 8, 112), (3, 8, 9, 136)]:
+        a, p0 = max(e0, 3), 24 * (t % 2)
+        u = T.rs[:, 64 * (a - 3) + 7:64 * (e1 - 3):8]
+        last = ["sc_%d" % (e - 3) for e in range(a, e1)]
+        op("lu%d" % t, "V", copy("V", T.lu[:, l0 + 8 * (a - e0):l0 + 8 * (e1 - e0)], u), last)
+        mm("pu%d" % t, [(power(0, p0 + 8 * (a - e0), 8 * (e1 - a)), T.eye[:], u, True, True)], last + ["g_eye", "eu%d" % (t - 1)], 256)
+        chain("%d" % t, 8 * e0, 8 * (e1 - e0), p0, l0, 896 + 128 * e0, ["lu%d" % t, "l_s1"], "eu%d" % (t - 1))
+    TAG = "001112223"
+    mm("p_d8", [(T.pp[:, 0:64], T.pls[:], T.vl[:, 512:576], True, True)], ["eu3", "g_pls", "l_s1"], 256)
+    op("e_d8", "S", copy("S", T.vl[:, 576:640], T.pp[:, 0:64]), ["p_d8"])
 
-    acol, bcol = [0, 64, 128], [320, 192, 256]
-    dsta = [dst_id(c, core, topo) for c in (ra, rb, rc)]
-    eng = topo.engines(core, ra)
-    half = [bits(eng[:len(eng) // 2]), bits(eng[len(eng) // 2:])]
-    nleft = 0
-    done = []
+    done, wdone, taps, tables = [], [], [], []
+    bank = [[], []]
+    seen = [[], [], []]
+    spread = ["e_ee"]
     for e in range(9):
         k, l = divmod(e, 3)
-        win = (vb[k] if l == 0 else wb[k])[:, 0:1024 * (l + 1)]
-        chunks = len(COPY[e])
-        n = 1024 // chunks
-        if e == 0:
-            need = ["ld_x"]
+        lo = 1024 * (l + 1)
+        win = (vb[k] if l == 0 else wb[k])[:, 0:lo]
+        lab, lc = (T.lab, T.lct) if k == 0 else (T.lab2, T.lc2)
+        cuts = CUTS[e]
+        if k == 0:
+            need = ["ld_x", "c_0"] if l == 0 else done + ["c_ab"]
         elif l == 0:
-            need = ["tap%d" % k]
-        elif k == 0:
-            need = done
+            need = taps + ["in_L"]
         else:
-            need = ["wS%d" % (e - 1), "cp%d" % k] + (["wV%d" % (e - 1)] if e in BOTH else [])
-        for c in range(chunks):
-            t = T.tb[:, 1024 * e + n * c:1024 * e + n * (c + 1)]
-            lb = T.lab[:, bcol[l] + n // 16 * c:bcol[l] + n // 16 * (c + 1)]
-            la = T.lab[:, acol[l] + n // 16 * c:acol[l] + n // 16 * (c + 1)]
-            out = vb[k][:, 1024 * (l + 1) + n * c:1024 * (l + 1) + n * (c + 1)]
-            op("B%d_%d" % (e, c), lambda t=t, lb=lb, win=win: S.activation(t, win.indirect(lb), ACT.Identity, bias=255.0, scale=-1.0),
-               need + ["c_b0" if l == 0 else "c_ab"] + after("B%d" % e, c))
-            op("A%d_%d" % (e, c), lambda t=t, la=la, win=win, out=out: V.tensor_tensor(out, win.indirect(la), t, ALU.min),
-               need + ["B%d_%d" % (e, c), "c_a0" if l == 0 else "c_ab"] + after("A%d" % e, c))
-            cp = T.vc[:, 1024 * e + n * c:1024 * e + n * (c + 1)]
-            if COPY[e][c] == "G":
-                op("vc%d_%d" % (e, c), lambda cp=cp, out=out, n=n: g.affine_select(cp, out, [[0, n]], ALU.is_ge, 0.0, 0, 0),
-                   ["A%d_%d" % (e, c)])
+            need = wdone + ["cp%d" % k]
+        for c, (a, b) in enumerate(cuts):
+            n = b - a
+            t = T.t0[:, lo + a:lo + b] if k == 0 else T.tb[:, 1024 * (e - 3) + a:1024 * (e - 3) + b]
+            lb = lab[:, bcol[l] + a // 16:bcol[l] + b // 16]
+            la = lab[:, acol[l] + a // 16:acol[l] + b // 16]
+            out = vb[k][:, lo + a:lo + b]
+            gather("B%d_%d" % (e, c), "S", lambda t=t, lb=lb, win=win: S.activation(t, win.indirect(lb), ACT.Identity, bias=255.0, scale=-1.0),
+                   need, n)
+            gather("A%d_%d" % (e, c), "V", lambda t=t, la=la, win=win, out=out: V.tensor_tensor(out, win.indirect(la), t, ALU.min),
+                   need + ["B%d_%d" % (e, c)], n)
+            if k > 0:
+                cp, q, name = T.vc[:, 1024 * e + a:1024 * e + b], COPY[e][c], "vc%d_%d" % (e, c)
+                if q == "G":
+                    op(name, q, lambda cp=cp, out=out, n=n: g.affine_select(cp, out, [[0, n]], ALU.is_ge, 0.0, 0, 0), ["A%d_%d" % (e, c)], 2 * n)
+                elif q == "Y":
+                    dma(name, [(cp, out)], ["A%d_%d" % (e, c)], kb=n // 4)
+                else:
+                    op(name, q, copy(q, cp, out), ["A%d_%d" % (e, c)], n if q == "S" else n // 2)
+        done = ["A%d_%d" % (e, c) for c in range(len(cuts))]
+        if k == 0:
+            dma("vc%d" % e, [(T.vc[:, 1024 * e:1024 * e + 1024], vb[0][:, lo:lo + 1024])], done, kb=256)
+        counted, votes = [], []
+        for c, (a, b) in enumerate(cuts if k else HALVES):
+            dfc = T.df[:, 1024 * e + a:1024 * e + b]
+            gather("vt%d_%d" % (e, c), "V", lambda a=a, b=b, e=e, l=l, k=k, lo=lo, dfc=dfc, lc=lc: V.tensor_tensor(
+                dfc, vb[k][:, 0:lo + b].indirect(lc[:, 64 * l + a // 16:64 * l + b // 16]), T.vc[:, 1024 * e + a:1024 * e + b], ALU.not_equal),
+                ["vc%d" % e, "c_ct"] if k == 0 else done[:c + 1] + ["vc%d_%d" % (e, c), "c_c2"], b - a)
+            votes.append("vt%d_%d" % (e, c))
+            if e in WIDE:
+                pv = [T.pv0, T.pv1][c % 2][:, 0:b - a]
+                mm("pv%d_%d" % (e, c), [(pv, T.oneb[:], dfc, True, True)], ["vt%d_%d" % (e, c), "m_oneb"] + bank[c % 2], b - a)
+                op("ev%d_%d" % (e, c), "S", copy("S", fl[k][:, lo + a:lo + b], pv), ["pv%d_%d" % (e, c)] + tables, b - a)
+                bank[c % 2] = ["ev%d_%d" % (e, c)]
+                counted += bank[c % 2]
             else:
-                op("vc%d_%d" % (e, c), copy(COPY[e][c], cp, out), ["A%d_%d" % (e, c)])
-        done = ["A%d_%d" % (e, c) for c in range(chunks)]
-        full = vb[k][:, 0:1024 * (l + 2)]
-        pv = [T.pv0, T.pv1][e % 2][:, 0:64]
-        for c, (a, b) in enumerate(VCH):
-            op("vt%d_%d" % (e, c), lambda a=a, b=b, e=e, l=l, full=full: V.tensor_tensor(
-                T.df[:, 1024 * e + a:1024 * e + b], full.indirect(T.lct[:, 64 * l + a // 16:64 * l + b // 16]),
-                T.vc[:, 1024 * e + a:1024 * e + b], ALU.not_equal),
-               done + ["vc%d_%d" % (e, j) for j in range(a // n, (b + n - 1) // n)] + ["c_ct"] + after("vt%d" % e, c))
-            ii = range(a // 64, b // 64)
-            op("pv%d_%d" % (e, c), mm([pv] * len(ii), [(T.zv[:, 15 - i:143 - i], T.df[:, 1024 * e + 64 * i:1024 * e + 64 * i + 64],
-                                                        i == 0, i == 15) for i in ii]),
-               ["vt%d_%d" % (e, c), "g_zv"] + after("pv%d" % e, c) + (["ev%d" % (e - 2)] if e > 1 else []))
-        xv = T.xv[:, 64 * e:64 * e + 64]
-        op("ev%d" % e, copy("S" if e < 2 else "V", xv, pv), ["pv%d_%d" % (e, len(VCH) - 1)])
-        defs["sv%d" % e] = ("rem", [RemoteDMATransfer(dst_ids=[dsta[h]], dma_engine_mask=half[h], remote_sem=T.sem["a%d" % e],
-                                                      src=xv, dst=T.rd[e]) for h in range(2)], ["ev%d" % e])
-        nleft += len(eng)
+                pv = [T.pv0, T.pv1][e % 2][:, 0:64]
+                z = slide(T.zv if k == 0 else T.zo)
+                mm("pv%d_%d" % (e, c), [(pv, z(i), T.df[:, 1024 * e + 64 * i:1024 * e + 64 * i + 64], i == 0, i == 15)
+                                        for i in range(a // 64, b // 64)],
+                   ["vt%d_%d" % (e, c), "g_zv" if k == 0 else "m_zo"] + (["~pv%d_%d" % (e, c - 1)] if c else bank[e % 2]))
+        seen[k] = seen[k] + votes
+        if e not in WIDE:
+            xv = T.xv[:, 64 * e:64 * e + 64]
+            op("ev%d" % e, "S", copy("S", xv, pv), ["pv" + votes[-1][2:]])
+            bank[e % 2] = ["ev%d" % e]
+            counted = ["F%d" % e]
+            if k == 0:
+                send("V%d" % e, [xv, xv], ["ev%d" % e], 100)
+                dma("F%d" % e, [(fl[0][16 * a + 8:16 * a + 16, lo:lo + 1024], T.kv[8 * e:8 * e + 8, mine, :]) for a in range(8)],
+                    ["aV%d" % e] + done, kb=128)
+            else:
+                dma("F%d" % e, [(fl[k][0:128:16, lo:lo + 1024], xv)], ["ev%d" % e] + (seen[0] if k == 1 else tables))
         if k > 0 and l < 2:
-            lst0 = 64 * (e - 3)
-            for q, a, b in ([("S", 0, 512), ("V", 512, 1024)] if e + 1 in BOTH else [("S", 0, 1024)]):
-                op("w%s%d" % (q, e), copy(q, wb[k][:, 1024 * (l + 1) + a:1024 * (l + 1) + b],
-                                          full.indirect(T.lr[:, lst0 + a // 16:lst0 + b // 16])), done + ["lr%d" % (e - 3)])
-        if l == 2 and k < 2:
-            lst = T.lct[:, 192:256] if k == 0 else T.lr[:, 128:192]
-            op("tap%d" % (k + 1), copy("S", vb[k + 1][:, 0:1024], full.indirect(lst)), done + (["c_ct"] if k == 0 else ["lr2"]))
-            dma("cp%d" % (k + 1), [(wb[k + 1][:, 0:1024], vb[k + 1][:, 0:1024])], ["tap%d" % (k + 1)])
+            wdone = []
+            for c, (a, b) in enumerate(cuts):
+                wdone += look("w%d_%d" % (e, c), wb[k], lo + a, vb[k][:, 0:lo + b], T.lr, 64 * (e - 3) + a // 16, b - a,
+                              done[:c + 1] + ["el%d" % (e - 3)])
+        if e == 2:
+            for c in range(4):
+                q = "VS"[c % 2]
+                gather("tap1_%d" % c, q, copy(q, T.tx[:, 256 * c:256 * c + 256], vb[0][:, :].indirect(T.lct[:, 192 + 16 * c:208 + 16 * c])),
+                       done + ["c_ct"], 256)
+            for h in range(2):
+                send("X%d" % h, [T.tx[:, 256 * c:256 * c + 256] for c in (2 * h, 2 * h + 1)], ["tap1_%d" % c for c in (2 * h, 2 * h + 1)], 128)
+                defs["aX%d" % h]["deps"].append("~aL")
+                dma("in_X%d" % h, [(T.vb1[:, 256 * c:256 * c + 256], T.kq[8 * c:8 * c + 8]) for c in (2 * h, 2 * h + 1)], ["aX%d" % h], kb=128)
+            taps = ["in_X0", "in_X1"]
+            dma("cp1", [(T.wb1[:, 0:1024], T.vb1[:, 0:1024])], taps, kb=200)
+            seen[0] = seen[0] + ["tap1_%d" % c for c in range(4)]
+        if e == 5:
+            taps = look("tap2", T.vb2, 0, vb[1][:, :], T.lr, 128, 1024, done + ["el2"])
+            dma("cp2", [(T.wb2[:, 0:1024], T.vb2[:, 0:1024])], taps, kb=200)
+            dma("id_R", [(T.vb1[16 * a:16 * a + 2, 0:1024], T.dt[0:2, 0:1024]) for a in range(8)], seen[1] + taps + ["dt_c"])
         if k == 2:
-            if l == 0:
-                dma("o_vi", [(T.yv[:, 0:1024], T.vb2[:, 0:1024])], ["tap2"])
-            dma("o_v%d" % l, [(T.yv[:, 1024 * (l + 1):1024 * (l + 2)], T.vb2[:, 1024 * (l + 1):1024 * (l + 2)])], done)
-        defs["av%d" % e] = ("ext", T.sem["a%d" % e], 16)
-        war = ["g_fl%d" % (l + 1)] if k == 0 else ["w1_%d" % (3 * k - 1), "w1v%d" % BOTH[k - 1]]
-        dma("F%d" % e, [(T.fl[16 * a + 8:16 * a + 16, 1024 * (l + 1):1024 * (l + 2)], T.dv[8 * e:8 * e + 8, mine, :]) for a in range(8)],
-            war + ["av%d" % e])
-        a0 = 32 * k + (24 if e == 2 else 8 * l)
-        parts = [("S", "w1_", 0, 16), ("V", "w1v", 16, 32)] if e in BOTH else [("S", "w1_", 0, 32)]
-        for q, nm, a, b in parts:
-            op(nm + "%d" % e, copy(q, T.gf[:, 512 * e + 16 * a:512 * e + 16 * b],
-                                   T.fl[:, 0:1024 * (l + 2)].indirect(T.lf[:, 4 * a0 + a:4 * a0 + b])),
-               ["F%d" % e, "lf" + TAG[e]] + (["g_fl0"] if e == 0 else ["F%d" % (e - 1), "~w1_%d" % (e - 1)]))
-        op("w2_%d" % e, pick(T.pf[:, :, 1:5], lambda i, e=e: T.gf[:, 512 * e + i:512 * e + 512:16], lambda i: T.zs[:, 120 - 8 * i:248 - 8 * i]),
-           [nm + "%d" % e for q, nm, a, b in parts] + ["g_zs", "m_pf"] + (["w3_%d" % (e - 1)] if e else []))
-        op("w3_%d" % e, lambda e=e: V.tensor_scalar(T.d0[:, 40 * e:40 * e + 40], T.pf[:, :, 0:5], 0.0, None, ALU.is_equal), ["w2_%d" % e])
-        op("sc_%d" % e, lambda e=e, a0=a0: V.tensor_tensor_scan(T.rs[:, 40 * e:40 * e + 40], T.d0[:, 40 * e:40 * e + 40],
-                                                               T.d1[:, 5 * a0:5 * a0 + 40], 0.0, ALU.mult, ALU.add),
-           ["w3_%d" % e, "ed" + TAG[e]])
-        res = T.rs[:, 40 * e + 4:40 * e + 40:5]
-        if e in BACK:
-            sem = T.sem["b%d" % e]
-            nleft += len(eng)
-            if e < 5 or e == 8:
-                tile = T.ru[:, 8 * e:8 * e + 8] if e < 5 else T.rf[:]
-                op("w5_%d" % e, copy("V", tile, res), ["sc_%d" % e])
-                tr = [(tile, back_sides(e, r, T)[0][0], bits(eng))]
-            else:
-                hi, lo = [T.rh[:, 16 * (e - 6) + 8 * h:16 * (e - 6) + 8 * h + 8] for h in range(2)]
-                op("w4_%d" % e, copy("V", hi, res), ["sc_%d" % e])
-                op("w5_%d" % e, lambda hi=hi, lo=lo, res=res: V.tensor_tensor(lo, res, hi, ALU.subtract), ["w4_%d" % e])
-                tr = [((hi, lo)[h], back_sides(e, r, T)[h][0], half[h]) for h in range(2)]
-            defs["sr%d" % e] = ("rem", [RemoteDMATransfer(dst_ids=[dsta[2]], dma_engine_mask=m, remote_sem=sem, src=a, dst=b)
-                                        for a, b, m in tr], ["w5_%d" % e])
-            defs["ar%d" % e] = ("ext", sem, 8 * len(tr))
+            ways = [("Y%d" % l, lo, 512, done)] if l < 2 else [("Y20", lo, 256, done[:1]), ("Y21", lo + 512, 256, done)]
+            for m, c0, w, deps in ([("Yi", 0, 512, taps)] if l == 0 else []) + ways:
+                send(m, [T.vb2[:, c0 + w * j:c0 + w * (j + 1)] for j in range(2)], deps, w // 2)
+                dma("o_" + m, [(T.yv[:, c0 + w * j:c0 + w * (j + 1)], T["k" + MSG[m][1]][8 * p[1]:8 * p[1] + 8])
+                               for j, p in enumerate(MSG[m][2])], ["a" + m], kb=w // 2)
+        looked = look("w1_%d" % e, T.gf, 512 * e, fl[k][:, 0:lo + 1024], T.lf, 32 * e, 512,
+                      counted + ["lf" + TAG[e]] + (["m_t0"] if e == 0 else []) + (before if l else []))
+        before = counted + (before if l else [])
+        if k == 0:
+            tables = tables + looked
+        pick("w2_%d" % e, T.pf[:, 1:64:2], lambda i, e=e: T.gf[:, 512 * e + i:512 * e + 512:16],
+             slide(T.zu if k == 0 else T.z1) if e < 8 else lambda i: T.zs[:, 120 - 8 * i:248 - 8 * i],
+             looked + ["g_zu" if k == 0 else "g_z1" if e < 8 else "g_zs", "m_pf"] + (["sc_%d" % (e - 1)] if e else []))
+        nodes = T.vl[:, 64 * e:64 * e + 64] if e < 8 else T.vl[:, 576:640]
+        op("sc_%d" % e, "V", lambda e=e, nodes=nodes: V.tensor_tensor_scan(T.rs[:, 64 * e:64 * e + 64], T.pf[:, 0:64], nodes,
+                                                                          0.0, ALU.max, ALU.min),
+           ["w2_%d" % e, "eu" + TAG[e] if e < 8 else "e_d8"])
+        if e == 8:
+            op("w5", "V", copy("V", T.rf[:], T.rs[:, 64 * e + 7:64 * e + 64:8]), ["sc_8"])
+            send("T", [T.rf[:]], ["w5"], 0)
+            dma("o_t", [(T.yt[:], T.kt[:])], ["aT"])
+        elif e != 5:
+            j = e - (e > 5)
+            mk = T.mk[:, 64 * j:64 * j + 64]
+            gather("mk%d" % e, "V", lambda e=e, mk=mk: V.tensor_tensor(mk, T.rs[:, 64 * e:64 * e + 64].indirect(T.of[:]), T.own[:], ALU.mult),
+                   ["sc_%d" % e, "c_of", "g_own"], 64)
             if e < 5:
-                dma("lr%d" % e, [(T.lr[:, 64 * e:64 * e + 64], T.ru2[8 * e:8 * e + 8])], ["ar%d" % e])
-            elif e < 8:
-                dma("lr%d" % e, [(T.tab[h:128:16, 1024 * (l + 1):1024 * (l + 2)], T.rh2[8 * (2 * l + h):8 * (2 * l + h) + 8])
-                                 for h in range(2)], ["ar%d" % e, "gu2"])
+                mm("pl%d" % e, [(T.pl[:, 0:64], T.ee[:], mk, True, True)], ["mk%d" % e] + spread, 256)
+                op("el%d" % e, "V", copy("V", T.lr[:, 64 * e:64 * e + 64], T.pl[:, 0:64]), ["pl%d" % e])
+                spread = ["el%d" % e]
             else:
-                dma("o_t", [(T.yt[:], T.rf2[:])], ["ar8"])
+                rh = T.rh[:, 16 * l:16 * l + 16]
+                mm("pl%d" % e, [(T.pl[64 * h:64 * h + 64, 0:16], mk, T.ee[:, 0:16], True, True) for h in range(2)], ["mk%d" % e] + spread, 256)
+                op("hi%d" % e, "V", copy("V", rh, T.pl[:, 0:16]), ["pl%d" % e])
+                op("lo%d" % e, "V", lambda rh=rh: V.tensor_tensor(rh[64:128, :], T.pl[64:128, 0:16], rh[64:128, :], ALU.subtract), ["hi%d" % e])
+                spread = ["lo%d" % e]
+                send("R%d" % e, [rh], ["lo%d" % e], 0)
+                dma("in_R%d" % e, [(T.vb1[h:128:16, lo:lo + 1024], T.kr[8 * l:8 * l + 8, 64 * h:64 * h + 64, :]) for h in range(2)],
+                    ["aR%d" % e, "id_R"])
     for l in (1, 2):
-        c0 = 2048 * (l - 1)
-        fw = T.tab[:, 0:1024 * (l + 1)]
-        deps = ["rm8", "lr6"] + (["lr7"] if l == 2 else [])
-        op("fa%d" % l, copy("S", T.gfin[:, c0:c0 + 1024], fw.indirect(T.lfin[:, 64 * (l - 1):64 * l])), deps)
-        for h in range(2):
-            op("fb%d_%d" % (l, h), copy("V", T.gfin[:, c0 + 1024 + 512 * h:c0 + 1536 + 512 * h],
-                                        fw.indirect(T.lfin[:, 64 * (l + 1) + 32 * h:64 * (l + 1) + 32 * h + 32])), deps)
-        po = [T.po0, T.po1][l - 1][:, 0:128]
-        op("xf%d" % l, pick(po, lambda i, c0=c0: T.gfin[:, c0 + i:c0 + 2048:16], zrow(0)), ["fa%d" % l, "fb%d_0" % l, "fb%d_1" % l, "t_lo"])
-        op("ef%d" % l, copy("S", T.oo[:, 128 * l:128 * l + 128], po), ["xf%d" % l])
+        po = [T.po0, T.po1][l - 1]
+        for j, (nm, col) in enumerate([("fa%d" % l, acol[l]), ("fb%d" % l, bcol[l])]):
+            c0 = 2048 * (l - 1) + 1024 * j
+            names = look(nm, T.gfin, c0, T.vb1[:, 0:1024 * (l + 1)], T.lab, col, 1024, ["in_R6"] + (["in_R7"] if l == 2 else []))
+            pick("x" + nm, po[:, 64 * j:64 * j + 64], lambda i, c0=c0: T.gfin[:, c0 + i:c0 + 1024:16], zrow(0), names + ["t_lo"])
+        op("ef%d" % l, "S", copy("S", T.oo[:, 128 * l:128 * l + 128], po[:, 0:128]), ["xfa%d" % l, "xfb%d" % l], 128)
         dma("o_l%d" % l, [(T.ya[:, 64 * l:64 * l + 64], T.oo[:, 128 * l:128 * l + 64]),
-                          (T.yb[:, 64 * l:64 * l + 64], T.oo[:, 128 * l + 64:128 * l + 128])], ["ef%d" % l])
+                          (T.yb[:, 64 * l:64 * l + 64], T.oo[:, 128 * l + 64:128 * l + 128])], ["ef%d" % l], q="S")
 
-    order = {
-        q: s for q, s in ORDER.items()}
+    if "order" not in PLAN:
+        PLAN["order"] = plan(defs)
+        PLAN["sends"] = [n[1:] for n in PLAN["order"]["G"] if defs[n]["kind"] == "rem"]
+    if not issue:
+        return
     queue = {"V": V, "S": S, "P": PE, "G": g, "Y": SY}
-    order = {q: s.split() for q, s in order.items()}
-    wanted = set(d for v in defs.values() if v[0] != "ext" for d in v[2] if d[0] != "~")
-    token, nd = {}, 0
-    for name, v in defs.items():
-        if v[0] == "ext":
-            token[name] = (name, v[1], v[2])
+    order = {q: PLAN["order"][q] for q in queue}
+    wanted = set(d for v in defs.values() if v["kind"] != "ext" for d in v["deps"] if d[0] != "~")
+    token, nd, left = {}, 0, 0
+    for name in PLAN["order"]["X"]:
+        token[name] = (name,) + defs[name]["what"]
     for q, names in order.items():
         cnt = 0
         for name in names:
-            kind = defs[name][0]
+            kind = defs[name]["kind"]
             if kind == "op" and name in wanted:
                 cnt += 1
                 token[name] = ("q" + q, T.sem["q" + q], cnt)
             elif kind == "dma":
-                token[name] = ("m%d" % nd, T.sem["m%d" % nd], 16 * len(defs[name][1]))
+                token[name] = ("m%d" % nd, T.sem["m%d" % nd], 16 * len(defs[name]["what"]))
                 nd += 1
-    placed = [n for names in order.values() for n in names]
-    assert sorted(placed) == sorted(n for n, v in defs.items() if v[0] != "ext")
     waited = {}
     for q, names in order.items():
         seen = {}
         for name in names:
-            kind, what, deps = defs[name]
+            kind, what = defs[name]["kind"], defs[name]["what"]
             most = {}
-            for d in [d for d in deps if d[0] != "~"]:
+            for d in [d for d in defs[name]["deps"] if d[0] != "~"]:
                 key, sem, val = token[d]
                 if val > most.get(key, (None, 0))[1]:
                     most[key] = (sem, val)
@@ -414,7 +492,8 @@ def rank_program(g, core, T, topo):
                     queue[q].dma_start(out, src).then_inc(token[name][1], 16)
             else:
                 g.remote_dma_fused(what, local_sem=T.sem.left)
-    g.wait_ge(T.sem.left, nleft)
+                left += len(eng)
+    g.wait_ge(T.sem.left, left)
     for name, (key, sem, val) in token.items():
         if val > waited.get(key, 0):
             g.wait_ge(sem, val)

@@ -5,36 +5,60 @@ B16, F32, I32, U16 = "bfloat16", "float32", "int32", "uint16"
 SCRATCH = {n: ("sbuf", [128] + list(s), d) for n, s, d in [
     ("vb0", [4096], B16), ("vb1", [4096], B16), ("vb2", [4096], B16), ("wb1", [3072], B16), ("wb2", [3072], B16),
     ("t0", [4096], B16), ("tb", [6144], B16), ("df", [9216], B16), ("vc", [9216], B16), ("tab", [4096], B16), ("tx", [1024], B16),
-    ("gf", [9 * 512], B16), ("gch", [2048], B16), ("gfin", [4096], B16), ("fi", [384], I32), ("ci", [256], I32), ("ci2", [192], I32),
+    ("gf", [9 * 512], B16), ("gch", [2048], B16), ("gfin", [4096], B16), ("fi", [384], I32), ("ci", [256], I32),
     ("lab", [384], U16), ("lab2", [384], U16), ("lct", [256], U16), ("lc2", [192], U16), ("lr", [5 * 64], U16),
-    ("cdi", [256], I32), ("cdf", [256], F32), ("idw", [128], I32), ("thl", [64], B16), ("si", [48], I32), ("sf", [48], F32),
+    ("cdi", [256], I32), ("cdf", [256], F32), ("idw", [128], I32), ("thl", [256], B16), ("si", [48], I32), ("sf", [48], F32),
     ("ones", [128], F32), ("oneb", [128], B16), ("one4", [4, 8], B16), ("zv", [144], B16), ("zu", [144], B16), ("zo", [144], B16),
-    ("z1", [144], B16), ("zj", [4, 144], B16), ("zs", [256], B16), ("i16", [16], F32), ("e16", [16], F32), ("f16", [128], F32),
-    ("ee", [128], F32), ("own", [64], F32), ("pls", [128], F32), ("psl", [128], F32), ("oi", [8], I32), ("of", [4], U16),
-    ("eye", [128], F32), ("big", [8], B16), ("vl", [80 * 8], F32), ("lf", [72 * 4], U16), ("rs", [72 * 8], F32),
-    ("lu", [144], U16), ("xv", [9 * 64], B16), ("mk", [7 * 64], F32), ("rh", [32], B16), ("rf", [8], F32), ("oo", [384], F32)]}
-SCRATCH.update({n: ("dram", s, d) for n, s, d in [
-    ("dt", [8, 4096], B16), ("hl", [4, 128, 96], U16), ("kl", [32, 128, 12], U16), ("hq", [8, 128, 256], B16), ("kq", [64, 128, 32], B16),
-    ("hh", [6, 128, 512], B16), ("kh", [48, 128, 64], B16), ("hv", [3, 128, 64], B16), ("kv", [24, 128, 64], B16),
-    ("hr", [2, 128, 16], B16), ("kr", [16, 128, 16], B16), ("ht", [1, 128, 8], F32), ("kt", [8, 128, 8], F32)]})
+    ("z1", [144], B16), ("zj", [4, 144], B16), ("zs", [256], B16), ("i16", [16], F32), ("f16", [128], F32), ("ee", [128], F32),
+    ("own", [128], F32), ("pls", [128], F32), ("psl", [128], F32), ("oi", [16], I32), ("of", [8], U16), ("sel", [8, 8], B16),
+    ("idn", [256], B16), ("p8", [1], F32), ("big", [8], B16), ("vl", [80 * 8], F32), ("lf", [72 * 4], U16), ("rs", [72 * 8], F32),
+    ("lu", [160], U16), ("xv", [9 * 64], B16), ("mk", [8 * 64], F32), ("rh", [32], B16), ("rf", [8], F32), ("oo", [2, 192], F32)]}
+SCRATCH["dt"] = ("dram", [10, 4096], B16)
 SCRATCH.update({n: ("psum", [128, 512], F32) for n in ("pv0", "pv1", "pp", "po0", "po1", "pl", "pf", "pc")})
+MSG = {"L": (True, U16, 384, [0, 1, 2, 3]), "X0": (True, B16, 512, [0, 2]), "X1": (True, B16, 512, [1, 3]),
+       "Yi": (True, B16, 1024, [0]), "Y0": (True, B16, 1024, [2]), "Y1": (True, B16, 1024, [0]),
+       "Y20": (True, B16, 512, [2]), "Y21": (True, B16, 512, [0, 3]),
+       "V0": (False, B16, 64, [1, 3]), "V1": (False, B16, 64, [1, 3]), "V2": (False, B16, 64, [1, 3]),
+       "R6": (False, B16, 16, [1]), "R7": (False, B16, 16, [1]), "T": (False, F32, 8, [1])}
+
+
+def buffers():
+    for m, (dealt, dtype, columns, by) in MSG.items():
+        parts = len(by) if dealt else 1
+        SCRATCH["h" + m] = ("dram", [parts, 128, columns // parts], dtype)
+        SCRATCH["k" + m] = ("dram", [8 * parts, 128, columns // parts // (8 if dealt else 1)], dtype)
+
+
+buffers()
+SEMAPHORES = ["qV", "qS", "qP", "qG", "left"] + ["a" + m for m in MSG] + ["m%d" % i for i in range(60)]
 AT = [7, 5, 3, 1, 0]
 BIG = 4096.0
-MSG = {"L": (True, "l", [(h, h, None) for h in range(4)]),
-       "X0": (True, "q", [(0, 0, None), (2, 1, None)]), "X1": (True, "q", [(1, 2, None), (3, 3, None)]),
-       "Yi": (True, "h", [(0, 0, None), (2, 1, None)]), "Y0": (True, "h", [(1, 2, None), (3, 3, None)]),
-       "Y1": (True, "h", [(0, 4, None), (2, 5, None)]),
-       "Y20": (True, "q", [(0, 4, None), (2, 5, None)]), "Y21": (True, "q", [(0, 6, None), (2, 7, None)]),
-       "V0": (False, "v", [(1, 0, 0), (3, 0, 1)]), "V1": (False, "v", [(1, 1, 0), (3, 1, 1)]), "V2": (False, "v", [(1, 2, 0), (3, 2, 1)]),
-       "R6": (False, "r", [(1, 0, None)]), "R7": (False, "r", [(1, 1, None)]), "T": (False, "t", [(1, 0, None)])}
-SEMAPHORES = ["qV", "qS", "qP", "qG", "left"] + ["a" + m for m in MSG] + ["m%d" % i for i in range(70)]
 HALVES, QUARTERS = [(0, 512), (512, 1024)], [(0, 256), (256, 512), (512, 768), (768, 1024)]
 CUTS = [QUARTERS] * 3 + [HALVES] * 5 + [[(0, 512), (512, 768), (768, 1024)]]
-COPY = [""] * 3 + ["YG"] * 5 + ["GSS"]
-WIDE = (7, 8)
-SHARE = {"w1_7": 2, "w1_8": 2, "tap2": 2, "fb1": 1, "fb2": 1}
-WAKE, TURNS, SEED = 80, 600, 2
-PLAN = {}
+COPY = [""] * 3 + ["GG"] * 5 + ["GYS"]
+WIDE = (8,)
+SHARE = {"w1_8": 2, "tap2": 2, "fb1": 1, "fb2": 1}
+CHAINS = [(2, 3, 5, 48, 32), (3, 5, 8, 112, 0), (4, 8, 9, 136, 24)]
+
+ORDER = {
+    "V": "m_tab0 m_tab2 m_oneb m_ones m_tab1 m_one4 c_0 c_ab A0_1 A0_2 A0_0 A0_3 c_cdf c_sf A1_1 A1_2 A1_0 A1_3 t_lo l_s1 c_ct "
+         "A2_3 A2_1 A2_2 A2_0 tap1_0 tap1_2 vt0_0 vt0_1 vt1_1 vt1_0 l_s2 vt2_0 vt2_1 c_of0 c_of1 c_o0 l_s3 lf0 "
+         "A3_0 c_og0 c_og1 c_of2 sc_0 mk0 el0 A3_1 sc_1 mk1 lu2 vt3_0 el1 vt3_1 A4_0 A4_1 lf1 vt4_0 lf2 vt4_1 sc_2 mk2 "
+         "A5_0 el2 A5_1 tap2V sc_3 mk3 vt5_0 el3 A6_0 vt5_1 sc_4 lu3 A6_1 mk4 vt6_0 lf3 el4 vt6_1 A7_0 A7_1 vt7_0 vt7_1 sc_5 lu4 "
+         "A8_0 sc_6 mk6 A8_1 lf4 hi6 lo6 vt8_0 sc_7 mk7 A8_2 hi7 lo7 vt8_1 vt8_2 w1_8V sc_8 w5 fb1V fb2V efb",
+    "S": "ld_0 m_tab3 m_pc m_pf0 m_pf B0_1 B0_2 B0_0 B0_3 B1_1 B1_2 B1_0 B1_3 t_hi B2_3 B2_1 B2_2 B2_0 tap1_1 tap1_3 "
+         "g_s1S ev0 g_s2S ev1 e_ee g_s3S ev2 B3_0 w1_0S eu0 B3_1 w1_1S w3_0S gu1S w3_1S B4_0 B4_1 gu2S w4_0S w4_1S eu1 w1_2S ev3 "
+         "B5_0 B5_1 w1_3S ev4 eu2 tap2S B6_0 w1_4S B6_1 w6_0S ev5 gu3S w6_1S B7_0 eu3 B7_1 ev6 w7_0S w1_5S w7_1S w1_6S "
+         "B8_0 ev7 B8_1 B8_2 gu4S w1_7S eu4 e_d8 vc8_2 ev8_0 ev8_1 ev8_2 w1_8S fa1S fa2S efa o_fa",
+    "P": "p_t p_s pv0_0 pv0_1 x_s1 pv1_0 pv1_1 p_ee x_s2 pv2_0 pv2_1 x_s3 w2_0 pl0 w2_1 pl1 xu31 xu11 xu21 xu01 pv3_0 pv3_1 xu2 w2_2 "
+         "pv4_0 pl2 pv4_1 w2_3 pl3 pv5_0 w2_4 pv5_1 xu3 pl4 pv6_0 pv6_1 w2_5 pv7_0 pv7_1 w2_6 xu4 pl6 w2_7 p_d8 pl7 "
+         "pv8_0 pv8_1 pv8_2 w2_8 xfa1 xfb1 xfa2 xfb2",
+    "G": "io_n0 io_cd io_n1 m_zv io_id g_zv0 g_i16 g_psl sL m_t0 m_zj sX0 sX1 g_zv g_zj0 g_zj g_f16 m_big sV0 io_of m_zu g_zu0 g_zu sV1 "
+         "g_own0 m_zo0 g_own m_zo m_sel io_og sV2 g_seb0 g_seb g_sea0 g_sea g_sel io_oh vc3_0 g_owo0 g_owo m_z1 g_z1 vc3_1 m_zs g_pls g_zs "
+         "vc4_0 vc4_1 vc5_0 vc5_1 sYi vc6_0 vc6_1 sY0 vc7_0 vc7_1 sY1 vc8_0 sR6 sY20 sY21 sR7 sT",
+    "Y": "ld_x ld_ab ld_c16 dt_n ld_id ld_si ld_ct tab_n vc0 dt_c vc1 tab_c vc2 dt_in c_c2 dt_1 in_L in_X0 in_X1 F0 dt_2 dt_3 F1 tab_j "
+         "cp1 F2 F3 F4 cp2 id_R F5 F6 o_Yi F7 vc8_1 o_Y0 in_R6 o_Y1 in_R7 o_Y20 o_Y21 o_t o_fb",
+}
 
 
 def relays(rank_core, T, topo):
@@ -66,89 +90,36 @@ def deal(core, dests, each, topo):
 def hand_on(g, core, s, h, T, topo):
     n = len(T.cores)
     engines = len(topo.engines(T.cores[s], core))
-    left = 0
-    mine = [(m, slot, share) for m in PLAN["sends"] for hh, slot, share in MSG[m][2] if hh == h]
-    for j, (m, slot, share) in enumerate(mine):
-        dealt, b, parts = MSG[m]
-        sem = T.sem["a" + m]
-        dests = [d for d in range(n) if share is None or (d - s) % 2 == share]
-        each = n // len(dests)
+    mine = [c[1:] for c in ORDER["G"].split() if c[0] == "s" and h in MSG[c[1:]][3]]
+    for j, m in enumerate(mine):
+        dealt, by = MSG[m][0], MSG[m][3]
+        sem, slot, each = T.sem["a" + m], by.index(h) if dealt else 0, 1 if dealt else len(by)
+        dests = [d for d in range(n) if (d - s) % each == by.index(h) % each]
         masks = deal(core, [T.cores[d] for d in dests], each, topo)
         if dealt:
-            g.sync.wait_ge(sem, engines // len(parts))
-            g.sync.dma_start(T["k" + b][n * slot:n * slot + n], T["h" + b][slot]).then_inc(T.sem["m%d" % j], 16)
+            g.sync.wait_ge(sem, engines // len(by))
+            g.sync.dma_start(T["k" + m][n * slot:n * slot + n], T["h" + m][slot]).then_inc(T.sem["m%d" % j], 16)
             g.wait_ge(T.sem["m%d" % j], 16)
         else:
-            g.wait_ge(sem, engines // len(parts))
+            g.wait_ge(sem, engines // len(by))
         g.remote_dma_fused([RemoteDMATransfer(dst_ids=[dst_id(T.cores[d], core, topo)], dma_engine_mask=masks[T.cores[d]], remote_sem=sem,
-                                              src=T["k" + b][n * slot + d] if dealt else T["h" + b][slot], dst=T["k" + b][n * slot + s])
+                                              src=T["k" + m][n * slot + d] if dealt else T["h" + m][slot], dst=T["k" + m][n * slot + s])
                             for d in dests], local_sem=T.sem.left)
-        left += each * len(dests)
-    g.wait_ge(T.sem.left, left)
-
-
-def plan(defs):
-    before = {n: [(d.lstrip("~"), 0 if d[0] == "~" else defs[d]["lat"] + WAKE) for d in v["deps"]] for n, v in defs.items()}
-    after = {n: [] for n in defs}
-    for n in defs:
-        for d, gap in before[n]:
-            after[d].append((n, gap))
-
-    def place(rank, needs, frees, lead):
-        end, busy = {}, {q: [] for q in "VSPGYX"}
-        missing = {n: len(needs[n]) for n in defs}
-        ready = [n for n in defs if not missing[n]]
-        while ready:
-            n = min(ready, key=rank.get)
-            ready.remove(n)
-            t, cost, taken = max([end[d] + gap for d, gap in needs[n]] + [lead[n]]), defs[n]["cost"], busy[defs[n]["q"]]
-            at = len(taken)
-            for j, (a, b) in enumerate(taken):
-                if t + cost <= a:
-                    at = j
-                    break
-                t = max(t, b)
-            end[n] = t + cost
-            taken.insert(at, (t, t + cost))
-            for u, gap in frees[n]:
-                missing[u] -= 1
-                if not missing[u]:
-                    ready.append(u)
-        return end
-    none, last = {n: 0 for n in defs}, {n: v["lat"] for n, v in defs.items()}
-    best, seed = (1e9, None, {n: -j for j, n in enumerate(defs)}), SEED
-    for turn in range(TURNS):
-        rank = dict(best[2])
-        for n in defs:
-            seed = (seed * 1103515245 + 12345) % 2 ** 31
-            if seed % 3000 < 1000:
-                rank[n] += seed // 3000 % 2000 - 1000
-        for twice in range(2):
-            back = place(rank, after, before, last)
-            ahead = place({n: -back[n] for n in defs}, before, after, none)
-            rank = {n: -ahead[n] - last[n] for n in defs}
-        length = max(ahead[n] + last[n] for n in defs)
-        if length <= best[0]:
-            best = (length, ahead, rank)
-    PLAN["began"] = best[1]
-    PLAN["defs"] = defs
-    return {q: sorted((n for n in defs if defs[n]["q"] == q), key=lambda n: best[1][n]) for q in "VSPGYX"}
+    g.wait_ge(T.sem.left, n * len(mine))
 
 
 def rank_program(g, core, T, topo):
     r = T.rank_of(core)
     if r is not None:
-        rank_calls(g, core, r, T, topo, True)
+        issue(g, rank_calls(g, core, r, T, topo), T, len(topo.engines(core, relays(core, T, topo)[0])))
         return
     for s, c in enumerate(T.cores):
         if core in topo.cores_of(c) and core in relays(c, T, topo):
-            if "sends" not in PLAN:
-                rank_calls(g, c, s, T, topo, False)
             hand_on(g, core, s, relays(c, T, topo).index(core), T, topo)
 
 
-def rank_calls(g, core, r, T, topo, issue):
-    V, S, PE, SY = g.vector, g.scalar, g.tensor, g.sync
+def rank_calls(g, core, r, T, topo):
+    V, S, PE = g.vector, g.scalar, g.tensor
     hands = relays(core, T, topo)
     eng = topo.engines(core, hands[0])
     defs = {}
@@ -156,26 +127,19 @@ def rank_calls(g, core, r, T, topo, issue):
     wb = [T.vb0, T.wb1, T.wb2]
     fl = [T.t0, T.vb0, T.t0]
 
-    def put(name, q, kind, what, deps, cost, lat=0):
-        defs[name] = {"q": q, "kind": kind, "what": what, "deps": list(deps), "cost": cost, "lat": lat}
+    def op(name, q, fn, deps=()):
+        defs[name] = ("op", q, fn, list(deps))
 
-    def op(name, q, fn, deps=(), cycles=64):
-        put(name, q, "op", fn, deps, (170 if q == "G" else 40) + 0.9 * max(64, cycles))
+    def dma(name, pairs, deps=(), q="Y"):
+        defs[name] = ("dma", q, pairs, list(deps))
 
-    def gather(name, q, fn, deps, n):
-        put(name, q, "op", fn, deps, 60 + 1.35 * n)
-
-    def dma(name, pairs, deps=(), q="Y", kb=0):
-        put(name, q, "dma", pairs, deps, 60 * len(pairs) + (3 * kb if q == "Y" else 0), 1100 + (0 if q == "Y" else 3 * kb))
-
-    def mm(name, parts, deps, cycles=64):
+    def mm(name, parts, deps):
         def fn():
             ins = None
             for out, lhs, rhs, st, sp in parts:
                 ins = PE.matmul(out, lhs, rhs, st, sp)
             return ins
-        put(name, "P", "op", fn, deps, 0.5 * cycles * len(parts))
-        defs[name]["parts"] = len(parts)
+        op(name, "P", fn, deps)
 
     def pick(name, out, rhs_of, lhs_of, deps):
         mm(name, [(out, lhs_of(i), rhs_of(i), i == 0, i == 15) for i in range(16)], deps)
@@ -197,121 +161,136 @@ def rank_calls(g, core, r, T, topo, issue):
     def look(name, out, c0, win, lst, l0, n, deps):
         parts = {0: [("S", 0, n)], 1: [("V", 0, n)], 2: [("S", 0, n // 2), ("V", n // 2, n)]}[SHARE.get(name, 0)]
         for q, a, b in parts:
-            gather(name + q, q, copy(q, out[:, c0 + a:c0 + b], win.indirect(lst[:, l0 + a // 16:l0 + b // 16])), deps, b - a)
+            op(name + q, q, copy(q, out[:, c0 + a:c0 + b], win.indirect(lst[:, l0 + a // 16:l0 + b // 16])), deps)
         return [name + q for q, a, b in parts]
 
-    def send(m, srcs, deps, kb):
-        dealt, b, parts = MSG[m]
-        each = len(eng) // len(parts)
-        put("s" + m, "G", "rem", [RemoteDMATransfer(dst_ids=[dst_id(hands[h], core, topo)], dma_engine_mask=bits(eng[each * j:each * j + each]),
-                                                    remote_sem=T.sem["a" + m], src=srcs[j], dst=T["h" + b][slot])
-                                  for j, (h, slot, share) in enumerate(parts)], deps, 3800 if m == "L" else 420)
-        put("a" + m, "X", "ext", (T.sem["a" + m], 8 * len(parts)), ["s" + m], 0, (3500 if dealt else 2300) + 8 * kb)
+    def send(m, tile, c0, deps):
+        dealt, dtype, columns, by = MSG[m]
+        each, w = len(eng) // len(by), columns // len(by) if dealt else columns
+        defs["s" + m] = ("rem", "G", [RemoteDMATransfer(
+            dst_ids=[dst_id(hands[h], core, topo)], dma_engine_mask=bits(eng[each * j:each * j + each]), remote_sem=T.sem["a" + m],
+            src=tile[:, c0 + w * j * dealt:c0 + w * (j * dealt + 1)], dst=T["h" + m][j * dealt]) for j, h in enumerate(by)], deps)
+        defs["a" + m] = ("ext", None, (T.sem["a" + m], 8 * len(by)), [])
+
+    def take(name, m, tile, c0):
+        columns, by = MSG[m][2:]
+        w = columns // len(by)
+        dma(name, [(tile[:, c0 + w * j:c0 + w * (j + 1)], T["k" + m][8 * j:8 * j + 8]) for j in range(len(by))], ["a" + m])
 
     mine = slice(16 * r, 16 * r + 16)
     acol, bcol = [64, 128, 192], [0, 256, 320]
-    dma("ld_0", [(T.fi[:, 0:64], T.fb[:, 0:64]), (T.fi[:, 64:128], T.fa[:, 0:64])], q="S", kb=250)
-    dma("ld_x", [(T.vb0[:, 0:1024], T.x[:])], kb=256)
-    dma("ld_ab", [(T.fi[:, 128:256], T.fa[:, 64:192]), (T.fi[:, 256:384], T.fb[:, 64:192])], ["~ld_x"], kb=150)
-    dma("ld_ct", [(T.ci[:, 0:192], T.cd[:]), (T.ci[:, 192:256], T.tp[:])], ["~ld_ab"], kb=150)
-    dma("ld_c16", [(T.cdi[0:16, 64:256], T.cd[mine, :])], ["~ld_ab"], kb=20)
-    dma("ld_si", [(T.si[:, 8 * l:8 * l + 8], T.cd[mine, 64 * l:64 * l + 64]) for l in range(3)] + [(T.si[:, 40:48], T.tp[mine, :])], ["~ld_ab"],
-        kb=100)
+    dma("ld_0", [(T.fi[:, 0:64], T.fb[:, 0:64]), (T.fi[:, 64:128], T.fa[:, 0:64])], q="S")
+    dma("ld_x", [(T.vb0[:, 0:1024], T.x[:])])
+    dma("ld_ab", [(T.fi[:, 128:256], T.fa[:, 64:192]), (T.fi[:, 256:384], T.fb[:, 64:192])])
+    dma("ld_ct", [(T.ci[:, 0:192], T.cd[:]), (T.ci[:, 192:256], T.tp[:])])
+    dma("ld_c16", [(T.cdi[0:16, 64:256], T.cd[mine, :])])
+    dma("ld_si", [(T.si[:, 8 * l:8 * l + 8], T.cd[mine, 64 * l:64 * l + 64]) for l in range(3)] + [(T.si[:, 40:48], T.tp[mine, :])])
     dma("ld_id", [(T.si[:, 24 + 8 * l:32 + 8 * l], T.idw[0:16, 64 * l:64 * l + 64]) for l in range(2)], ["io_id"])
-    dma("ld_c2", [(T.ci2[16 * a:16 * a + 16, :], T.cd[mine, :]) for a in range(8)], ["~ld_ct"], kb=96)
-    for nm, ap, val, n in [("ones", T.ones[:], 1.0, 128), ("oneb", T.oneb[:], 1.0, 64), ("one4", T.one4[:], 1.0, 16), ("zj", T.zj[:], 0.0, 288),
-                           ("tab0", T.tab[:, 0:1024], 0.0, 512), ("tab1", T.tab[:, 1024:2048], 0.0, 512), ("tab2", T.tab[:, 2048:3072], 0.0, 512),
-                           ("pc", T.pc[:, 0:384:2], BIG, 192), ("pf0", T.pf[:, 0:64:2], 0.0, 32),
-                           ("pf", T.pf[:, 0:64:8], BIG, 8)]:
-        op("m_" + nm, "V", lambda ap=ap, val=val: V.memset(ap, val), ["m_pf0"] if nm == "pf" else [], n)
-    for nm, ap, val, n in [("zv", T.zv[:], 0, 144), ("zu", T.zu[:], 0, 144), ("zo0", T.zo[:], 0, 144), ("z1", T.z1[:], 0, 144),
-                           ("zs", T.zs[:], 0, 256), ("t0", T.t0[:, 0:1024], 0, 1024), ("big", T.big[:], int(BIG), 8),
-                           ("zo", T.zo[:, 15:143:16], 1, 8)]:
+    for nm, ap, val in [("ones", T.ones[:], 1.0), ("oneb", T.oneb[:], 1.0), ("one4", T.one4[:], 1.0)] + [
+            ("tab%d" % j, T.tab[:, 1024 * j:1024 * j + 1024], BIG) for j in range(3)]:
+        op("m_" + nm, "V", lambda ap=ap, val=val: V.memset(ap, val))
+    op("m_tab3", "S", copy("S", T.tab[:, 3072:4096], T.tab[:, 0:1024]), ["m_tab0"])
+    for nm, ap, val, n in [("pc", T.pc[:, 0:256:2], BIG, 128), ("pf0", T.pf[:, 0:64:2], 0.0, 32), ("pf", T.pf[:, 0:64:8], BIG, 8)]:
+        op("m_" + nm, "S", lambda ap=ap, val=val, n=n: S.activation(ap, T.oneb[:, 0:n], ACT.Identity, scale=val),
+           ["m_oneb"] + (["m_pf0"] if nm == "pf" else []))
+    for nm, ap, val, n in [("zj", T.zj[:], 0, 576), ("zv", T.zv[:], 0, 144), ("zu", T.zu[:], 0, 144), ("zo0", T.zo[:], 0, 144),
+                           ("z1", T.z1[:], 0, 144), ("zs", T.zs[:], 0, 256), ("t0", T.t0[:, 0:1024], 0, 1024), ("big", T.big[:], int(BIG), 8),
+                           ("sel", T.sel[:], 1, 64), ("zo", T.zo[:, 15:143:16], 1, 8)]:
         op("m_" + nm, "G", lambda ap=ap, val=val, n=n: g.iota(ap, [[0, n]], val, 0, allow_small_or_imprecise_dtypes=True),
-           ["m_zo0"] if nm == "zo" else [], 2 * n)
-    op("m_tab3", "S", copy("S", T.tab[:, 3072:4096], T.tab[:, 0:1024]), ["m_tab0"], 1024)
-    op("io_cd", "G", lambda: g.iota(T.cdi[0:16, 0:64], [[16, 64]], 0, 1), [], 128)
-    op("io_id", "G", lambda: g.iota(T.idw[0:16, :], [[16, 128]], 1024, 1), [], 256)
-    op("io_of", "G", lambda: g.iota(T.oi[:, 0:4], [[0, 4]], 0, 1))
-    zvv, zuv, zjv, one8 = T.zv[:, 15:143:16], T.zu[:, 15:143:16], T.zj[:, :, 15:143:16], T.oneb[:, 0:8]
-    for nm, out, src, pat, cmp, base, deps, n in [
-            ("i16", T.i16[0:16, :], T.ones[0:16, 0:16], [[-1, 16]], ALU.is_equal, 0, ["m_ones"], 16),
-            ("f16", T.f16[0:16, :], T.ones[0:16, :], [[0, 8], [-1, 16]], ALU.is_equal, 0, ["m_ones"], 128),
-            ("psl", T.psl[:], T.ones[:], [[-1, 8], [-8, 16]], ALU.is_equal, 0, ["m_ones"], 128),
-            ("pls", T.pls[:], T.ones[:], [[-1, 16], [-16, 8]], ALU.is_equal, 0, ["m_ones"], 128),
-            ("eye", T.eye[:], T.ones[:], [[-1, 128]], ALU.is_equal, 0, ["m_ones"], 128),
-            ("z1", T.z1[:, 15:143:16], T.big[:], [[-16, 8]], ALU.is_equal, 0, ["m_big", "m_z1"], 8),
-            ("zs", T.zs[:, 120:128], T.big[:], [[-16, 8]], ALU.is_equal, 0, ["m_big", "m_zs"], 8),
-            ("zv0", zvv, one8, [[-16, 8]], ALU.is_ge, 0, ["m_oneb", "m_zv"], 8),
-            ("zu0", zuv, T.big[:], [[-16, 8]], ALU.is_ge, -8, ["m_big", "m_zu"], 8),
-            ("zj0", zjv, T.one4[:], [[-2, 4], [-16, 8]], ALU.is_ge, 0, ["m_one4", "m_zj"], 32),
-            ("own0", T.own[:], T.ones[:, 0:64], [[-16, 8], [0, 8]], ALU.is_ge, 0, ["m_ones"], 64)]:
-        op("g_" + nm, "G", lambda a=(out, src, pat, cmp, 0.0, base, 1): g.affine_select(*a), deps, 2 * n)
-    for nm, out, pat, base, n in [("zv", zvv, [[16, 8]], 15, 8), ("zu", zuv, [[16, 8]], 15, 8), ("zj", zjv, [[2, 4], [16, 8]], 1, 32),
-                                  ("own", T.own[:], [[16, 8], [0, 8]], 15, 64)]:
-        op("g_" + nm, "G", lambda a=(out, out, pat, ALU.is_ge, 0.0, base, -1): g.affine_select(*a), ["g_%s0" % nm], 2 * n)
-    mm("p_ee", [(T.pl[:, 0:128], T.f16[0:16, :], T.f16[0:16, :], True, True)], ["g_f16"], 512)
-    op("e_ee", "S", copy("S", T.ee[:], T.pl[:, 0:128]), ["p_ee"], 128)
-    op("c_of0", "V", lambda: V.tensor_scalar(T.oi[:, 4:8], T.oi[:, 0:4], 7, None, ALU.bitwise_and), ["io_of"])
-    op("c_of", "V", lambda: V.tensor_scalar(T.of[:], T.oi[:, 4:8], 8.0, 7.0, ALU.mult, ALU.add), ["c_of0"])
-    op("c_0", "V", copy("V", T.lab[:, 0:128], T.fi[:, 0:128]), ["ld_0"], 128)
-    op("c_ab", "V", copy("V", T.lab[:, 128:384], T.fi[:, 128:384]), ["ld_ab"], 256)
-    op("c_ct", "V", copy("V", T.lct[:], T.ci[:]), ["ld_ct"], 256)
-    op("c_c2", "V", copy("V", T.lc2[:], T.ci2[:]), ["ld_c2"], 192)
-    op("c_o0", "V", copy("V", T.oo[:, 0:128], T.fi[:, 0:128]), ["ld_0"], 128)
-    dma("o_l0", [(T.yb[:, 0:64], T.oo[:, 0:64]), (T.ya[:, 0:64], T.oo[:, 64:128])], ["c_o0"])
-    send("L", [T.lab[:, 96 * h:96 * h + 96] for h in range(4)], ["c_0", "c_ab"], 480)
-    dma("in_L", [(T.lab2[:, 96 * h:96 * h + 96], T.kl[8 * h:8 * h + 8]) for h in range(4)], ["aL"], kb=96)
-    op("c_cdf", "V", copy("V", T.cdf[0:16, :], T.cdi[0:16, :]), ["ld_c16", "io_cd"], 256)
-    mm("p_t", [(T.po0[:, 16 * h:16 * h + 16], T.cdf[0:16, 128 * h:128 * h + 128], T.i16[0:16, :], True, True) for h in range(2)],
-       ["c_cdf", "g_i16"], 256)
-    op("t_hi", "S", copy("S", T.thl[:, 0:32], T.po0[:, 0:32]), ["p_t"])
-    op("t_lo", "V", lambda: V.tensor_tensor(T.thl[:, 32:64], T.po0[:, 0:32], T.thl[:, 0:32], ALU.subtract), ["t_hi"])
-    dma("dt_c", [(T.dt[h, 2048 * a:2048 * a + 2048], T.thl[:, 32 * h + 16 * a:32 * h + 16 * a + 16]) for h in range(2) for a in range(2)],
-        ["t_hi", "t_lo"])
-    dma("tab_c", [(T.tab[16 * a:16 * a + 2, :], T.dt[0:2, :]) for a in range(8)], ["dt_c", "m_tab1", "m_tab2", "m_tab3"], kb=128)
+           ["m_zo0"] if nm == "zo" else [])
+    op("io_cd", "G", lambda: g.iota(T.cdi[0:16, 0:64], [[16, 64]], 0, 1))
+    op("io_id", "G", lambda: g.iota(T.idw[0:16, :], [[16, 128]], 1024, 1))
+    zvv, zuv, zjv = T.zv[:, 15:143:16], T.zu[:, 15:143:16], T.zj[:, :, 15:143:16]
+    sea, seb, sec = T.sel[:, :, 1:7:2], T.sel[:, :, 0:8:7], T.sel[:, :, 2:8:2]
+    for nm, out, src, pat, cmp, base, deps in [
+            ("i16", T.i16[0:16, :], T.ones[0:16, 0:16], [[-1, 16]], ALU.is_equal, 0, ["m_ones"]),
+            ("f16", T.f16[0:16, :], T.ones[0:16, :], [[0, 8], [-1, 16]], ALU.is_equal, 0, ["m_ones"]),
+            ("psl", T.psl[:], T.ones[:], [[-1, 8], [-8, 16]], ALU.is_equal, 0, ["m_ones"]),
+            ("pls", T.pls[:], T.ones[:], [[-1, 16], [-16, 8]], ALU.is_equal, 0, ["m_ones"]),
+            ("z1", T.z1[:, 15:143:16], T.big[:], [[-16, 8]], ALU.is_equal, 0, ["m_big", "m_z1"]),
+            ("zs", T.zs[:, 120:128], T.big[:], [[-16, 8]], ALU.is_equal, 0, ["m_big", "m_zs"]),
+            ("zv0", zvv, T.oneb[:, 0:8], [[-16, 8]], ALU.is_ge, 0, ["m_oneb", "m_zv"]),
+            ("zu0", zuv, T.big[:], [[-16, 8]], ALU.is_ge, -8, ["m_big", "m_zu"]),
+            ("zj0", zjv, T.one4[:], [[-2, 4], [-16, 8]], ALU.is_ge, 0, ["m_one4", "m_zj"]),
+            ("own0", T.own[:, 0:64], T.ones[:, 0:64], [[-16, 8], [0, 8]], ALU.is_ge, 0, ["m_ones"]),
+            ("owo0", T.own[:, 64:128], T.ones[:, 0:64], [[0, 8], [-16, 8]], ALU.is_ge, 0, ["m_ones"]),
+            ("sea0", sea, sea, [[-16, 8], [2, 3]], ALU.is_ge, -4, ["m_sel"]),
+            ("seb0", seb, seb, [[-16, 8], [-2, 2]], ALU.is_ge, -6, ["m_sel"]),
+            ("sel", sec, sec, [[-16, 8], [0, 3]], ALU.is_equal, -10, ["g_sea", "g_seb"])]:
+        op("g_" + nm, "G", lambda a=(out, src, pat, cmp, 0.0, base, 1): g.affine_select(*a), deps)
+    for nm, out, pat, base in [("zv", zvv, [[16, 8]], 15), ("zu", zuv, [[16, 8]], 15), ("zj", zjv, [[2, 4], [16, 8]], 1),
+                               ("own", T.own[:, 0:64], [[16, 8], [0, 8]], 15), ("owo", T.own[:, 64:128], [[0, 8], [16, 8]], 15),
+                               ("sea", sea, [[16, 8], [-2, 3]], 5), ("seb", seb, [[16, 8], [2, 2]], 7)]:
+        op("g_" + nm, "G", lambda a=(out, out, pat, ALU.is_ge, 0.0, base, -1): g.affine_select(*a), ["g_%s0" % nm])
+    mm("p_ee", [(T.pl[:, 0:128], T.f16[0:16, :], T.f16[0:16, :], True, True)], ["g_f16"])
+    op("e_ee", "S", copy("S", T.ee[:], T.pl[:, 0:128]), ["p_ee"])
+    op("io_of", "G", lambda: g.iota(T.oi[:, 0:4], [[0, 4]], 7, 8))
+    op("c_of0", "V", lambda: V.tensor_scalar(T.oi[:, 4:8], T.oi[:, 0:4], 63, None, ALU.bitwise_and), ["io_of"])
+    op("c_of1", "V", copy("V", T.of[:, 0:4], T.oi[:, 4:8]), ["c_of0"])
+    op("io_og", "G", lambda: g.iota(T.oi[:, 8:12], [[16, 4]], 7, 0))
+    op("io_oh", "G", lambda: g.iota(T.oi[:, 12:13], [[0, 1]], 0, 1))
+    op("c_og0", "V", lambda: V.tensor_scalar(T.oi[:, 13:14], T.oi[:, 12:13], 8, None, ALU.bitwise_and), ["io_oh"])
+    op("c_og1", "V", copy("V", T.p8[:], T.oi[:, 13:14]), ["c_og0"])
+    op("c_of2", "V", lambda: V.tensor_scalar(T.of[:, 4:8], T.oi[:, 8:12], T.p8[:], None, ALU.add), ["c_og1", "io_og"])
+    op("c_0", "V", copy("V", T.lab[:, 0:128], T.fi[:, 0:128]), ["ld_0"])
+    op("c_ab", "V", copy("V", T.lab[:, 128:384], T.fi[:, 128:384]), ["ld_ab"])
+    op("c_ct", "V", copy("V", T.lct[:], T.ci[:]), ["ld_ct"])
+    dma("c_c2", [(T.lc2[16 * a:16 * a + 16, :], T.lct[mine, 0:192]) for a in range(8)], ["c_ct"])
+    op("c_o0", "V", copy("V", T.oo[:, :, 0:64], T.fi[:, 0:128]), ["ld_0"])
+    send("L", T.lab, 0, ["c_0", "c_ab"])
+    take("in_L", "L", T.lab2, 0)
+    fills = ["m_tab1", "m_tab2", "m_tab3"]
+    op("c_cdf", "V", copy("V", T.cdf[0:16, :], T.cdi[0:16, :]), ["ld_c16", "io_cd"])
+    mm("p_t", [(T.po0[0:32, 16 * c:16 * c + 16], T.cdf[0:16, c:256:8], T.i16[0:16, :], True, True) for c in range(8)], ["c_cdf", "g_i16"])
+    op("t_hi", "S", copy("S", T.thl[0:32, 0:128], T.po0[0:32, 0:128]), ["p_t"])
+    op("t_lo", "V", lambda: V.tensor_tensor(T.thl[0:32, 128:256], T.po0[0:32, 0:128], T.thl[0:32, 0:128], ALU.subtract), ["t_hi"])
+    dma("dt_c", [(T.dt[h, :], T.thl[0:32, 128 * h:128 * h + 128]) for h in range(2)], ["t_hi", "t_lo"])
+    dma("tab_c", [(T.tab[16 * a:16 * a + 2, :], T.dt[0:2, :]) for a in range(8)], ["dt_c"] + fills)
     dma("dt_in", [(T.dt[2 * j:2 * j + 2, 0:1024], T.dt[0:2, 0:1024]) for j in range(1, 4)], ["dt_c"])
+    for h, (pat, cm) in enumerate([([[16, 8], [0, 16]], 128), ([[0, 8], [1, 16]], 0)]):
+        op("io_n%d" % h, "G", lambda h=h, pat=pat, cm=cm: g.iota(T.idn[0:32, 128 * h:128 * h + 128], pat, 0, cm,
+                                                                 allow_small_or_imprecise_dtypes=True))
+    dma("dt_n", [(T.dt[8 + h, :], T.idn[0:32, 128 * h:128 * h + 128]) for h in range(2)], ["io_n0", "io_n1"])
+    dma("tab_n", [(T.tab[16 * a + 8:16 * a + 10, :], T.dt[8:10, :]) for a in range(8)], ["dt_n"] + fills)
     op("c_sf", "V", copy("V", T.sf[:], T.si[:]), ["ld_si", "ld_id"])
     mm("p_s", [(T.pp[:, 0:48], T.psl[:], T.sf[:], True, True), (power(1, 0, 16), T.psl[:], T.sf[:, 0:16], True, True),
                (power(0, 0, 16), T.psl[:], T.sf[:, 24:40], True, True), (power(0, 24, 8), T.psl[:], T.sf[:, 40:48], True, True)],
-       ["c_sf", "g_psl", "m_pc"], 256)
+       ["c_sf", "g_psl", "m_pc"])
     op("l_s1", "V", copy("V", T.lu[:, 0:48], T.pp[:, 0:48]), ["p_s"])
     for j in range(1, 4):
         c0 = 384 * (j - 1)
-        names = look("g_s%d" % j, T.gch, c0, T.tab[:, :], T.lu, [0, 64, 88][j - 1], 384, ["l_s%d" % j, "tab_c"])
+        names = look("g_s%d" % j, T.gch, c0, T.tab[:, :], T.lu, [0, 64, 88][j - 1], 384, ["l_s%d" % j, "tab_c", "tab_n"])
         pick("x_s%d" % j, power(j + 1, 0, 24), lambda i, c0=c0: T.gch[:, c0 + i:c0 + 384:16], zrow(0), names + ["g_zj"])
         if j < 3:
             op("l_s%d" % (j + 1), "V", copy("V", T.lu[:, 40 + 24 * j:64 + 24 * j], power(j + 1, 0, 24)), ["x_s%d" % j])
         dma("dt_%d" % j, [(T.dt[2 * j + h, 1024 * (l + 1):1024 * (l + 2)], T.gch[h:128:16, c0 + 128 * l:c0 + 128 * l + 128])
                           for h in range(2) for l in range(3)], names)
-    dma("tab_j", [(T.tab[16 * a + 2:16 * a + 8, :], T.dt[2:8, :]) for a in range(8)], ["dt_1", "dt_2", "dt_3", "dt_in"], kb=384)
+    dma("tab_j", [(T.tab[16 * a + 2:16 * a + 8, :], T.dt[2:8, :]) for a in range(8)], ["dt_1", "dt_2", "dt_3", "dt_in"])
 
-    def finish(tag, a, n, p0, deps):
-        op("lf" + tag, "V", copy("V", T.lf[:, 4 * a:4 * (a + n)], T.pc[:, 8 * p0 + 1:8 * (p0 + n):2]), deps, 4 * n)
-        op("eu" + tag, "S", copy("S", T.vl[:, 8 * a:8 * (a + n)], T.pc[:, 8 * p0:8 * (p0 + n)]), ["lf" + tag], 8 * n)
+    def finish(t, a, n, p0, deps):
+        op("lf%d" % t, "V", copy("V", T.lf[:, 4 * a:4 * (a + n)], T.pc[:, 8 * p0 + 1:8 * (p0 + n):2]), deps)
+        op("eu%d" % t, "S", copy("S", T.vl[:, 8 * a:8 * (a + n)], T.pc[:, 8 * p0:8 * (p0 + n)]), ["lf%d" % t])
 
-    def chain(t, a, n, p0, l0, c0, deps, before):
-        names = look("gu" + t, T.gch, c0, T.tab[:, :], T.lu, l0, 16 * n, deps + ["tab_j"])
-        for j in range(4):
-            pick("xu%d" % j + t, power(j + 1, p0, n), lambda i: T.gch[:, c0 + i:c0 + 16 * n:16], zrow(j), names + [before])
-        finish(t, a, n, p0, ["xu%d" % j + t for j in range(4)] + ["pu" + t])
-
-    finish("0", 0, 16, 0, ["x_s3"])
-    for t, e0, e1, l0 in [(1, 2, 5, 40), (2, 5, 8, 112), (3, 8, 9, 136)]:
-        a, p0 = max(e0, 3), 24 * (t % 2)
-        u = T.rs[:, 64 * (a - 3) + 7:64 * (e1 - 3):8]
-        last = ["sc_%d" % (e - 3) for e in range(a, e1)]
-        op("lu%d" % t, "V", copy("V", T.lu[:, l0 + 8 * (a - e0):l0 + 8 * (e1 - e0)], u), last)
-        mm("pu%d" % t, [(power(0, p0 + 8 * (a - e0), 8 * (e1 - a)), T.eye[:], u, True, True)], last + ["g_eye", "eu%d" % (t - 1)], 256)
-        chain("%d" % t, 8 * e0, 8 * (e1 - e0), p0, l0, 896 + 128 * e0, ["lu%d" % t, "l_s1"], "eu%d" % (t - 1))
-    TAG = "001112223"
-    mm("p_d8", [(T.pp[:, 0:64], T.pls[:], T.vl[:, 512:576], True, True)], ["eu3", "g_pls", "l_s1"], 256)
+    finish(0, 0, 16, 0, ["x_s3"])
+    names = look("gu1", T.gch, 1152, T.tab[:, :], T.lu, 40, 128, ["l_s1", "tab_j"])
+    for j in range(4):
+        pick("xu%d1" % j, power(j + 1, 24, 8), lambda i: T.gch[:, 1152 + i:1280:16], zrow(j), names + ["eu0"])
+    finish(1, 16, 8, 24, ["xu%d1" % j for j in range(4)])
+    tag = [0, 0, 1] + [c[0] for c in CHAINS for e in range(c[1], c[2])]
+    for t, e0, e1, l0, p0 in CHAINS:
+        n, c0 = 8 * (e1 - e0), 896 + 128 * e0
+        op("lu%d" % t, "V", copy("V", T.lu[:, l0:l0 + n], T.rs[:, 64 * (e0 - 3) + 7:64 * (e1 - 3):8]), ["sc_%d" % (e - 3) for e in range(e0, e1)])
+        names = look("gu%d" % t, T.gch, c0, T.tab[:, :], T.lu, l0, 16 * n, ["lu%d" % t, "tab_j"])
+        mm("xu%d" % t, [(T.pc[:, 8 * p0 + 64 * s:8 * p0 + 64 * s + 64], T.gch[:, c0 + 128 * s:c0 + 128 * s + 128], T.sel[:], True, True)
+                        for s in range(n // 8)], names + ["eu%d" % (t - 1), "g_sel"])
+        finish(t, 8 * e0, n, p0, ["xu%d" % t])
+    mm("p_d8", [(T.pp[:, 0:64], T.pls[:], T.vl[:, 512:576], True, True)], ["eu%d" % tag[8], "g_pls", "l_s1"])
     op("e_d8", "S", copy("S", T.vl[:, 576:640], T.pp[:, 0:64]), ["p_d8"])
 
-    done, wdone, taps, tables = [], [], [], []
+    done, wdone, taps, tables, counted = [], [], [], [], []
     bank = [[], []]
     seen = [[], [], []]
-    spread = ["e_ee"]
+    spread = "e_ee"
     for e in range(9):
         k, l = divmod(e, 3)
         lo = 1024 * (l + 1)
@@ -325,55 +304,51 @@ def rank_calls(g, core, r, T, topo, issue):
         else:
             need = wdone + ["cp%d" % k]
         for c, (a, b) in enumerate(cuts):
-            n = b - a
             t = T.t0[:, lo + a:lo + b] if k == 0 else T.tb[:, 1024 * (e - 3) + a:1024 * (e - 3) + b]
             lb = lab[:, bcol[l] + a // 16:bcol[l] + b // 16]
             la = lab[:, acol[l] + a // 16:acol[l] + b // 16]
             out = vb[k][:, lo + a:lo + b]
-            gather("B%d_%d" % (e, c), "S", lambda t=t, lb=lb, win=win: S.activation(t, win.indirect(lb), ACT.Identity, bias=255.0, scale=-1.0),
-                   need, n)
-            gather("A%d_%d" % (e, c), "V", lambda t=t, la=la, win=win, out=out: V.tensor_tensor(out, win.indirect(la), t, ALU.min),
-                   need + ["B%d_%d" % (e, c)], n)
+            op("B%d_%d" % (e, c), "S", lambda t=t, lb=lb, win=win: S.activation(t, win.indirect(lb), ACT.Identity, bias=255.0, scale=-1.0), need)
+            op("A%d_%d" % (e, c), "V", lambda t=t, la=la, win=win, out=out: V.tensor_tensor(out, win.indirect(la), t, ALU.min),
+               need + ["B%d_%d" % (e, c)])
             if k > 0:
                 cp, q, name = T.vc[:, 1024 * e + a:1024 * e + b], COPY[e][c], "vc%d_%d" % (e, c)
                 if q == "G":
-                    op(name, q, lambda cp=cp, out=out, n=n: g.affine_select(cp, out, [[0, n]], ALU.is_ge, 0.0, 0, 0), ["A%d_%d" % (e, c)], 2 * n)
+                    op(name, q, lambda cp=cp, out=out, n=b - a: g.affine_select(cp, out, [[0, n]], ALU.is_ge, 0.0, 0, 0), ["A%d_%d" % (e, c)])
                 elif q == "Y":
-                    dma(name, [(cp, out)], ["A%d_%d" % (e, c)], kb=n // 4)
+                    dma(name, [(cp, out)], ["A%d_%d" % (e, c)])
                 else:
-                    op(name, q, copy(q, cp, out), ["A%d_%d" % (e, c)], n if q == "S" else n // 2)
+                    op(name, q, copy(q, cp, out), ["A%d_%d" % (e, c)])
         done = ["A%d_%d" % (e, c) for c in range(len(cuts))]
         if k == 0:
-            dma("vc%d" % e, [(T.vc[:, 1024 * e:1024 * e + 1024], vb[0][:, lo:lo + 1024])], done, kb=256)
-        counted, votes = [], []
+            dma("vc%d" % e, [(T.vc[:, 1024 * e:1024 * e + 1024], vb[0][:, lo:lo + 1024])], done)
+        if l == 0:
+            counted = []
         for c, (a, b) in enumerate(cuts if k else HALVES):
-            dfc = T.df[:, 1024 * e + a:1024 * e + b]
-            gather("vt%d_%d" % (e, c), "V", lambda a=a, b=b, e=e, l=l, k=k, lo=lo, dfc=dfc, lc=lc: V.tensor_tensor(
+            dfc, vote = T.df[:, 1024 * e + a:1024 * e + b], "vt%d_%d" % (e, c)
+            op(vote, "V", lambda a=a, b=b, e=e, l=l, k=k, lo=lo, dfc=dfc, lc=lc: V.tensor_tensor(
                 dfc, vb[k][:, 0:lo + b].indirect(lc[:, 64 * l + a // 16:64 * l + b // 16]), T.vc[:, 1024 * e + a:1024 * e + b], ALU.not_equal),
-                ["vc%d" % e, "c_ct"] if k == 0 else done[:c + 1] + ["vc%d_%d" % (e, c), "c_c2"], b - a)
-            votes.append("vt%d_%d" % (e, c))
+               ["vc%d" % e, "c_ct"] if k == 0 else done[:c + 1] + ["vc%d_%d" % (e, c), "c_c2"])
+            seen[k].append(vote)
             if e in WIDE:
                 pv = [T.pv0, T.pv1][c % 2][:, 0:b - a]
-                mm("pv%d_%d" % (e, c), [(pv, T.oneb[:], dfc, True, True)], ["vt%d_%d" % (e, c), "m_oneb"] + bank[c % 2], b - a)
-                op("ev%d_%d" % (e, c), "S", copy("S", fl[k][:, lo + a:lo + b], pv), ["pv%d_%d" % (e, c)] + tables, b - a)
+                mm("pv%d_%d" % (e, c), [(pv, T.oneb[:], dfc, True, True)], [vote, "m_oneb"] + bank[c % 2])
+                op("ev%d_%d" % (e, c), "S", copy("S", fl[k][:, lo + a:lo + b], pv), ["pv%d_%d" % (e, c)] + tables)
                 bank[c % 2] = ["ev%d_%d" % (e, c)]
-                counted += bank[c % 2]
+                counted = counted + bank[c % 2]
             else:
                 pv = [T.pv0, T.pv1][e % 2][:, 0:64]
                 z = slide(T.zv if k == 0 else T.zo)
                 mm("pv%d_%d" % (e, c), [(pv, z(i), T.df[:, 1024 * e + 64 * i:1024 * e + 64 * i + 64], i == 0, i == 15)
-                                        for i in range(a // 64, b // 64)],
-                   ["vt%d_%d" % (e, c), "g_zv" if k == 0 else "m_zo"] + (["~pv%d_%d" % (e, c - 1)] if c else bank[e % 2]))
-        seen[k] = seen[k] + votes
+                                        for i in range(a // 64, b // 64)], [vote, "g_zv" if k == 0 else "m_zo"] + ([] if c else bank[e % 2]))
         if e not in WIDE:
             xv = T.xv[:, 64 * e:64 * e + 64]
-            op("ev%d" % e, "S", copy("S", xv, pv), ["pv" + votes[-1][2:]])
+            op("ev%d" % e, "S", copy("S", xv, pv), ["pv%d_1" % e])
             bank[e % 2] = ["ev%d" % e]
-            counted = ["F%d" % e]
+            counted = counted + ["F%d" % e]
             if k == 0:
-                send("V%d" % e, [xv, xv], ["ev%d" % e], 100)
-                dma("F%d" % e, [(fl[0][16 * a + 8:16 * a + 16, lo:lo + 1024], T.kv[8 * e:8 * e + 8, mine, :]) for a in range(8)],
-                    ["aV%d" % e] + done, kb=128)
+                send("V%d" % e, T.xv, 64 * e, ["ev%d" % e])
+                dma("F%d" % e, [(fl[0][16 * a + 8:16 * a + 16, lo:lo + 1024], T["kV%d" % e][:, mine, :]) for a in range(8)], ["aV%d" % e] + done)
             else:
                 dma("F%d" % e, [(fl[k][0:128:16, lo:lo + 1024], xv)], ["ev%d" % e] + (seen[0] if k == 1 else tables))
         if k > 0 and l < 2:
@@ -382,99 +357,91 @@ def rank_calls(g, core, r, T, topo, issue):
                 wdone += look("w%d_%d" % (e, c), wb[k], lo + a, vb[k][:, 0:lo + b], T.lr, 64 * (e - 3) + a // 16, b - a,
                               done[:c + 1] + ["el%d" % (e - 3)])
         if e == 2:
-            for c in range(4):
+            for c, (a, b) in enumerate(QUARTERS):
                 q = "VS"[c % 2]
-                gather("tap1_%d" % c, q, copy(q, T.tx[:, 256 * c:256 * c + 256], vb[0][:, :].indirect(T.lct[:, 192 + 16 * c:208 + 16 * c])),
-                       done + ["c_ct"], 256)
+                op("tap1_%d" % c, q, copy(q, T.tx[:, a:b], vb[0][:, :].indirect(T.lct[:, 192 + a // 16:192 + b // 16])), done + ["c_ct"])
+                seen[0].append("tap1_%d" % c)
             for h in range(2):
-                send("X%d" % h, [T.tx[:, 256 * c:256 * c + 256] for c in (2 * h, 2 * h + 1)], ["tap1_%d" % c for c in (2 * h, 2 * h + 1)], 128)
-                defs["aX%d" % h]["deps"].append("~aL")
-                dma("in_X%d" % h, [(T.vb1[:, 256 * c:256 * c + 256], T.kq[8 * c:8 * c + 8]) for c in (2 * h, 2 * h + 1)], ["aX%d" % h], kb=128)
+                send("X%d" % h, T.tx, 512 * h, ["tap1_%d" % c for c in (2 * h, 2 * h + 1)])
+                take("in_X%d" % h, "X%d" % h, T.vb1, 512 * h)
             taps = ["in_X0", "in_X1"]
-            dma("cp1", [(T.wb1[:, 0:1024], T.vb1[:, 0:1024])], taps, kb=200)
-            seen[0] = seen[0] + ["tap1_%d" % c for c in range(4)]
         if e == 5:
             taps = look("tap2", T.vb2, 0, vb[1][:, :], T.lr, 128, 1024, done + ["el2"])
-            dma("cp2", [(T.wb2[:, 0:1024], T.vb2[:, 0:1024])], taps, kb=200)
             dma("id_R", [(T.vb1[16 * a:16 * a + 2, 0:1024], T.dt[0:2, 0:1024]) for a in range(8)], seen[1] + taps + ["dt_c"])
+        if e in (2, 5):
+            dma("cp%d" % (k + 1), [(wb[k + 1][:, 0:1024], vb[k + 1][:, 0:1024])], taps)
         if k == 2:
-            ways = [("Y%d" % l, lo, 512, done)] if l < 2 else [("Y20", lo, 256, done[:1]), ("Y21", lo + 512, 256, done)]
-            for m, c0, w, deps in ([("Yi", 0, 512, taps)] if l == 0 else []) + ways:
-                send(m, [T.vb2[:, c0 + w * j:c0 + w * (j + 1)] for j in range(2)], deps, w // 2)
-                dma("o_" + m, [(T.yv[:, c0 + w * j:c0 + w * (j + 1)], T["k" + MSG[m][1]][8 * p[1]:8 * p[1] + 8])
-                               for j, p in enumerate(MSG[m][2])], ["a" + m], kb=w // 2)
+            ways = [("Y%d" % l, lo, done)] if l < 2 else [("Y20", lo, done[:1]), ("Y21", lo + 512, done)]
+            for m, c0, deps in ([("Yi", 0, taps)] if l == 0 else []) + ways:
+                send(m, T.vb2, c0, deps)
+                take("o_" + m, m, T.yv, c0)
         looked = look("w1_%d" % e, T.gf, 512 * e, fl[k][:, 0:lo + 1024], T.lf, 32 * e, 512,
-                      counted + ["lf" + TAG[e]] + (["m_t0"] if e == 0 else []) + (before if l else []))
-        before = counted + (before if l else [])
+                      counted + ["lf%d" % tag[e]] + (["m_t0"] if e == 0 else []))
         if k == 0:
             tables = tables + looked
         pick("w2_%d" % e, T.pf[:, 1:64:2], lambda i, e=e: T.gf[:, 512 * e + i:512 * e + 512:16],
              slide(T.zu if k == 0 else T.z1) if e < 8 else lambda i: T.zs[:, 120 - 8 * i:248 - 8 * i],
              looked + ["g_zu" if k == 0 else "g_z1" if e < 8 else "g_zs", "m_pf"] + (["sc_%d" % (e - 1)] if e else []))
-        nodes = T.vl[:, 64 * e:64 * e + 64] if e < 8 else T.vl[:, 576:640]
-        op("sc_%d" % e, "V", lambda e=e, nodes=nodes: V.tensor_tensor_scan(T.rs[:, 64 * e:64 * e + 64], T.pf[:, 0:64], nodes,
-                                                                          0.0, ALU.max, ALU.min),
-           ["w2_%d" % e, "eu" + TAG[e] if e < 8 else "e_d8"])
+        nodes, rs = T.vl[:, 64 * e:64 * e + 64] if e < 8 else T.vl[:, 576:640], T.rs[:, 64 * e:64 * e + 64]
+        op("sc_%d" % e, "V", lambda rs=rs, nodes=nodes: V.tensor_tensor_scan(rs, T.pf[:, 0:64], nodes, 0.0, ALU.max, ALU.min),
+           ["w2_%d" % e, "eu%d" % tag[e] if e < 8 else "e_d8"])
         if e == 8:
-            op("w5", "V", copy("V", T.rf[:], T.rs[:, 64 * e + 7:64 * e + 64:8]), ["sc_8"])
-            send("T", [T.rf[:]], ["w5"], 0)
-            dma("o_t", [(T.yt[:], T.kt[:])], ["aT"])
+            op("w5", "V", copy("V", T.rf[:], rs[:, 7:64:8]), ["sc_8"])
+            send("T", T.rf, 0, ["w5"])
+            dma("o_t", [(T.yt[:], T.kT[:])], ["aT"])
         elif e != 5:
-            j = e - (e > 5)
-            mk = T.mk[:, 64 * j:64 * j + 64]
-            gather("mk%d" % e, "V", lambda e=e, mk=mk: V.tensor_tensor(mk, T.rs[:, 64 * e:64 * e + 64].indirect(T.of[:]), T.own[:], ALU.mult),
-                   ["sc_%d" % e, "c_of", "g_own"], 64)
+            mk = T.mk[:, 64 * e:64 * e + 64]
+            op("mk%d" % e, "V", lambda rs=rs, mk=mk, j=k % 2: V.tensor_tensor(mk, rs.indirect(T.of[:, 4 * j:4 * j + 4]),
+                                                                             T.own[:, 64 * j:64 * j + 64], ALU.mult),
+               ["sc_%d" % e] + [["c_of1", "g_own"], ["c_of2", "g_owo"]][k % 2])
             if e < 5:
-                mm("pl%d" % e, [(T.pl[:, 0:64], T.ee[:], mk, True, True)], ["mk%d" % e] + spread, 256)
+                mm("pl%d" % e, [(T.pl[:, 0:64], T.ee[:], mk, True, True)], ["mk%d" % e, spread])
                 op("el%d" % e, "V", copy("V", T.lr[:, 64 * e:64 * e + 64], T.pl[:, 0:64]), ["pl%d" % e])
-                spread = ["el%d" % e]
+                spread = "el%d" % e
             else:
                 rh = T.rh[:, 16 * l:16 * l + 16]
-                mm("pl%d" % e, [(T.pl[64 * h:64 * h + 64, 0:16], mk, T.ee[:, 0:16], True, True) for h in range(2)], ["mk%d" % e] + spread, 256)
+                mm("pl%d" % e, [(T.pl[64 * h:64 * h + 64, 0:16], mk, T.ee[:, 0:16], True, True) for h in range(2)], ["mk%d" % e, spread])
                 op("hi%d" % e, "V", copy("V", rh, T.pl[:, 0:16]), ["pl%d" % e])
                 op("lo%d" % e, "V", lambda rh=rh: V.tensor_tensor(rh[64:128, :], T.pl[64:128, 0:16], rh[64:128, :], ALU.subtract), ["hi%d" % e])
-                spread = ["lo%d" % e]
-                send("R%d" % e, [rh], ["lo%d" % e], 0)
-                dma("in_R%d" % e, [(T.vb1[h:128:16, lo:lo + 1024], T.kr[8 * l:8 * l + 8, 64 * h:64 * h + 64, :]) for h in range(2)],
+                spread = "lo%d" % e
+                send("R%d" % e, T.rh, 16 * l, [spread])
+                dma("in_R%d" % e, [(T.vb1[h:128:16, lo:lo + 1024], T["kR%d" % e][:, 64 * h:64 * h + 64, :]) for h in range(2)],
                     ["aR%d" % e, "id_R"])
-    for l in (1, 2):
-        po = [T.po0, T.po1][l - 1]
-        for j, (nm, col) in enumerate([("fa%d" % l, acol[l]), ("fb%d" % l, bcol[l])]):
-            c0 = 2048 * (l - 1) + 1024 * j
-            names = look(nm, T.gfin, c0, T.vb1[:, 0:1024 * (l + 1)], T.lab, col, 1024, ["in_R6"] + (["in_R7"] if l == 2 else []))
-            pick("x" + nm, po[:, 64 * j:64 * j + 64], lambda i, c0=c0: T.gfin[:, c0 + i:c0 + 1024:16], zrow(0), names + ["t_lo"])
-        op("ef%d" % l, "S", copy("S", T.oo[:, 128 * l:128 * l + 128], po[:, 0:128]), ["xfa%d" % l, "xfb%d" % l], 128)
-        dma("o_l%d" % l, [(T.ya[:, 64 * l:64 * l + 64], T.oo[:, 128 * l:128 * l + 64]),
-                          (T.yb[:, 64 * l:64 * l + 64], T.oo[:, 128 * l + 64:128 * l + 128])], ["ef%d" % l], q="S")
+    for j, (nm, q, col, y) in enumerate([("fb", "V", bcol, T.yb), ("fa", "S", acol, T.ya)]):
+        po = [T.po0, T.po1][j]
+        for l in (1, 2):
+            c0 = 2048 * j + 1024 * (l - 1)
+            names = look(nm + "%d" % l, T.gfin, c0, T.vb1[:, 0:1024 * (l + 1)], T.lab, col[l], 1024, ["in_R6", "in_R7"][:l])
+            pick("x%s%d" % (nm, l), po[:, 64 * l:64 * l + 64], lambda i, c0=c0: T.gfin[:, c0 + i:c0 + 1024:16], zrow(0), names + ["t_lo"])
+        op("e" + nm, q, copy(q, T.oo[:, j, 64:192], po[:, 64:192]), ["x%s1" % nm, "x%s2" % nm])
+        dma("o_" + nm, [(y[:], T.oo[:, j, :])], ["e" + nm, "c_o0"], q="Y" if q == "V" else q)
+    return defs
 
-    if "order" not in PLAN:
-        PLAN["order"] = plan(defs)
-        PLAN["sends"] = [n[1:] for n in PLAN["order"]["G"] if defs[n]["kind"] == "rem"]
-    if not issue:
-        return
-    queue = {"V": V, "S": S, "P": PE, "G": g, "Y": SY}
-    order = {q: PLAN["order"][q] for q in queue}
-    wanted = set(d for v in defs.values() if v["kind"] != "ext" for d in v["deps"] if d[0] != "~")
-    token, nd, left = {}, 0, 0
-    for name in PLAN["order"]["X"]:
-        token[name] = (name,) + defs[name]["what"]
+
+def issue(g, defs, T, engines):
+    queue = {"V": g.vector, "S": g.scalar, "P": g.tensor, "G": g, "Y": g.sync}
+    order = {q: ORDER[q].split() for q in queue}
+    assert sorted(n for q in order for n in order[q]) == sorted(n for n, v in defs.items() if v[0] != "ext")
+    wanted = set(d for v in defs.values() for d in v[3])
+    token = {n: (n,) + v[2] for n, v in defs.items() if v[0] == "ext"}
+    nd, left = 0, 0
     for q, names in order.items():
         cnt = 0
         for name in names:
-            kind = defs[name]["kind"]
+            kind = defs[name][0]
             if kind == "op" and name in wanted:
                 cnt += 1
                 token[name] = ("q" + q, T.sem["q" + q], cnt)
             elif kind == "dma":
-                token[name] = ("m%d" % nd, T.sem["m%d" % nd], 16 * len(defs[name]["what"]))
+                token[name] = ("m%d" % nd, T.sem["m%d" % nd], 16 * len(defs[name][2]))
                 nd += 1
     waited = {}
     for q, names in order.items():
         seen = {}
         for name in names:
-            kind, what = defs[name]["kind"], defs[name]["what"]
+            kind, _, what, deps = defs[name]
             most = {}
-            for d in [d for d in defs[name]["deps"] if d[0] != "~"]:
+            for d in deps:
                 key, sem, val = token[d]
                 if val > most.get(key, (None, 0))[1]:
                     most[key] = (sem, val)
@@ -492,7 +459,7 @@ def rank_calls(g, core, r, T, topo, issue):
                     queue[q].dma_start(out, src).then_inc(token[name][1], 16)
             else:
                 g.remote_dma_fused(what, local_sem=T.sem.left)
-                left += len(eng)
+                left += engines
     g.wait_ge(T.sem.left, left)
     for name, (key, sem, val) in token.items():
         if val > waited.get(key, 0):

from concourse.bass import DstId, RemoteDMATransfer
from concourse.mybir import AluOpType as ALU, ActivationFunctionType as ACT

B16, F32, I32, U16 = "bfloat16", "float32", "int32", "uint16"
SCRATCH = {n: ("sbuf", [128] + list(s), d) for n, s, d in [
    ("vb0", [4096], B16), ("vb1", [4096], B16), ("vb2", [4096], B16), ("wb1", [3072], B16), ("wb2", [3072], B16),
    ("t0", [4096], B16), ("tb", [6144], B16), ("df", [9216], B16), ("vc", [9216], B16), ("tab", [4096], B16), ("tx", [1024], B16),
    ("gf", [9 * 512], B16), ("gch", [2048], B16), ("gfin", [4096], B16), ("fi", [384], I32), ("ci", [256], I32),
    ("lab", [384], U16), ("lab2", [384], U16), ("lct", [256], U16), ("lc2", [192], U16), ("lr", [5 * 64], U16),
    ("cdi", [256], I32), ("cdf", [256], F32), ("idw", [128], I32), ("thl", [256], B16), ("si", [48], I32), ("sf", [48], F32),
    ("ones", [128], F32), ("oneb", [128], B16), ("one4", [4, 8], B16), ("zv", [144], B16), ("zu", [144], B16), ("zo", [144], B16),
    ("z1", [144], B16), ("zj", [4, 144], B16), ("zs", [256], B16), ("i16", [16], F32), ("f16", [128], F32), ("ee", [128], F32),
    ("own", [128], F32), ("pls", [128], F32), ("psl", [128], F32), ("oi", [16], I32), ("of", [8], U16), ("sel", [8, 8], B16),
    ("idn", [256], B16), ("p8", [1], F32), ("big", [8], B16), ("vl", [80 * 8], F32), ("lf", [72 * 4], U16), ("rs", [72 * 8], F32),
    ("lu", [160], U16), ("xv", [9 * 64], B16), ("mk", [8 * 64], F32), ("rh", [32], B16), ("rf", [8], F32), ("oo", [2, 192], F32)]}
SCRATCH["dt"] = ("dram", [10, 4096], B16)
SCRATCH.update({n: ("psum", [128, 512], F32) for n in ("pv0", "pv1", "pp", "po0", "po1", "pl", "pf", "pc")})
MSG = {"L": (True, U16, 384, [0, 1, 2, 3]), "X0": (True, B16, 512, [0, 2]), "X1": (True, B16, 512, [1, 3]),
       "Yi": (True, B16, 1024, [0]), "Y0": (True, B16, 1024, [2]), "Y1": (True, B16, 1024, [0]),
       "Y20": (True, B16, 512, [2]), "Y21": (True, B16, 512, [0, 3]),
       "V0": (False, B16, 64, [1, 3]), "V1": (False, B16, 64, [1, 3]), "V2": (False, B16, 64, [1, 3]),
       "R6": (False, B16, 16, [1]), "R7": (False, B16, 16, [1]), "T": (False, F32, 8, [1])}


def buffers():
    for m, (dealt, dtype, columns, by) in MSG.items():
        parts = len(by) if dealt else 1
        SCRATCH["h" + m] = ("dram", [parts, 128, columns // parts], dtype)
        SCRATCH["k" + m] = ("dram", [8 * parts, 128, columns // parts // (8 if dealt else 1)], dtype)


buffers()
SEMAPHORES = ["qV", "qS", "qP", "qG", "left"] + ["a" + m for m in MSG] + ["m%d" % i for i in range(60)]
AT = [7, 5, 3, 1, 0]
BIG = 4096.0
HALVES, QUARTERS = [(0, 512), (512, 1024)], [(0, 256), (256, 512), (512, 768), (768, 1024)]
CUTS = [QUARTERS] * 3 + [HALVES] * 5 + [[(0, 512), (512, 768), (768, 1024)]]
COPY = [""] * 3 + ["GG"] * 5 + ["GYS"]
WIDE = (8,)
SHARE = {"w1_8": 2, "tap2": 2, "fb1": 1, "fb2": 1}
CHAINS = [(2, 3, 5, 48, 32), (3, 5, 8, 112, 0), (4, 8, 9, 136, 24)]

ORDER = {
    "V": "m_tab0 m_tab2 m_oneb m_ones m_tab1 m_one4 c_0 c_ab A0_1 A0_2 A0_0 A0_3 c_cdf c_sf A1_1 A1_2 A1_0 A1_3 t_lo l_s1 c_ct "
         "A2_3 A2_1 A2_2 A2_0 tap1_0 tap1_2 vt0_0 vt0_1 vt1_1 vt1_0 l_s2 vt2_0 vt2_1 c_of0 c_of1 c_o0 l_s3 lf0 "
         "A3_0 c_og0 c_og1 c_of2 sc_0 mk0 el0 A3_1 sc_1 mk1 lu2 vt3_0 el1 vt3_1 A4_0 A4_1 lf1 vt4_0 lf2 vt4_1 sc_2 mk2 "
         "A5_0 el2 A5_1 tap2V sc_3 mk3 vt5_0 el3 A6_0 vt5_1 sc_4 lu3 A6_1 mk4 vt6_0 lf3 el4 vt6_1 A7_0 A7_1 vt7_0 vt7_1 sc_5 lu4 "
         "A8_0 sc_6 mk6 A8_1 lf4 hi6 lo6 vt8_0 sc_7 mk7 A8_2 hi7 lo7 vt8_1 vt8_2 w1_8V sc_8 w5 fb1V fb2V efb",
    "S": "ld_0 m_tab3 m_pc m_pf0 m_pf B0_1 B0_2 B0_0 B0_3 B1_1 B1_2 B1_0 B1_3 t_hi B2_3 B2_1 B2_2 B2_0 tap1_1 tap1_3 "
         "g_s1S ev0 g_s2S ev1 e_ee g_s3S ev2 B3_0 w1_0S eu0 B3_1 w1_1S w3_0S gu1S w3_1S B4_0 B4_1 gu2S w4_0S w4_1S eu1 w1_2S ev3 "
         "B5_0 B5_1 w1_3S ev4 eu2 tap2S B6_0 w1_4S B6_1 w6_0S ev5 gu3S w6_1S B7_0 eu3 B7_1 ev6 w7_0S w1_5S w7_1S w1_6S "
         "B8_0 ev7 B8_1 B8_2 gu4S w1_7S eu4 e_d8 vc8_2 ev8_0 ev8_1 ev8_2 w1_8S fa1S fa2S efa o_fa",
    "P": "p_t p_s pv0_0 pv0_1 x_s1 pv1_0 pv1_1 p_ee x_s2 pv2_0 pv2_1 x_s3 w2_0 pl0 w2_1 pl1 xu31 xu11 xu21 xu01 pv3_0 pv3_1 xu2 w2_2 "
         "pv4_0 pl2 pv4_1 w2_3 pl3 pv5_0 w2_4 pv5_1 xu3 pl4 pv6_0 pv6_1 w2_5 pv7_0 pv7_1 w2_6 xu4 pl6 w2_7 p_d8 pl7 "
         "pv8_0 pv8_1 pv8_2 w2_8 xfa1 xfb1 xfa2 xfb2",
    "G": "io_n0 io_cd io_n1 m_zv io_id g_zv0 g_i16 g_psl sL m_t0 m_zj sX0 sX1 g_zv g_zj0 g_zj g_f16 m_big sV0 io_of m_zu g_zu0 g_zu sV1 "
         "g_own0 m_zo0 g_own m_zo m_sel io_og sV2 g_seb0 g_seb g_sea0 g_sea g_sel io_oh vc3_0 g_owo0 g_owo m_z1 g_z1 vc3_1 m_zs g_pls g_zs "
         "vc4_0 vc4_1 vc5_0 vc5_1 sYi vc6_0 vc6_1 sY0 vc7_0 vc7_1 sY1 vc8_0 sR6 sY20 sY21 sR7 sT",
    "Y": "ld_x ld_ab ld_c16 dt_n ld_id ld_si ld_ct tab_n vc0 dt_c vc1 tab_c vc2 dt_in c_c2 dt_1 in_L in_X0 in_X1 F0 dt_2 dt_3 F1 tab_j "
         "cp1 F2 F3 F4 cp2 id_R F5 F6 o_Yi F7 vc8_1 o_Y0 in_R6 o_Y1 in_R7 o_Y20 o_Y21 o_t o_fb",
}


def relays(rank_core, T, topo):
    ok = [c for c in topo.cores_of(rank_core) if c != rank_core and all(topo.may_write(c, d) for d in T.cores)]
    near = [c for c in ok if topo.die(c) == topo.die(rank_core)]
    far = [c for c in ok if topo.die(c) != topo.die(rank_core)]
    return near[:2] + far[:2]


def bits(engines):
    return sum(1 << e for e in engines)


def dst_id(d, src, topo):
    rid, pid = topo.addr(d, src)
    return DstId(rid=rid, pnc=pid)


def deal(core, dests, each, topo):
    masks = {}
    used = []
    for d in sorted(dests, key=lambda c: len(topo.engines(core, c))):
        e = [x for x in topo.engines(core, d) if x not in used][:each]
        used += e
        masks[d] = bits(e)
    return masks


def hand_on(g, core, s, h, T, topo):
    n = len(T.cores)
    engines = len(topo.engines(T.cores[s], core))
    mine = [c[1:] for c in ORDER["G"].split() if c[0] == "s" and h in MSG[c[1:]][3]]
    for j, m in enumerate(mine):
        dealt, by = MSG[m][0], MSG[m][3]
        sem, slot, each = T.sem["a" + m], by.index(h) if dealt else 0, 1 if dealt else len(by)
        dests = [d for d in range(n) if (d - s) % each == by.index(h) % each]
        masks = deal(core, [T.cores[d] for d in dests], each, topo)
        if dealt:
            g.sync.wait_ge(sem, engines // len(by))
            g.sync.dma_start(T["k" + m][n * slot:n * slot + n], T["h" + m][slot]).then_inc(T.sem["m%d" % j], 16)
            g.wait_ge(T.sem["m%d" % j], 16)
        else:
            g.wait_ge(sem, engines // len(by))
        g.remote_dma_fused([RemoteDMATransfer(dst_ids=[dst_id(T.cores[d], core, topo)], dma_engine_mask=masks[T.cores[d]], remote_sem=sem,
                                              src=T["k" + m][n * slot + d] if dealt else T["h" + m][slot], dst=T["k" + m][n * slot + s])
                            for d in dests], local_sem=T.sem.left)
    g.wait_ge(T.sem.left, n * len(mine))


def rank_program(g, core, T, topo):
    r = T.rank_of(core)
    if r is not None:
        issue(g, rank_calls(g, core, r, T, topo), T, len(topo.engines(core, relays(core, T, topo)[0])))
        return
    for s, c in enumerate(T.cores):
        if core in topo.cores_of(c) and core in relays(c, T, topo):
            hand_on(g, core, s, relays(c, T, topo).index(core), T, topo)


def rank_calls(g, core, r, T, topo):
    V, S, PE = g.vector, g.scalar, g.tensor
    hands = relays(core, T, topo)
    eng = topo.engines(core, hands[0])
    defs = {}
    vb = [T.vb0, T.vb1, T.vb2]
    wb = [T.vb0, T.wb1, T.wb2]
    fl = [T.t0, T.vb0, T.t0]

    def op(name, q, fn, deps=()):
        defs[name] = ("op", q, fn, list(deps))

    def dma(name, pairs, deps=(), q="Y"):
        defs[name] = ("dma", q, pairs, list(deps))

    def mm(name, parts, deps):
        def fn():
            ins = None
            for out, lhs, rhs, st, sp in parts:
                ins = PE.matmul(out, lhs, rhs, st, sp)
            return ins
        op(name, "P", fn, deps)

    def pick(name, out, rhs_of, lhs_of, deps):
        mm(name, [(out, lhs_of(i), rhs_of(i), i == 0, i == 15) for i in range(16)], deps)

    def slide(z):
        return lambda i: z[:, 15 - i:143 - i]

    def zrow(j):
        return lambda i: T.zj[:, j, 15 - i:143 - i]

    def power(j, p0, n):
        return T.pc[:, 8 * p0 + AT[j]:8 * (p0 + n):8]

    def copy(q, out, src):
        if q == "S":
            return lambda: S.activation(out, src, ACT.Copy)
        return lambda: V.tensor_copy(out, src)

    def look(name, out, c0, win, lst, l0, n, deps):
        parts = {0: [("S", 0, n)], 1: [("V", 0, n)], 2: [("S", 0, n // 2), ("V", n // 2, n)]}[SHARE.get(name, 0)]
        for q, a, b in parts:
            op(name + q, q, copy(q, out[:, c0 + a:c0 + b], win.indirect(lst[:, l0 + a // 16:l0 + b // 16])), deps)
        return [name + q for q, a, b in parts]

    def send(m, tile, c0, deps):
        dealt, dtype, columns, by = MSG[m]
        each, w = len(eng) // len(by), columns // len(by) if dealt else columns
        defs["s" + m] = ("rem", "G", [RemoteDMATransfer(
            dst_ids=[dst_id(hands[h], core, topo)], dma_engine_mask=bits(eng[each * j:each * j + each]), remote_sem=T.sem["a" + m],
            src=tile[:, c0 + w * j * dealt:c0 + w * (j * dealt + 1)], dst=T["h" + m][j * dealt]) for j, h in enumerate(by)], deps)
        defs["a" + m] = ("ext", None, (T.sem["a" + m], 8 * len(by)), [])

    def take(name, m, tile, c0):
        columns, by = MSG[m][2:]
        w = columns // len(by)
        dma(name, [(tile[:, c0 + w * j:c0 + w * (j + 1)], T["k" + m][8 * j:8 * j + 8]) for j in range(len(by))], ["a" + m])

    mine = slice(16 * r, 16 * r + 16)
    acol, bcol = [64, 128, 192], [0, 256, 320]
    dma("ld_0", [(T.fi[:, 0:64], T.fb[:, 0:64]), (T.fi[:, 64:128], T.fa[:, 0:64])], q="S")
    dma("ld_x", [(T.vb0[:, 0:1024], T.x[:])])
    dma("ld_ab", [(T.fi[:, 128:256], T.fa[:, 64:192]), (T.fi[:, 256:384], T.fb[:, 64:192])])
    dma("ld_ct", [(T.ci[:, 0:192], T.cd[:]), (T.ci[:, 192:256], T.tp[:])])
    dma("ld_c16", [(T.cdi[0:16, 64:256], T.cd[mine, :])])
    dma("ld_si", [(T.si[:, 8 * l:8 * l + 8], T.cd[mine, 64 * l:64 * l + 64]) for l in range(3)] + [(T.si[:, 40:48], T.tp[mine, :])])
    dma("ld_id", [(T.si[:, 24 + 8 * l:32 + 8 * l], T.idw[0:16, 64 * l:64 * l + 64]) for l in range(2)], ["io_id"])
    for nm, ap, val in [("ones", T.ones[:], 1.0), ("oneb", T.oneb[:], 1.0), ("one4", T.one4[:], 1.0)] + [
            ("tab%d" % j, T.tab[:, 1024 * j:1024 * j + 1024], BIG) for j in range(3)]:
        op("m_" + nm, "V", lambda ap=ap, val=val: V.memset(ap, val))
    op("m_tab3", "S", copy("S", T.tab[:, 3072:4096], T.tab[:, 0:1024]), ["m_tab0"])
    for nm, ap, val, n in [("pc", T.pc[:, 0:256:2], BIG, 128), ("pf0", T.pf[:, 0:64:2], 0.0, 32), ("pf", T.pf[:, 0:64:8], BIG, 8)]:
        op("m_" + nm, "S", lambda ap=ap, val=val, n=n: S.activation(ap, T.oneb[:, 0:n], ACT.Identity, scale=val),
           ["m_oneb"] + (["m_pf0"] if nm == "pf" else []))
    for nm, ap, val, n in [("zj", T.zj[:], 0, 576), ("zv", T.zv[:], 0, 144), ("zu", T.zu[:], 0, 144), ("zo0", T.zo[:], 0, 144),
                           ("z1", T.z1[:], 0, 144), ("zs", T.zs[:], 0, 256), ("t0", T.t0[:, 0:1024], 0, 1024), ("big", T.big[:], int(BIG), 8),
                           ("sel", T.sel[:], 1, 64), ("zo", T.zo[:, 15:143:16], 1, 8)]:
        op("m_" + nm, "G", lambda ap=ap, val=val, n=n: g.iota(ap, [[0, n]], val, 0, allow_small_or_imprecise_dtypes=True),
           ["m_zo0"] if nm == "zo" else [])
    op("io_cd", "G", lambda: g.iota(T.cdi[0:16, 0:64], [[16, 64]], 0, 1))
    op("io_id", "G", lambda: g.iota(T.idw[0:16, :], [[16, 128]], 1024, 1))
    zvv, zuv, zjv = T.zv[:, 15:143:16], T.zu[:, 15:143:16], T.zj[:, :, 15:143:16]
    sea, seb, sec = T.sel[:, :, 1:7:2], T.sel[:, :, 0:8:7], T.sel[:, :, 2:8:2]
    for nm, out, src, pat, cmp, base, deps in [
            ("i16", T.i16[0:16, :], T.ones[0:16, 0:16], [[-1, 16]], ALU.is_equal, 0, ["m_ones"]),
            ("f16", T.f16[0:16, :], T.ones[0:16, :], [[0, 8], [-1, 16]], ALU.is_equal, 0, ["m_ones"]),
            ("psl", T.psl[:], T.ones[:], [[-1, 8], [-8, 16]], ALU.is_equal, 0, ["m_ones"]),
            ("pls", T.pls[:], T.ones[:], [[-1, 16], [-16, 8]], ALU.is_equal, 0, ["m_ones"]),
            ("z1", T.z1[:, 15:143:16], T.big[:], [[-16, 8]], ALU.is_equal, 0, ["m_big", "m_z1"]),
            ("zs", T.zs[:, 120:128], T.big[:], [[-16, 8]], ALU.is_equal, 0, ["m_big", "m_zs"]),
            ("zv0", zvv, T.oneb[:, 0:8], [[-16, 8]], ALU.is_ge, 0, ["m_oneb", "m_zv"]),
            ("zu0", zuv, T.big[:], [[-16, 8]], ALU.is_ge, -8, ["m_big", "m_zu"]),
            ("zj0", zjv, T.one4[:], [[-2, 4], [-16, 8]], ALU.is_ge, 0, ["m_one4", "m_zj"]),
            ("own0", T.own[:, 0:64], T.ones[:, 0:64], [[-16, 8], [0, 8]], ALU.is_ge, 0, ["m_ones"]),
            ("owo0", T.own[:, 64:128], T.ones[:, 0:64], [[0, 8], [-16, 8]], ALU.is_ge, 0, ["m_ones"]),
            ("sea0", sea, sea, [[-16, 8], [2, 3]], ALU.is_ge, -4, ["m_sel"]),
            ("seb0", seb, seb, [[-16, 8], [-2, 2]], ALU.is_ge, -6, ["m_sel"]),
            ("sel", sec, sec, [[-16, 8], [0, 3]], ALU.is_equal, -10, ["g_sea", "g_seb"])]:
        op("g_" + nm, "G", lambda a=(out, src, pat, cmp, 0.0, base, 1): g.affine_select(*a), deps)
    for nm, out, pat, base in [("zv", zvv, [[16, 8]], 15), ("zu", zuv, [[16, 8]], 15), ("zj", zjv, [[2, 4], [16, 8]], 1),
                               ("own", T.own[:, 0:64], [[16, 8], [0, 8]], 15), ("owo", T.own[:, 64:128], [[0, 8], [16, 8]], 15),
                               ("sea", sea, [[16, 8], [-2, 3]], 5), ("seb", seb, [[16, 8], [2, 2]], 7)]:
        op("g_" + nm, "G", lambda a=(out, out, pat, ALU.is_ge, 0.0, base, -1): g.affine_select(*a), ["g_%s0" % nm])
    mm("p_ee", [(T.pl[:, 0:128], T.f16[0:16, :], T.f16[0:16, :], True, True)], ["g_f16"])
    op("e_ee", "S", copy("S", T.ee[:], T.pl[:, 0:128]), ["p_ee"])
    op("io_of", "G", lambda: g.iota(T.oi[:, 0:4], [[0, 4]], 7, 8))
    op("c_of0", "V", lambda: V.tensor_scalar(T.oi[:, 4:8], T.oi[:, 0:4], 63, None, ALU.bitwise_and), ["io_of"])
    op("c_of1", "V", copy("V", T.of[:, 0:4], T.oi[:, 4:8]), ["c_of0"])
    op("io_og", "G", lambda: g.iota(T.oi[:, 8:12], [[16, 4]], 7, 0))
    op("io_oh", "G", lambda: g.iota(T.oi[:, 12:13], [[0, 1]], 0, 1))
    op("c_og0", "V", lambda: V.tensor_scalar(T.oi[:, 13:14], T.oi[:, 12:13], 8, None, ALU.bitwise_and), ["io_oh"])
    op("c_og1", "V", copy("V", T.p8[:], T.oi[:, 13:14]), ["c_og0"])
    op("c_of2", "V", lambda: V.tensor_scalar(T.of[:, 4:8], T.oi[:, 8:12], T.p8[:], None, ALU.add), ["c_og1", "io_og"])
    op("c_0", "V", copy("V", T.lab[:, 0:128], T.fi[:, 0:128]), ["ld_0"])
    op("c_ab", "V", copy("V", T.lab[:, 128:384], T.fi[:, 128:384]), ["ld_ab"])
    op("c_ct", "V", copy("V", T.lct[:], T.ci[:]), ["ld_ct"])
    dma("c_c2", [(T.lc2[16 * a:16 * a + 16, :], T.lct[mine, 0:192]) for a in range(8)], ["c_ct"])
    op("c_o0", "V", copy("V", T.oo[:, :, 0:64], T.fi[:, 0:128]), ["ld_0"])
    send("L", T.lab, 0, ["c_0", "c_ab"])
    take("in_L", "L", T.lab2, 0)
    fills = ["m_tab1", "m_tab2", "m_tab3"]
    op("c_cdf", "V", copy("V", T.cdf[0:16, :], T.cdi[0:16, :]), ["ld_c16", "io_cd"])
    mm("p_t", [(T.po0[0:32, 16 * c:16 * c + 16], T.cdf[0:16, c:256:8], T.i16[0:16, :], True, True) for c in range(8)], ["c_cdf", "g_i16"])
    op("t_hi", "S", copy("S", T.thl[0:32, 0:128], T.po0[0:32, 0:128]), ["p_t"])
    op("t_lo", "V", lambda: V.tensor_tensor(T.thl[0:32, 128:256], T.po0[0:32, 0:128], T.thl[0:32, 0:128], ALU.subtract), ["t_hi"])
    dma("dt_c", [(T.dt[h, :], T.thl[0:32, 128 * h:128 * h + 128]) for h in range(2)], ["t_hi", "t_lo"])
    dma("tab_c", [(T.tab[16 * a:16 * a + 2, :], T.dt[0:2, :]) for a in range(8)], ["dt_c"] + fills)
    dma("dt_in", [(T.dt[2 * j:2 * j + 2, 0:1024], T.dt[0:2, 0:1024]) for j in range(1, 4)], ["dt_c"])
    for h, (pat, cm) in enumerate([([[16, 8], [0, 16]], 128), ([[0, 8], [1, 16]], 0)]):
        op("io_n%d" % h, "G", lambda h=h, pat=pat, cm=cm: g.iota(T.idn[0:32, 128 * h:128 * h + 128], pat, 0, cm,
                                                                 allow_small_or_imprecise_dtypes=True))
    dma("dt_n", [(T.dt[8 + h, :], T.idn[0:32, 128 * h:128 * h + 128]) for h in range(2)], ["io_n0", "io_n1"])
    dma("tab_n", [(T.tab[16 * a + 8:16 * a + 10, :], T.dt[8:10, :]) for a in range(8)], ["dt_n"] + fills)
    op("c_sf", "V", copy("V", T.sf[:], T.si[:]), ["ld_si", "ld_id"])
    mm("p_s", [(T.pp[:, 0:48], T.psl[:], T.sf[:], True, True), (power(1, 0, 16), T.psl[:], T.sf[:, 0:16], True, True),
               (power(0, 0, 16), T.psl[:], T.sf[:, 24:40], True, True), (power(0, 24, 8), T.psl[:], T.sf[:, 40:48], True, True)],
       ["c_sf", "g_psl", "m_pc"])
    op("l_s1", "V", copy("V", T.lu[:, 0:48], T.pp[:, 0:48]), ["p_s"])
    for j in range(1, 4):
        c0 = 384 * (j - 1)
        names = look("g_s%d" % j, T.gch, c0, T.tab[:, :], T.lu, [0, 64, 88][j - 1], 384, ["l_s%d" % j, "tab_c", "tab_n"])
        pick("x_s%d" % j, power(j + 1, 0, 24), lambda i, c0=c0: T.gch[:, c0 + i:c0 + 384:16], zrow(0), names + ["g_zj"])
        if j < 3:
            op("l_s%d" % (j + 1), "V", copy("V", T.lu[:, 40 + 24 * j:64 + 24 * j], power(j + 1, 0, 24)), ["x_s%d" % j])
        dma("dt_%d" % j, [(T.dt[2 * j + h, 1024 * (l + 1):1024 * (l + 2)], T.gch[h:128:16, c0 + 128 * l:c0 + 128 * l + 128])
                          for h in range(2) for l in range(3)], names)
    dma("tab_j", [(T.tab[16 * a + 2:16 * a + 8, :], T.dt[2:8, :]) for a in range(8)], ["dt_1", "dt_2", "dt_3", "dt_in"])

    def finish(t, a, n, p0, deps):
        op("lf%d" % t, "V", copy("V", T.lf[:, 4 * a:4 * (a + n)], T.pc[:, 8 * p0 + 1:8 * (p0 + n):2]), deps)
        op("eu%d" % t, "S", copy("S", T.vl[:, 8 * a:8 * (a + n)], T.pc[:, 8 * p0:8 * (p0 + n)]), ["lf%d" % t])

    finish(0, 0, 16, 0, ["x_s3"])
    names = look("gu1", T.gch, 1152, T.tab[:, :], T.lu, 40, 128, ["l_s1", "tab_j"])
    for j in range(4):
        pick("xu%d1" % j, power(j + 1, 24, 8), lambda i: T.gch[:, 1152 + i:1280:16], zrow(j), names + ["eu0"])
    finish(1, 16, 8, 24, ["xu%d1" % j for j in range(4)])
    tag = [0, 0, 1] + [c[0] for c in CHAINS for e in range(c[1], c[2])]
    for t, e0, e1, l0, p0 in CHAINS:
        n, c0 = 8 * (e1 - e0), 896 + 128 * e0
        op("lu%d" % t, "V", copy("V", T.lu[:, l0:l0 + n], T.rs[:, 64 * (e0 - 3) + 7:64 * (e1 - 3):8]), ["sc_%d" % (e - 3) for e in range(e0, e1)])
        names = look("gu%d" % t, T.gch, c0, T.tab[:, :], T.lu, l0, 16 * n, ["lu%d" % t, "tab_j"])
        mm("xu%d" % t, [(T.pc[:, 8 * p0 + 64 * s:8 * p0 + 64 * s + 64], T.gch[:, c0 + 128 * s:c0 + 128 * s + 128], T.sel[:], True, True)
                        for s in range(n // 8)], names + ["eu%d" % (t - 1), "g_sel"])
        finish(t, 8 * e0, n, p0, ["xu%d" % t])
    mm("p_d8", [(T.pp[:, 0:64], T.pls[:], T.vl[:, 512:576], True, True)], ["eu%d" % tag[8], "g_pls", "l_s1"])
    op("e_d8", "S", copy("S", T.vl[:, 576:640], T.pp[:, 0:64]), ["p_d8"])

    done, wdone, taps, tables, counted = [], [], [], [], []
    bank = [[], []]
    seen = [[], [], []]
    spread = "e_ee"
    for e in range(9):
        k, l = divmod(e, 3)
        lo = 1024 * (l + 1)
        win = (vb[k] if l == 0 else wb[k])[:, 0:lo]
        lab, lc = (T.lab, T.lct) if k == 0 else (T.lab2, T.lc2)
        cuts = CUTS[e]
        if k == 0:
            need = ["ld_x", "c_0"] if l == 0 else done + ["c_ab"]
        elif l == 0:
            need = taps + ["in_L"]
        else:
            need = wdone + ["cp%d" % k]
        for c, (a, b) in enumerate(cuts):
            t = T.t0[:, lo + a:lo + b] if k == 0 else T.tb[:, 1024 * (e - 3) + a:1024 * (e - 3) + b]
            lb = lab[:, bcol[l] + a // 16:bcol[l] + b // 16]
            la = lab[:, acol[l] + a // 16:acol[l] + b // 16]
            out = vb[k][:, lo + a:lo + b]
            op("B%d_%d" % (e, c), "S", lambda t=t, lb=lb, win=win: S.activation(t, win.indirect(lb), ACT.Identity, bias=255.0, scale=-1.0), need)
            op("A%d_%d" % (e, c), "V", lambda t=t, la=la, win=win, out=out: V.tensor_tensor(out, win.indirect(la), t, ALU.min),
               need + ["B%d_%d" % (e, c)])
            if k > 0:
                cp, q, name = T.vc[:, 1024 * e + a:1024 * e + b], COPY[e][c], "vc%d_%d" % (e, c)
                if q == "G":
                    op(name, q, lambda cp=cp, out=out, n=b - a: g.affine_select(cp, out, [[0, n]], ALU.is_ge, 0.0, 0, 0), ["A%d_%d" % (e, c)])
                elif q == "Y":
                    dma(name, [(cp, out)], ["A%d_%d" % (e, c)])
                else:
                    op(name, q, copy(q, cp, out), ["A%d_%d" % (e, c)])
        done = ["A%d_%d" % (e, c) for c in range(len(cuts))]
        if k == 0:
            dma("vc%d" % e, [(T.vc[:, 1024 * e:1024 * e + 1024], vb[0][:, lo:lo + 1024])], done)
        if l == 0:
            counted = []
        for c, (a, b) in enumerate(cuts if k else HALVES):
            dfc, vote = T.df[:, 1024 * e + a:1024 * e + b], "vt%d_%d" % (e, c)
            op(vote, "V", lambda a=a, b=b, e=e, l=l, k=k, lo=lo, dfc=dfc, lc=lc: V.tensor_tensor(
                dfc, vb[k][:, 0:lo + b].indirect(lc[:, 64 * l + a // 16:64 * l + b // 16]), T.vc[:, 1024 * e + a:1024 * e + b], ALU.not_equal),
               ["vc%d" % e, "c_ct"] if k == 0 else done[:c + 1] + ["vc%d_%d" % (e, c), "c_c2"])
            seen[k].append(vote)
            if e in WIDE:
                pv = [T.pv0, T.pv1][c % 2][:, 0:b - a]
                mm("pv%d_%d" % (e, c), [(pv, T.oneb[:], dfc, True, True)], [vote, "m_oneb"] + bank[c % 2])
                op("ev%d_%d" % (e, c), "S", copy("S", fl[k][:, lo + a:lo + b], pv), ["pv%d_%d" % (e, c)] + tables)
                bank[c % 2] = ["ev%d_%d" % (e, c)]
                counted = counted + bank[c % 2]
            else:
                pv = [T.pv0, T.pv1][e % 2][:, 0:64]
                z = slide(T.zv if k == 0 else T.zo)
                mm("pv%d_%d" % (e, c), [(pv, z(i), T.df[:, 1024 * e + 64 * i:1024 * e + 64 * i + 64], i == 0, i == 15)
                                        for i in range(a // 64, b // 64)], [vote, "g_zv" if k == 0 else "m_zo"] + ([] if c else bank[e % 2]))
        if e not in WIDE:
            xv = T.xv[:, 64 * e:64 * e + 64]
            op("ev%d" % e, "S", copy("S", xv, pv), ["pv%d_1" % e])
            bank[e % 2] = ["ev%d" % e]
            counted = counted + ["F%d" % e]
            if k == 0:
                send("V%d" % e, T.xv, 64 * e, ["ev%d" % e])
                dma("F%d" % e, [(fl[0][16 * a + 8:16 * a + 16, lo:lo + 1024], T["kV%d" % e][:, mine, :]) for a in range(8)], ["aV%d" % e] + done)
            else:
                dma("F%d" % e, [(fl[k][0:128:16, lo:lo + 1024], xv)], ["ev%d" % e] + (seen[0] if k == 1 else tables))
        if k > 0 and l < 2:
            wdone = []
            for c, (a, b) in enumerate(cuts):
                wdone += look("w%d_%d" % (e, c), wb[k], lo + a, vb[k][:, 0:lo + b], T.lr, 64 * (e - 3) + a // 16, b - a,
                              done[:c + 1] + ["el%d" % (e - 3)])
        if e == 2:
            for c, (a, b) in enumerate(QUARTERS):
                q = "VS"[c % 2]
                op("tap1_%d" % c, q, copy(q, T.tx[:, a:b], vb[0][:, :].indirect(T.lct[:, 192 + a // 16:192 + b // 16])), done + ["c_ct"])
                seen[0].append("tap1_%d" % c)
            for h in range(2):
                send("X%d" % h, T.tx, 512 * h, ["tap1_%d" % c for c in (2 * h, 2 * h + 1)])
                take("in_X%d" % h, "X%d" % h, T.vb1, 512 * h)
            taps = ["in_X0", "in_X1"]
        if e == 5:
            taps = look("tap2", T.vb2, 0, vb[1][:, :], T.lr, 128, 1024, done + ["el2"])
            dma("id_R", [(T.vb1[16 * a:16 * a + 2, 0:1024], T.dt[0:2, 0:1024]) for a in range(8)], seen[1] + taps + ["dt_c"])
        if e in (2, 5):
            dma("cp%d" % (k + 1), [(wb[k + 1][:, 0:1024], vb[k + 1][:, 0:1024])], taps)
        if k == 2:
            ways = [("Y%d" % l, lo, done)] if l < 2 else [("Y20", lo, done[:1]), ("Y21", lo + 512, done)]
            for m, c0, deps in ([("Yi", 0, taps)] if l == 0 else []) + ways:
                send(m, T.vb2, c0, deps)
                take("o_" + m, m, T.yv, c0)
        looked = look("w1_%d" % e, T.gf, 512 * e, fl[k][:, 0:lo + 1024], T.lf, 32 * e, 512,
                      counted + ["lf%d" % tag[e]] + (["m_t0"] if e == 0 else []))
        if k == 0:
            tables = tables + looked
        pick("w2_%d" % e, T.pf[:, 1:64:2], lambda i, e=e: T.gf[:, 512 * e + i:512 * e + 512:16],
             slide(T.zu if k == 0 else T.z1) if e < 8 else lambda i: T.zs[:, 120 - 8 * i:248 - 8 * i],
             looked + ["g_zu" if k == 0 else "g_z1" if e < 8 else "g_zs", "m_pf"] + (["sc_%d" % (e - 1)] if e else []))
        nodes, rs = T.vl[:, 64 * e:64 * e + 64] if e < 8 else T.vl[:, 576:640], T.rs[:, 64 * e:64 * e + 64]
        op("sc_%d" % e, "V", lambda rs=rs, nodes=nodes: V.tensor_tensor_scan(rs, T.pf[:, 0:64], nodes, 0.0, ALU.max, ALU.min),
           ["w2_%d" % e, "eu%d" % tag[e] if e < 8 else "e_d8"])
        if e == 8:
            op("w5", "V", copy("V", T.rf[:], rs[:, 7:64:8]), ["sc_8"])
            send("T", T.rf, 0, ["w5"])
            dma("o_t", [(T.yt[:], T.kT[:])], ["aT"])
        elif e != 5:
            mk = T.mk[:, 64 * e:64 * e + 64]
            op("mk%d" % e, "V", lambda rs=rs, mk=mk, j=k % 2: V.tensor_tensor(mk, rs.indirect(T.of[:, 4 * j:4 * j + 4]),
                                                                             T.own[:, 64 * j:64 * j + 64], ALU.mult),
               ["sc_%d" % e] + [["c_of1", "g_own"], ["c_of2", "g_owo"]][k % 2])
            if e < 5:
                mm("pl%d" % e, [(T.pl[:, 0:64], T.ee[:], mk, True, True)], ["mk%d" % e, spread])
                op("el%d" % e, "V", copy("V", T.lr[:, 64 * e:64 * e + 64], T.pl[:, 0:64]), ["pl%d" % e])
                spread = "el%d" % e
            else:
                rh = T.rh[:, 16 * l:16 * l + 16]
                mm("pl%d" % e, [(T.pl[64 * h:64 * h + 64, 0:16], mk, T.ee[:, 0:16], True, True) for h in range(2)], ["mk%d" % e, spread])
                op("hi%d" % e, "V", copy("V", rh, T.pl[:, 0:16]), ["pl%d" % e])
                op("lo%d" % e, "V", lambda rh=rh: V.tensor_tensor(rh[64:128, :], T.pl[64:128, 0:16], rh[64:128, :], ALU.subtract), ["hi%d" % e])
                spread = "lo%d" % e
                send("R%d" % e, T.rh, 16 * l, [spread])
                dma("in_R%d" % e, [(T.vb1[h:128:16, lo:lo + 1024], T["kR%d" % e][:, 64 * h:64 * h + 64, :]) for h in range(2)],
                    ["aR%d" % e, "id_R"])
    for j, (nm, q, col, y) in enumerate([("fb", "V", bcol, T.yb), ("fa", "S", acol, T.ya)]):
        po = [T.po0, T.po1][j]
        for l in (1, 2):
            c0 = 2048 * j + 1024 * (l - 1)
            names = look(nm + "%d" % l, T.gfin, c0, T.vb1[:, 0:1024 * (l + 1)], T.lab, col[l], 1024, ["in_R6", "in_R7"][:l])
            pick("x%s%d" % (nm, l), po[:, 64 * l:64 * l + 64], lambda i, c0=c0: T.gfin[:, c0 + i:c0 + 1024:16], zrow(0), names + ["t_lo"])
        op("e" + nm, q, copy(q, T.oo[:, j, 64:192], po[:, 64:192]), ["x%s1" % nm, "x%s2" % nm])
        dma("o_" + nm, [(y[:], T.oo[:, j, :])], ["e" + nm, "c_o0"], q="Y" if q == "V" else q)
    return defs


def issue(g, defs, T, engines):
    queue = {"V": g.vector, "S": g.scalar, "P": g.tensor, "G": g, "Y": g.sync}
    order = {q: ORDER[q].split() for q in queue}
    assert sorted(n for q in order for n in order[q]) == sorted(n for n, v in defs.items() if v[0] != "ext")
    wanted = set(d for v in defs.values() for d in v[3])
    token = {n: (n,) + v[2] for n, v in defs.items() if v[0] == "ext"}
    nd, left = 0, 0
    for q, names in order.items():
        cnt = 0
        for name in names:
            kind = defs[name][0]
            if kind == "op" and name in wanted:
                cnt += 1
                token[name] = ("q" + q, T.sem["q" + q], cnt)
            elif kind == "dma":
                token[name] = ("m%d" % nd, T.sem["m%d" % nd], 16 * len(defs[name][2]))
                nd += 1
    waited = {}
    for q, names in order.items():
        seen = {}
        for name in names:
            kind, _, what, deps = defs[name]
            most = {}
            for d in deps:
                key, sem, val = token[d]
                if val > most.get(key, (None, 0))[1]:
                    most[key] = (sem, val)
            for key, (sem, val) in most.items():
                if val > seen.get(key, 0):
                    queue[q].wait_ge(sem, val)
                    seen[key] = val
                    waited[key] = max(waited.get(key, 0), val)
            if kind == "op":
                ins = what()
                if name in wanted:
                    ins.then_inc(token[name][1], 1)
            elif kind == "dma":
                for out, src in what:
                    queue[q].dma_start(out, src).then_inc(token[name][1], 16)
            else:
                g.remote_dma_fused(what, local_sem=T.sem.left)
                left += engines
    g.wait_ge(T.sem.left, left)
    for name, (key, sem, val) in token.items():
        if val > waited.get(key, 0):
            g.wait_ge(sem, val)
